import numpy as np
import ml_dtypes


def mxq(x, axis, fmt="e4m3"):
    dtype, down = {"e4m3": (ml_dtypes.float8_e4m3fn, 7), "e5m2": (ml_dtypes.float8_e5m2, 14)}[fmt]
    v = np.moveaxis(np.asarray(x, np.float32).astype(ml_dtypes.bfloat16).astype(np.float64), axis, -1)
    blocks = v.reshape(v.shape[:-1] + (-1, 32))
    amax = np.abs(blocks).max(-1, keepdims=True)
    byte = np.maximum(np.where(amax > 0, np.frexp(amax)[1] - 1 + 127, 0) - down, 1)
    scale = np.exp2(byte - 127.0)
    codes = (blocks / scale).astype(np.float32).astype(dtype).astype(np.float64)
    return np.moveaxis((codes * scale).reshape(v.shape), -1, axis)


WIDE = False


def mx_kscale(k):
    if not WIDE:
        return np.ones(k)
    levels = np.array([10, -10, 5, -5, 0])
    if k % 512:
        return np.exp2(np.random.permutation(np.resize(levels, k // 32))).repeat(32)
    a = np.empty((k // 512, 16))
    for p in range(k // 512):
        a[p, :8] = np.random.permutation(np.resize(levels, 8))
        for g in range(8):
            far = levels[np.abs(levels - a[p, g]) >= 10]
            a[p, g + 8] = far[np.random.randint(len(far))]
    return np.exp2(a.ravel()).repeat(32)


def f64(x):
    return np.asarray(x).astype(np.float64)


def striped8(idx):
    return np.concatenate([x.reshape(-1, 16).T for x in idx]).astype(np.uint16)


def runs(offs, k):
    lists = np.stack([offs[16 * r : 16 * r + 16].T.reshape(-1) for r in range(8)]).astype(np.int64)
    return lists[np.arange(k) % 512 // 64]


def pack_weight(w):
    k, n = w.shape
    w = f64(np.asarray(w, np.float32).astype(ml_dtypes.bfloat16)).reshape(k // 32, 32, n)
    amax = np.abs(w).max(1)
    byte = np.clip(np.where(amax > 0, np.frexp(amax)[1] - 1 + 127 - 7, 1), 1, 254)
    scaled = (w * np.exp2(127.0 - byte)[:, None, :]).reshape(k, n).astype(np.float32)
    words = np.ascontiguousarray(scaled.reshape(k // 512, 128, 4, n).transpose(0, 1, 3, 2)).astype(ml_dtypes.float8_e4m3fn).view(np.uint8)
    return words, np.ascontiguousarray(byte.astype(np.uint8).reshape(k // 512, 16, n))


def unpack_weight(words, scales):
    g, p, n, _ = words.shape
    vals = np.ascontiguousarray(words).view(ml_dtypes.float8_e4m3fn).astype(np.float64) * np.repeat(np.exp2(scales.astype(np.float64) - 127.0), 8, axis=1)[..., None]
    return vals.transpose(0, 1, 3, 2).reshape(g * 512, n)

def planes(y):
    n, m = y.shape
    v = y.astype(np.float32).astype(ml_dtypes.bfloat16).astype(np.float64).reshape(n // 32, 32, m)
    top = np.abs(v).max(1)
    byte = np.clip(np.where(top > 0, np.frexp(top)[1] - 1 + 127 - 7, 1), 1, 254)
    codes = (v * np.exp2(127.0 - byte)[:, None, :]).reshape(n, m).astype(np.float32).astype(ml_dtypes.float8_e4m3fn).view(np.uint8)
    words = codes.reshape(n // 512, 128, 4, m).transpose(0, 1, 3, 2)
    return np.ascontiguousarray(words), np.ascontiguousarray(byte.astype(np.uint8).reshape(n // 512, 16, m))


K, T, S, N, H = 512, 2048, 512, 512, 512
P = 2 ** 7


def setup_inputs():
    n = np.random.standard_normal
    s = mx_kscale(K)[:, None]
    u = mx_kscale(H)
    packed_xT = pack_weight(n((K, T)) * s)
    packed_w2 = pack_weight(n((H, N)) / np.sqrt(H) / u[:, None])
    return {
        "x_words": packed_xT[0],
        "x_scales": packed_xT[1],
        "w1": (n((K, H)) / np.sqrt(K) / s * u).astype(np.float32),
        "prev": (n((H, S)) * u[:, None]).astype(np.float32),
        "c2": np.tile(np.random.uniform(0.05, 0.4, S), (P, 1)).astype(np.float32),
        "w2_words": packed_w2[0],
        "w2_scales": packed_w2[1],
        "offs": striped8(np.stack([np.random.permutation(T)[:S] for _ in range(8)])),
        "east": striped8(np.stack([np.random.permutation(S) for _ in range(8)])),
        "west": striped8(np.stack([np.random.permutation(S) for _ in range(8)])),
    }


def reference(x_words, x_scales, w1, prev, c2, w2_words, w2_scales, offs, east, west):
    xq = unpack_weight(x_words, x_scales)[np.arange(K)[:, None], runs(offs, K)]
    y = mxq(f64(w1), 0, "e4m3").T @ xq
    z = 2.0 * y - f64(prev) + f64(c2)[:1] * (y[np.arange(H)[:, None], runs(east, H)] + y[np.arange(H)[:, None], runs(west, H)] - (2.0 * y))
    out_0 = unpack_weight(w2_words, w2_scales).T @ mxq(z, 0, "e4m3")
    return (out_0,) + planes(out_0)

@@ -1,0 +1,291 @@
+from contextlib import ExitStack
+
+import concourse.mybir as mybir
+from concourse.masks import make_identity
+
+K, T, S, H, N = 512, 2048, 512, 512, 512
+FLOPS = 2 * K * H * S + 2 * H * N * S
+
+F32 = mybir.dt.float32
+BF16 = mybir.dt.bfloat16
+I32 = mybir.dt.int32
+U32 = mybir.dt.uint32
+U16 = mybir.dt.uint16
+U8 = mybir.dt.uint8
+FP8X4 = mybir.dt.float8_e4m3fn_x4
+COPY = mybir.ActivationFunctionType.Copy
+MULT = mybir.AluOpType.mult
+ADD = mybir.AluOpType.add
+SUB = mybir.AluOpType.subtract
+
+P = 128
+PACK = 4
+BLOCKS = S // P
+FUSE = 0
+CHUNKS = [(0, 256), (256, 384), (384, 512)]
+W1_VECTOR_M = 80
+
+
+def tile_picked_waveeq_none_po_kernel(
+    tc, x_words, x_scales, w1, prev, c2, w2_words, w2_scales, offs, east, west, out_0, out_1, out_2
+):
+    nc = tc.nc
+    with ExitStack() as ctx:
+        lists = ctx.enter_context(tc.tile_pool(name="lists", bufs=1))
+        keep = ctx.enter_context(tc.tile_pool(name="keep", bufs=1))
+        psum = ctx.enter_context(tc.psum_pool(name="psum", bufs=1))
+
+        def bank(index, shape, name):
+            return psum.tile(shape, F32, name=name, tag="bank%d" % index)
+
+        offs_sb = lists.tile([P, S // 16], U16, name="offs_sb")
+        east_sb = lists.tile([P, S // 16], U16, name="east_sb")
+        west_sb = lists.tile([P, S // 16], U16, name="west_sb")
+
+        nc.sync.dma_start(offs_sb[:], offs)
+        xs_window = keep.tile([P, T], U8, name="xs_window", tag="early", align_bytes=64)
+        nc.sync.dma_start(
+            xs_window[:].bitcast(I32), x_scales[0].bitcast(I32).unsqueeze(1).to_broadcast([16, 8, T // 4])
+        )
+        w1_raw = keep.tile([P, PACK, H], F32, name="w1_raw", tag="big")
+        nc.sync.dma_start(w1_raw[:], w1.rearrange("(p j) c -> p j c", j=PACK))
+        x_window = keep.tile([P, T], I32, name="x_window", align_bytes=64)
+        nc.sync.dma_start(x_window[:], x_words[0].rearrange("p n t -> p (n t)").bitcast(I32))
+        nc.sync.dma_start(east_sb[:], east)
+        nc.sync.dma_start(west_sb[:], west)
+        c_rows = keep.tile([P, P], F32, name="c_rows")
+        nc.sync.dma_start(c_rows[:], c2.rearrange("a (b j) -> (a b) j", j=P)[0:P, :])
+
+        w2s_raw = keep.tile([P, N], U8, name="w2s_raw", align_bytes=64)
+        w2s_rows = w2_scales[0].bitcast(I32).rearrange("(q a) c -> a q c", a=4)
+        for a in range(4):
+            nc.gpsimd.dma_start(w2s_raw[a:P:4, :].bitcast(I32), w2s_rows[a].unsqueeze(1).to_broadcast([4, 8, N // 4]))
+        ident = keep.tile([P, P], F32, name="ident")
+        make_identity(nc, ident[:])
+
+        c_bank = bank(4, [P, P], "c_bank")
+        nc.tensor.transpose(c_bank[:], c_rows[:], ident[:])
+        c_col = keep.tile([P, BLOCKS], F32, name="c_col")
+        nc.scalar.copy(c_col[:], c_bank[:, 0:BLOCKS])
+
+        xs_plane = keep.tile([P, S], U8, name="xs_plane", align_bytes=64)
+        nc.vector.memset(xs_plane[:].bitcast(I32), 0)
+        xs_picked = keep.tile([P, S], U8, name="xs_picked", align_bytes=64)
+        nc.vector.tensor_copy(xs_picked[:], xs_window[:].indirect(offs_sb[:]))
+        for a in range(4):
+            nc.sync.dma_start(xs_plane[a:P:32, :].bitcast(I32), xs_picked[8 * a : P : 32, :].bitcast(I32))
+
+        w2_raw = keep.tile([P, N], I32, name="w2_raw", tag="early", align_bytes=64)
+        nc.sync.dma_start(w2_raw[:], w2_words[0].rearrange("p n t -> p (n t)").bitcast(I32))
+
+        w1_grouped = keep.tile([P, PACK, P, PACK], BF16, name="w1_grouped", align_bytes=64)
+        w1_dst = w1_grouped[:].rearrange("p t m j -> p m j t")
+        w1_src = w1_raw[:].rearrange("p j (m t) -> p m j t", t=PACK)
+        nc.vector.tensor_copy(w1_dst[:, 0:W1_VECTOR_M], w1_src[:, 0:W1_VECTOR_M])
+        nc.scalar.copy(w1_dst[:, W1_VECTOR_M:P], w1_src[:, W1_VECTOR_M:P])
+        w1_codes = keep.tile([P, H], U32, name="w1_codes", align_bytes=64)
+        w1_scales = keep.tile([P, H], U8, name="w1_scales", align_bytes=64)
+        nc.vector.quantize_mx(
+            out=w1_codes[:].bitcast(FP8X4), scales=w1_scales[:], in_=w1_grouped[:].rearrange("p t m j -> p (t m j)")
+        )
+
+        prev_sb = keep.tile([P, 2, PACK, S // 2], F32, name="prev_sb", tag="big")
+        prev_rows = prev.rearrange("(p t) (h j) -> p h t j", t=PACK, h=2)
+        for h in range(2):
+            nc.sync.dma_start(prev_sb[:, h], prev_rows[:, h])
+
+        x_picked = keep.tile([P, S], U32, name="x_picked", align_bytes=64)
+        for h in range(2):
+            nc.vector.tensor_copy(
+                x_picked[:, 256 * h : 256 * (h + 1)],
+                x_window[:].bitcast(U32).indirect(offs_sb[:, 16 * h : 16 * (h + 1)]),
+            )
+
+        w2_codes = keep.tile([P, PACK, P], I32, name="w2_codes", align_bytes=64)
+        w2_planes = keep.tile([P, PACK, P], U8, name="w2_planes", align_bytes=64)
+        nc.vector.tensor_copy(
+            w2_codes[:].rearrange("p t m -> p m t"), w2_raw[:].rearrange("p (m t) -> p m t", t=PACK)
+        )
+        nc.vector.tensor_copy(
+            w2_planes[:].rearrange("p t m -> p m t"), w2s_raw[:].rearrange("p (m t) -> p m t", t=PACK)
+        )
+
+        y = [keep.tile([P, S], F32, name="y%d" % t) for t in range(PACK)]
+        minus2y = [keep.tile([P, S], F32, name="minus2y%d" % t) for t in range(PACK)]
+        y_banks = []
+        for t in range(PACK):
+            y_bank = bank(t, [P, S], "y_bank%d" % t)
+            for h in range(2):
+                cols = slice(256 * h, 256 * (h + 1))
+                nc.tensor.matmul_mx(
+                    out=y_bank[:, cols],
+                    lhsT=w1_codes[:, P * t : P * (t + 1)].bitcast(FP8X4),
+                    lhsT_scale=w1_scales[:, P * t : P * (t + 1)],
+                    rhs=x_picked[:, cols].bitcast(FP8X4),
+                    rhs_scale=xs_plane[:, cols],
+                    start=True,
+                    stop=True,
+                )
+            y_banks.append(y_bank)
+        for kind, t in [("y", 0), ("u", 0), ("y", 1), ("u", 1), ("y", 2), ("y", 3), ("u", 2), ("u", 3)]:
+            if kind == "y":
+                nc.scalar.copy(y[t][:], y_banks[t][:])
+            else:
+                nc.scalar.activation(minus2y[t][:], y_banks[t][:], COPY, scale=-2.0)
+
+        def add_transposed(dst, terms):
+            for n, term in enumerate(terms):
+                nc.tensor.matmul(dst, term, ident[:], start=(n == 0), stop=(n == len(terms) - 1), is_transpose=True)
+
+        rest = {}
+
+        def make_rest(b):
+            rest_bank = bank(4 + b, [P, PACK, P], "rest_bank%d" % b)
+            for t in range(PACK):
+                j0 = P * (b % 2)
+                add_transposed(
+                    rest_bank[:, t, :], [prev_sb[:, b // 2, t, j0 : j0 + P], minus2y[t][:, P * b : P * (b + 1)]]
+                )
+            rest_sb = keep.tile([P, 2, P, 2], F32, name="rest%d" % b, tag="rest%d" % b, align_bytes=64)
+            nc.scalar.copy(rest_sb[:], rest_bank[:].rearrange("j (u e) p -> j u p e", e=2))
+            rest[b] = rest_sb
+
+        out_words = keep.tile([P, S], U32, name="out_words", align_bytes=64)
+        out_scales = keep.tile([P, S], U8, name="out_scales", align_bytes=64)
+        out_rows = out_0.rearrange("(p t) j -> p t j", t=PACK)
+        out_word_rows = out_1[0].rearrange("p n t -> p (n t)").bitcast(I32)
+
+        terms = {}
+        lap_banks = {}
+        z_turned = {}
+        z_grouped = {}
+        o_grouped = {}
+
+        def gather(c, t, tag):
+            j0, j1 = CHUNKS[c]
+            lcols = slice(j0 // 16, j1 // 16)
+            pair = keep.tile([P, 2, j1 - j0], F32, name="pair%d_%d" % (c, t), tag=tag, align_bytes=64)
+            ge = pair[:, 0, :]
+            gw = pair[:, 1, :]
+            if FUSE == 0:
+                nc.vector.tensor_copy(ge, y[t][:].indirect(east_sb[:, lcols]))
+                nc.vector.tensor_copy(gw, y[t][:].indirect(west_sb[:, lcols]))
+            elif FUSE == 1:
+                nc.vector.tensor_tensor(ge, y[t][:].indirect(east_sb[:, lcols]), minus2y[t][:, j0:j1], ADD)
+                nc.vector.tensor_copy(gw, y[t][:].indirect(west_sb[:, lcols]))
+            else:
+                nc.vector.tensor_tensor(ge, y[t][:].indirect(east_sb[:, lcols]), minus2y[t][:, j0:j1], ADD)
+                nc.vector.tensor_tensor(gw, y[t][:].indirect(west_sb[:, lcols]), ge, ADD)
+            for b in range(j0 // P, j1 // P):
+                part = slice(P * b - j0, P * (b + 1) - j0)
+                if FUSE == 0:
+                    terms[b, t] = [minus2y[t][:, P * b : P * (b + 1)], ge[:, part], gw[:, part]]
+                elif FUSE == 1:
+                    terms[b, t] = [ge[:, part], gw[:, part]]
+                else:
+                    terms[b, t] = [gw[:, part]]
+
+        def turn(b, u):
+            lap_banks[b, u] = bank((2 * b + u) % 4, [P, 2, P], "lap%d_%d" % (b, u))
+            for e in range(2):
+                add_transposed(lap_banks[b, u][:, e, :], terms[b, 2 * u + e])
+
+        def combine(b, u):
+            if u == 0:
+                z_turned[b] = keep.tile([P, 2, P, 2], BF16, name="z_turned%d" % b)
+            nc.vector.scalar_tensor_tensor(
+                z_turned[b][:, u],
+                lap_banks[b, u][:].rearrange("j e p -> j p e"),
+                c_col[:, b : b + 1],
+                rest[b][:, u],
+                MULT,
+                SUB,
+            )
+
+        def turn_back(b):
+            words = z_turned[b][:].rearrange("j u p e -> j (u p e)").bitcast(F32)
+            back = bank(4 + b % 2, [P, 2, P], "back%d" % b)
+            for u in range(2):
+                nc.tensor.transpose(back[:, u, :], words[:, P * u : P * (u + 1)], ident[:])
+            z_grouped[b] = keep.tile([P, P * PACK], BF16, name="z_grouped%d" % b, tag="z_grouped%d" % b, align_bytes=64)
+            nc.scalar.copy(
+                z_grouped[b][:].bitcast(F32).rearrange("p (j u) -> p j u", u=2), back[:].rearrange("p u j -> p j u")
+            )
+
+        def second_product(b):
+            z_codes = keep.tile([P, P], U32, name="z_codes%d" % b, align_bytes=64)
+            z_scales = keep.tile([P, P], U8, name="z_scales%d" % b, align_bytes=64)
+            nc.vector.quantize_mx(out=z_codes[:].bitcast(FP8X4), scales=z_scales[:], in_=z_grouped[b][:])
+            out_bank = bank(6 + b % 2, [P, PACK, P], "out_bank%d" % b)
+            for t in range(PACK):
+                nc.tensor.matmul_mx(
+                    out=out_bank[:, t, :],
+                    lhsT=w2_codes[:, t, :].bitcast(FP8X4),
+                    lhsT_scale=w2_planes[:, t, :],
+                    rhs=z_codes[:].bitcast(FP8X4),
+                    rhs_scale=z_scales[:],
+                    start=True,
+                    stop=True,
+                )
+            o_grouped[b] = keep.tile([P, P * PACK], BF16, name="o_grouped%d" % b, tag="o_grouped%d" % b, align_bytes=64)
+            nc.scalar.copy(
+                o_grouped[b][:].rearrange("p (j t) -> p j t", t=PACK), out_bank[:].rearrange("p t j -> p j t")
+            )
+            o_sb = keep.tile([P, PACK, P], F32, name="o_sb%d" % b)
+            nc.scalar.copy(o_sb[:], out_bank[:])
+            queue = nc.scalar if b == BLOCKS - 1 else nc.sync
+            queue.dma_start(out_rows[:, :, P * b : P * (b + 1)], o_sb[:])
+
+        def planes(b):
+            cols = slice(P * b, P * (b + 1))
+            nc.vector.quantize_mx(out=out_words[:, cols].bitcast(FP8X4), scales=out_scales[:, cols], in_=o_grouped[b][:])
+            nc.sync.dma_start(out_word_rows[:, cols], out_words[:, cols].bitcast(I32))
+
+        for t in range(PACK):
+            gather(0, t, "pair%d" % t)
+        turn(0, 0)
+        turn(1, 0)
+        make_rest(0)
+        turn(0, 1)
+        turn(1, 1)
+        make_rest(1)
+        gather(1, 0, "pair0")
+        combine(0, 0)
+        combine(0, 1)
+        turn_back(0)
+        make_rest(2)
+        gather(1, 1, "rest0")
+        combine(1, 0)
+        combine(1, 1)
+        turn_back(1)
+        make_rest(3)
+        turn(2, 0)
+        gather(1, 2, "rest1")
+        second_product(0)
+        gather(1, 3, "z_grouped0")
+        turn(2, 1)
+        second_product(1)
+        gather(2, 0, "z_grouped1")
+        combine(2, 0)
+        combine(2, 1)
+        turn_back(2)
+        gather(2, 1, "rest2")
+        turn(3, 0)
+        planes(0)
+        gather(2, 2, "o_grouped0")
+        second_product(2)
+        planes(1)
+        combine(3, 0)
+        gather(2, 3, "z_grouped2")
+        turn(3, 1)
+        combine(3, 1)
+        turn_back(3)
+        planes(2)
+        second_product(3)
+        planes(3)
+
+        for q in range(4):
+            queue = nc.sync if q % 2 == 0 else nc.scalar
+            queue.dma_start(
+                out_2[0, 4 * q : 4 * q + 4, :].bitcast(I32), out_scales[32 * q : 32 * q + 4, :].bitcast(I32)
+            )

@@ -21,8 +21,6 @@ SUB = mybir.AluOpType.subtract
 P = 128
 PACK = 4
 BLOCKS = S // P
-FUSE = 0
-CHUNKS = [(0, 256), (256, 384), (384, 512)]
 W1_VECTOR_M = 80
 
 
@@ -47,23 +45,26 @@ def tile_picked_waveeq_none_po_kernel(
         nc.sync.dma_start(
             xs_window[:].bitcast(I32), x_scales[0].bitcast(I32).unsqueeze(1).to_broadcast([16, 8, T // 4])
         )
+        w2s_raw = keep.tile([P, N], U8, name="w2s_raw", align_bytes=64)
+        nc.sync.dma_start(
+            w2s_raw[:].bitcast(I32), w2_scales[0].bitcast(I32).unsqueeze(1).to_broadcast([16, 8, N // 4])
+        )
         w1_raw = keep.tile([P, PACK, H], F32, name="w1_raw", tag="big")
         nc.sync.dma_start(w1_raw[:], w1.rearrange("(p j) c -> p j c", j=PACK))
         x_window = keep.tile([P, T], I32, name="x_window", align_bytes=64)
         nc.sync.dma_start(x_window[:], x_words[0].rearrange("p n t -> p (n t)").bitcast(I32))
         nc.sync.dma_start(east_sb[:], east)
         nc.sync.dma_start(west_sb[:], west)
-        c_rows = keep.tile([P, P], F32, name="c_rows")
-        nc.sync.dma_start(c_rows[:], c2.rearrange("a (b j) -> (a b) j", j=P)[0:P, :])
 
-        w2s_raw = keep.tile([P, N], U8, name="w2s_raw", align_bytes=64)
-        w2s_rows = w2_scales[0].bitcast(I32).rearrange("(q a) c -> a q c", a=4)
-        for a in range(4):
-            nc.gpsimd.dma_start(w2s_raw[a:P:4, :].bitcast(I32), w2s_rows[a].unsqueeze(1).to_broadcast([4, 8, N // 4]))
         ident = keep.tile([P, P], F32, name="ident")
         make_identity(nc, ident[:])
+        c_rows = keep.tile([P, P], F32, name="c_rows")
+        nc.gpsimd.memset(c_rows[:], 0.0)
+        nc.gpsimd.dma_start(c_rows[0:BLOCKS, :], c2[0:1, :].rearrange("a (b j) -> (a b) j", j=P))
+        w2_planes = keep.tile([P, PACK, P], U8, name="w2_planes", align_bytes=64)
+        nc.gpsimd.memset(w2_planes[:].bitcast(I32), 0)
 
-        c_bank = bank(4, [P, P], "c_bank")
+        c_bank = bank(7, [P, P], "c_bank")
         nc.tensor.transpose(c_bank[:], c_rows[:], ident[:])
         c_col = keep.tile([P, BLOCKS], F32, name="c_col")
         nc.scalar.copy(c_col[:], c_bank[:, 0:BLOCKS])
@@ -75,12 +76,20 @@ def tile_picked_waveeq_none_po_kernel(
         for a in range(4):
             nc.sync.dma_start(xs_plane[a:P:32, :].bitcast(I32), xs_picked[8 * a : P : 32, :].bitcast(I32))
 
+        w2s_dealt = keep.tile([P, PACK, P], U8, name="w2s_dealt", align_bytes=64)
+        nc.vector.tensor_copy(
+            w2s_dealt[:].rearrange("p t (g i) -> p g t i", i=16),
+            w2s_raw[:].rearrange("p (g i t) -> p g t i", i=16, t=PACK),
+        )
+        for a in range(4):
+            nc.gpsimd.dma_start(w2_planes[a:P:32].bitcast(I32), w2s_dealt[8 * a : P : 32].bitcast(I32))
+
         w2_raw = keep.tile([P, N], I32, name="w2_raw", tag="early", align_bytes=64)
         nc.sync.dma_start(w2_raw[:], w2_words[0].rearrange("p n t -> p (n t)").bitcast(I32))
 
-        w1_grouped = keep.tile([P, PACK, P, PACK], BF16, name="w1_grouped", align_bytes=64)
-        w1_dst = w1_grouped[:].rearrange("p t m j -> p m j t")
-        w1_src = w1_raw[:].rearrange("p j (m t) -> p m j t", t=PACK)
+        w1_grouped = keep.tile([P, PACK, P, PACK], BF16, name="w1_grouped", tag="w1_grouped", align_bytes=64)
+        w1_dst = w1_grouped[:].rearrange("p t m j -> p m t j")
+        w1_src = w1_raw[:].rearrange("p j (m t) -> p m t j", t=PACK)
         nc.vector.tensor_copy(w1_dst[:, 0:W1_VECTOR_M], w1_src[:, 0:W1_VECTOR_M])
         nc.scalar.copy(w1_dst[:, W1_VECTOR_M:P], w1_src[:, W1_VECTOR_M:P])
         w1_codes = keep.tile([P, H], U32, name="w1_codes", align_bytes=64)
@@ -94,7 +103,7 @@ def tile_picked_waveeq_none_po_kernel(
         for h in range(2):
             nc.sync.dma_start(prev_sb[:, h], prev_rows[:, h])
 
-        x_picked = keep.tile([P, S], U32, name="x_picked", align_bytes=64)
+        x_picked = keep.tile([P, S], U32, name="x_picked", tag="w1_grouped", align_bytes=64)
         for h in range(2):
             nc.vector.tensor_copy(
                 x_picked[:, 256 * h : 256 * (h + 1)],
@@ -102,23 +111,21 @@ def tile_picked_waveeq_none_po_kernel(
             )
 
         w2_codes = keep.tile([P, PACK, P], I32, name="w2_codes", align_bytes=64)
-        w2_planes = keep.tile([P, PACK, P], U8, name="w2_planes", align_bytes=64)
         nc.vector.tensor_copy(
-            w2_codes[:].rearrange("p t m -> p m t"), w2_raw[:].rearrange("p (m t) -> p m t", t=PACK)
-        )
-        nc.vector.tensor_copy(
-            w2_planes[:].rearrange("p t m -> p m t"), w2s_raw[:].rearrange("p (m t) -> p m t", t=PACK)
+            w2_codes[:].rearrange("p t (g i) -> p g t i", i=4),
+            w2_raw[:].rearrange("p (g i t) -> p g t i", i=4, t=PACK),
         )
 
         y = [keep.tile([P, S], F32, name="y%d" % t) for t in range(PACK)]
         minus2y = [keep.tile([P, S], F32, name="minus2y%d" % t) for t in range(PACK)]
-        y_banks = []
-        for t in range(PACK):
-            y_bank = bank(t, [P, S], "y_bank%d" % t)
-            for h in range(2):
+        y_banks = {}
+
+        def first_product(t, halves, index):
+            y_bank = bank(index, [P, 256 * len(halves)], "y_bank%d_%d" % (t, halves[0]))
+            for n, h in enumerate(halves):
                 cols = slice(256 * h, 256 * (h + 1))
                 nc.tensor.matmul_mx(
-                    out=y_bank[:, cols],
+                    out=y_bank[:, 256 * n : 256 * (n + 1)],
                     lhsT=w1_codes[:, P * t : P * (t + 1)].bitcast(FP8X4),
                     lhsT_scale=w1_scales[:, P * t : P * (t + 1)],
                     rhs=x_picked[:, cols].bitcast(FP8X4),
@@ -126,12 +133,15 @@ def tile_picked_waveeq_none_po_kernel(
                     start=True,
                     stop=True,
                 )
-            y_banks.append(y_bank)
-        for kind, t in [("y", 0), ("u", 0), ("y", 1), ("u", 1), ("y", 2), ("y", 3), ("u", 2), ("u", 3)]:
-            if kind == "y":
-                nc.scalar.copy(y[t][:], y_banks[t][:])
-            else:
-                nc.scalar.activation(minus2y[t][:], y_banks[t][:], COPY, scale=-2.0)
+            y_banks[t, halves[0]] = (y_bank, slice(256 * halves[0], 256 * (halves[-1] + 1)))
+
+        def take_y(t, h):
+            y_bank, cols = y_banks[t, h]
+            nc.scalar.copy(y[t][:, cols], y_bank[:])
+
+        def take_u(t, h):
+            y_bank, cols = y_banks[t, h]
+            nc.scalar.activation(minus2y[t][:, cols], y_bank[:], COPY, scale=-2.0)
 
         def add_transposed(dst, terms):
             for n, term in enumerate(terms):
@@ -139,16 +149,18 @@ def tile_picked_waveeq_none_po_kernel(
 
         rest = {}
 
-        def make_rest(b):
-            rest_bank = bank(4 + b, [P, PACK, P], "rest_bank%d" % b)
-            for t in range(PACK):
-                j0 = P * (b % 2)
+        def make_rest(b, u):
+            rest_bank = bank(4 + (len(rest) + 1) % 4, [P, 2, P], "rest_bank%d_%d" % (b, u))
+            j0 = P * (b % 2)
+            for e in range(2):
+                t = 2 * u + e
                 add_transposed(
-                    rest_bank[:, t, :], [prev_sb[:, b // 2, t, j0 : j0 + P], minus2y[t][:, P * b : P * (b + 1)]]
+                    rest_bank[:, e, :], [prev_sb[:, b // 2, t, j0 : j0 + P], minus2y[t][:, P * b : P * (b + 1)]]
                 )
-            rest_sb = keep.tile([P, 2, P, 2], F32, name="rest%d" % b, tag="rest%d" % b, align_bytes=64)
-            nc.scalar.copy(rest_sb[:], rest_bank[:].rearrange("j (u e) p -> j u p e", e=2))
-            rest[b] = rest_sb
+            rest[b, u] = keep.tile(
+                [P, P, 2], F32, name="rest%d_%d" % (b, u), tag="rest%d_%d" % (b, u), align_bytes=64
+            )
+            nc.scalar.copy(rest[b, u][:], rest_bank[:].rearrange("j e p -> j p e"))
 
         out_words = keep.tile([P, S], U32, name="out_words", align_bytes=64)
         out_scales = keep.tile([P, S], U8, name="out_scales", align_bytes=64)
@@ -161,29 +173,29 @@ def tile_picked_waveeq_none_po_kernel(
         z_grouped = {}
         o_grouped = {}
 
-        def gather(c, t, tag):
-            j0, j1 = CHUNKS[c]
-            lcols = slice(j0 // 16, j1 // 16)
-            pair = keep.tile([P, 2, j1 - j0], F32, name="pair%d_%d" % (c, t), tag=tag, align_bytes=64)
-            ge = pair[:, 0, :]
-            gw = pair[:, 1, :]
-            if FUSE == 0:
-                nc.vector.tensor_copy(ge, y[t][:].indirect(east_sb[:, lcols]))
-                nc.vector.tensor_copy(gw, y[t][:].indirect(west_sb[:, lcols]))
-            elif FUSE == 1:
-                nc.vector.tensor_tensor(ge, y[t][:].indirect(east_sb[:, lcols]), minus2y[t][:, j0:j1], ADD)
-                nc.vector.tensor_copy(gw, y[t][:].indirect(west_sb[:, lcols]))
-            else:
-                nc.vector.tensor_tensor(ge, y[t][:].indirect(east_sb[:, lcols]), minus2y[t][:, j0:j1], ADD)
-                nc.vector.tensor_tensor(gw, y[t][:].indirect(west_sb[:, lcols]), ge, ADD)
-            for b in range(j0 // P, j1 // P):
-                part = slice(P * b - j0, P * (b + 1) - j0)
-                if FUSE == 0:
-                    terms[b, t] = [minus2y[t][:, P * b : P * (b + 1)], ge[:, part], gw[:, part]]
-                elif FUSE == 1:
-                    terms[b, t] = [ge[:, part], gw[:, part]]
-                else:
-                    terms[b, t] = [gw[:, part]]
+        half = {}
+
+        def gather_east(h, t, tag):
+            j0, j1 = 256 * h, 256 * (h + 1)
+            half[h, t] = keep.tile(
+                [P, 256], F32, name="half%d_%d" % (h, t), tag=tag, align_bytes=64
+            )
+            nc.vector.tensor_tensor(
+                half[h, t][:], y[t][:].indirect(east_sb[:, j0 // 16 : j1 // 16]), minus2y[t][:, j0:j1], ADD
+            )
+
+        def gather_west(b0, b1, t, tag):
+            j0, j1 = P * b0, P * b1
+            h = j0 // 256
+            lap = keep.tile([P, j1 - j0], F32, name="lap_sb%d_%d" % (b0, t), tag=tag, align_bytes=64)
+            nc.vector.tensor_tensor(
+                lap[:],
+                y[t][:].indirect(west_sb[:, j0 // 16 : j1 // 16]),
+                half[h, t][:, j0 - 256 * h : j1 - 256 * h],
+                ADD,
+            )
+            for b in range(b0, b1):
+                terms[b, t] = [lap[:, P * (b - b0) : P * (b - b0 + 1)]]
 
         def turn(b, u):
             lap_banks[b, u] = bank((2 * b + u) % 4, [P, 2, P], "lap%d_%d" % (b, u))
@@ -192,12 +204,12 @@ def tile_picked_waveeq_none_po_kernel(
 
         def combine(b, u):
             if u == 0:
-                z_turned[b] = keep.tile([P, 2, P, 2], BF16, name="z_turned%d" % b)
+                z_turned[b] = keep.tile([P, 2, P, 2], BF16, name="z_turned%d" % b, tag=["z_turned0", "z_turned1", "half1_2", "half0_3"][b], align_bytes=64)
             nc.vector.scalar_tensor_tensor(
                 z_turned[b][:, u],
                 lap_banks[b, u][:].rearrange("j e p -> j p e"),
                 c_col[:, b : b + 1],
-                rest[b][:, u],
+                rest[b, u][:],
                 MULT,
                 SUB,
             )
@@ -232,7 +244,10 @@ def tile_picked_waveeq_none_po_kernel(
                 o_grouped[b][:].rearrange("p (j t) -> p j t", t=PACK), out_bank[:].rearrange("p t j -> p j t")
             )
             o_sb = keep.tile([P, PACK, P], F32, name="o_sb%d" % b)
-            nc.scalar.copy(o_sb[:], out_bank[:])
+            if b in (1, 2):
+                nc.vector.tensor_copy(o_sb[:], out_bank[:])
+            else:
+                nc.scalar.copy(o_sb[:], out_bank[:])
             queue = nc.scalar if b == BLOCKS - 1 else nc.sync
             queue.dma_start(out_rows[:, :, P * b : P * (b + 1)], o_sb[:])
 
@@ -241,51 +256,68 @@ def tile_picked_waveeq_none_po_kernel(
             nc.vector.quantize_mx(out=out_words[:, cols].bitcast(FP8X4), scales=out_scales[:, cols], in_=o_grouped[b][:])
             nc.sync.dma_start(out_word_rows[:, cols], out_words[:, cols].bitcast(I32))
 
+        first_product(0, [0], 4)
+        first_product(0, [1], 0)
+        for t in range(1, PACK):
+            first_product(t, [0, 1], t)
+        for h in range(2):
+            take_y(0, h)
+            take_u(0, h)
+        take_y(1, 0)
+        take_u(1, 0)
+        take_y(2, 0)
+        make_rest(0, 0)
+        make_rest(1, 0)
+        take_u(2, 0)
+        take_y(3, 0)
+        take_u(3, 0)
+        make_rest(0, 1)
+        make_rest(1, 1)
+        for b in range(2, 4):
+            for u in range(2):
+                make_rest(b, u)
         for t in range(PACK):
-            gather(0, t, "pair%d" % t)
-        turn(0, 0)
-        turn(1, 0)
-        make_rest(0)
+            gather_east(0, t, "half0_%d" % t)
+            gather_west(0, 2, t, "lap_first%d" % t)
+            if t < 3:
+                gather_east(1, t, "half1_%d" % t)
+            if t == 1:
+                turn(0, 0)
+                turn(1, 0)
+                combine(0, 0)
+                combine(1, 0)
         turn(0, 1)
         turn(1, 1)
-        make_rest(1)
-        gather(1, 0, "pair0")
-        combine(0, 0)
+        gather_east(1, 3, "half0_3")
         combine(0, 1)
         turn_back(0)
-        make_rest(2)
-        gather(1, 1, "rest0")
-        combine(1, 0)
         combine(1, 1)
         turn_back(1)
-        make_rest(3)
+        gather_west(2, 4, 0, "rest0_1")
+        gather_west(2, 4, 1, "rest1_1")
         turn(2, 0)
-        gather(1, 2, "rest1")
+        turn(3, 0)
+        gather_west(2, 4, 2, "z_turned1")
         second_product(0)
-        gather(1, 3, "z_grouped0")
-        turn(2, 1)
         second_product(1)
-        gather(2, 0, "z_grouped1")
+        gather_west(2, 4, 3, "z_grouped0")
+        turn(2, 1)
+        turn(3, 1)
         combine(2, 0)
+        combine(3, 0)
         combine(2, 1)
         turn_back(2)
-        gather(2, 1, "rest2")
-        turn(3, 0)
-        planes(0)
-        gather(2, 2, "o_grouped0")
-        second_product(2)
-        planes(1)
-        combine(3, 0)
-        gather(2, 3, "z_grouped2")
-        turn(3, 1)
         combine(3, 1)
         turn_back(3)
-        planes(2)
+        planes(0)
+        second_product(2)
         second_product(3)
+        planes(1)
+        planes(2)
         planes(3)
 
         for q in range(4):
-            queue = nc.sync if q % 2 == 0 else nc.scalar
+            queue = nc.sync if q < 3 else nc.scalar
             queue.dma_start(
                 out_2[0, 4 * q : 4 * q + 4, :].bitcast(I32), out_scales[32 * q : 32 * q + 4, :].bitcast(I32)
             )

@@ -20,8 +20,14 @@ SUB = mybir.AluOpType.subtract
 
 P = 128
 PACK = 4
+GROUP = 16
+QUAD = 32
+ROWS = 16
+SPREAD = P // ROWS
 BLOCKS = S // P
-W1_VECTOR_M = 80
+HALF = S // 2
+W1_ON_VECTOR = 72
+LAST = PACK - 1
 
 
 def tile_picked_waveeq_none_po_kernel(
@@ -36,20 +42,32 @@ def tile_picked_waveeq_none_po_kernel(
         def bank(index, shape, name):
             return psum.tile(shape, F32, name=name, tag="bank%d" % index)
 
-        offs_sb = lists.tile([P, S // 16], U16, name="offs_sb")
-        east_sb = lists.tile([P, S // 16], U16, name="east_sb")
-        west_sb = lists.tile([P, S // 16], U16, name="west_sb")
+        def half_cols(h):
+            return slice(HALF * h, HALF * (h + 1))
 
+        def block_cols(b):
+            return slice(P * b, P * (b + 1))
+
+        def list_cols(h):
+            return slice(HALF * h // GROUP, HALF * (h + 1) // GROUP)
+
+        def spread_rows(scales):
+            rows = scales[0].bitcast(I32)
+            return rows.unsqueeze(1).to_broadcast([ROWS, SPREAD, rows.shape[1]])
+
+        def place_rows(plane, spread):
+            for a in range(PACK):
+                nc.sync.dma_start(plane[a:P:QUAD].bitcast(I32), spread[SPREAD * a : P : QUAD].bitcast(I32))
+
+        offs_sb = lists.tile([P, S // GROUP], U16, name="offs_sb")
+        east_sb = lists.tile([P, S // GROUP], U16, name="east_sb")
+        west_sb = lists.tile([P, S // GROUP], U16, name="west_sb")
         nc.sync.dma_start(offs_sb[:], offs)
-        xs_window = keep.tile([P, T], U8, name="xs_window", tag="early", align_bytes=64)
-        nc.sync.dma_start(
-            xs_window[:].bitcast(I32), x_scales[0].bitcast(I32).unsqueeze(1).to_broadcast([16, 8, T // 4])
-        )
+        xs_window = keep.tile([P, T], U8, name="xs_window", tag="xs_window", align_bytes=64)
+        nc.sync.dma_start(xs_window[:].bitcast(I32), spread_rows(x_scales))
         w2s_raw = keep.tile([P, N], U8, name="w2s_raw", align_bytes=64)
-        nc.sync.dma_start(
-            w2s_raw[:].bitcast(I32), w2_scales[0].bitcast(I32).unsqueeze(1).to_broadcast([16, 8, N // 4])
-        )
-        w1_raw = keep.tile([P, PACK, H], F32, name="w1_raw", tag="big")
+        nc.sync.dma_start(w2s_raw[:].bitcast(I32), spread_rows(w2_scales))
+        w1_raw = keep.tile([P, PACK, H], F32, name="w1_raw", tag="w1_raw")
         nc.sync.dma_start(w1_raw[:], w1.rearrange("(p j) c -> p j c", j=PACK))
         x_window = keep.tile([P, T], I32, name="x_window", align_bytes=64)
         nc.sync.dma_start(x_window[:], x_words[0].rearrange("p n t -> p (n t)").bitcast(I32))
@@ -61,44 +79,38 @@ def tile_picked_waveeq_none_po_kernel(
         c_rows = keep.tile([P, P], F32, name="c_rows")
         nc.gpsimd.memset(c_rows[:], 0.0)
         nc.gpsimd.dma_start(c_rows[0:BLOCKS, :], c2[0:1, :].rearrange("a (b j) -> (a b) j", j=P))
-        w2_planes = keep.tile([P, PACK, P], U8, name="w2_planes", align_bytes=64)
-        nc.gpsimd.memset(w2_planes[:].bitcast(I32), 0)
-
         c_bank = bank(7, [P, P], "c_bank")
         nc.tensor.transpose(c_bank[:], c_rows[:], ident[:])
         c_col = keep.tile([P, BLOCKS], F32, name="c_col")
         nc.scalar.copy(c_col[:], c_bank[:, 0:BLOCKS])
 
-        xs_plane = keep.tile([P, S], U8, name="xs_plane", align_bytes=64)
+        xs_plane = keep.tile([P, S], U8, name="xs_plane", tag="xs_plane", align_bytes=64)
         nc.vector.memset(xs_plane[:].bitcast(I32), 0)
         xs_picked = keep.tile([P, S], U8, name="xs_picked", align_bytes=64)
         nc.vector.tensor_copy(xs_picked[:], xs_window[:].indirect(offs_sb[:]))
-        for a in range(4):
-            nc.sync.dma_start(xs_plane[a:P:32, :].bitcast(I32), xs_picked[8 * a : P : 32, :].bitcast(I32))
+        place_rows(xs_plane, xs_picked)
 
         w2s_dealt = keep.tile([P, PACK, P], U8, name="w2s_dealt", align_bytes=64)
         nc.vector.tensor_copy(
             w2s_dealt[:].rearrange("p t (g i) -> p g t i", i=16),
             w2s_raw[:].rearrange("p (g i t) -> p g t i", i=16, t=PACK),
         )
-        for a in range(4):
-            nc.gpsimd.dma_start(w2_planes[a:P:32].bitcast(I32), w2s_dealt[8 * a : P : 32].bitcast(I32))
 
-        w2_raw = keep.tile([P, N], I32, name="w2_raw", tag="early", align_bytes=64)
+        w2_raw = keep.tile([P, N], I32, name="w2_raw", tag="xs_window", align_bytes=64)
         nc.sync.dma_start(w2_raw[:], w2_words[0].rearrange("p n t -> p (n t)").bitcast(I32))
 
         w1_grouped = keep.tile([P, PACK, P, PACK], BF16, name="w1_grouped", tag="w1_grouped", align_bytes=64)
         w1_dst = w1_grouped[:].rearrange("p t m j -> p m t j")
         w1_src = w1_raw[:].rearrange("p j (m t) -> p m t j", t=PACK)
-        nc.vector.tensor_copy(w1_dst[:, 0:W1_VECTOR_M], w1_src[:, 0:W1_VECTOR_M])
-        nc.scalar.copy(w1_dst[:, W1_VECTOR_M:P], w1_src[:, W1_VECTOR_M:P])
+        nc.vector.tensor_copy(w1_dst[:, 0:W1_ON_VECTOR], w1_src[:, 0:W1_ON_VECTOR])
+        nc.scalar.copy(w1_dst[:, W1_ON_VECTOR:P], w1_src[:, W1_ON_VECTOR:P])
         w1_codes = keep.tile([P, H], U32, name="w1_codes", align_bytes=64)
         w1_scales = keep.tile([P, H], U8, name="w1_scales", align_bytes=64)
         nc.vector.quantize_mx(
             out=w1_codes[:].bitcast(FP8X4), scales=w1_scales[:], in_=w1_grouped[:].rearrange("p t m j -> p (t m j)")
         )
 
-        prev_sb = keep.tile([P, 2, PACK, S // 2], F32, name="prev_sb", tag="big")
+        prev_sb = keep.tile([P, 2, PACK, HALF], F32, name="prev_sb", tag="w1_raw")
         prev_rows = prev.rearrange("(p t) (h j) -> p h t j", t=PACK, h=2)
         for h in range(2):
             nc.sync.dma_start(prev_sb[:, h], prev_rows[:, h])
@@ -106,8 +118,7 @@ def tile_picked_waveeq_none_po_kernel(
         x_picked = keep.tile([P, S], U32, name="x_picked", tag="w1_grouped", align_bytes=64)
         for h in range(2):
             nc.vector.tensor_copy(
-                x_picked[:, 256 * h : 256 * (h + 1)],
-                x_window[:].bitcast(U32).indirect(offs_sb[:, 16 * h : 16 * (h + 1)]),
+                x_picked[:, half_cols(h)], x_window[:].bitcast(U32).indirect(offs_sb[:, list_cols(h)])
             )
 
         w2_codes = keep.tile([P, PACK, P], I32, name="w2_codes", align_bytes=64)
@@ -118,96 +129,72 @@ def tile_picked_waveeq_none_po_kernel(
 
         y = [keep.tile([P, S], F32, name="y%d" % t) for t in range(PACK)]
         minus2y = [keep.tile([P, S], F32, name="minus2y%d" % t) for t in range(PACK)]
-        y_banks = {}
-
-        def first_product(t, halves, index):
-            y_bank = bank(index, [P, 256 * len(halves)], "y_bank%d_%d" % (t, halves[0]))
-            for n, h in enumerate(halves):
-                cols = slice(256 * h, 256 * (h + 1))
-                nc.tensor.matmul_mx(
-                    out=y_bank[:, 256 * n : 256 * (n + 1)],
-                    lhsT=w1_codes[:, P * t : P * (t + 1)].bitcast(FP8X4),
-                    lhsT_scale=w1_scales[:, P * t : P * (t + 1)],
-                    rhs=x_picked[:, cols].bitcast(FP8X4),
-                    rhs_scale=xs_plane[:, cols],
-                    start=True,
-                    stop=True,
-                )
-            y_banks[t, halves[0]] = (y_bank, slice(256 * halves[0], 256 * (halves[-1] + 1)))
-
-        def take_y(t, h):
-            y_bank, cols = y_banks[t, h]
-            nc.scalar.copy(y[t][:, cols], y_bank[:])
-
-        def take_u(t, h):
-            y_bank, cols = y_banks[t, h]
-            nc.scalar.activation(minus2y[t][:, cols], y_bank[:], COPY, scale=-2.0)
-
-        def add_transposed(dst, terms):
-            for n, term in enumerate(terms):
-                nc.tensor.matmul(dst, term, ident[:], start=(n == 0), stop=(n == len(terms) - 1), is_transpose=True)
-
-        rest = {}
-
-        def make_rest(b, u):
-            rest_bank = bank(4 + (len(rest) + 1) % 4, [P, 2, P], "rest_bank%d_%d" % (b, u))
-            j0 = P * (b % 2)
-            for e in range(2):
-                t = 2 * u + e
-                add_transposed(
-                    rest_bank[:, e, :], [prev_sb[:, b // 2, t, j0 : j0 + P], minus2y[t][:, P * b : P * (b + 1)]]
-                )
-            rest[b, u] = keep.tile(
-                [P, P, 2], F32, name="rest%d_%d" % (b, u), tag="rest%d_%d" % (b, u), align_bytes=64
-            )
-            nc.scalar.copy(rest[b, u][:], rest_bank[:].rearrange("j e p -> j p e"))
-
         out_words = keep.tile([P, S], U32, name="out_words", align_bytes=64)
         out_scales = keep.tile([P, S], U8, name="out_scales", align_bytes=64)
         out_rows = out_0.rearrange("(p t) j -> p t j", t=PACK)
         out_word_rows = out_1[0].rearrange("p n t -> p (n t)").bitcast(I32)
+        rest, east_sum, lap, lap_turned, z_turned, z_grouped, out_grouped = {}, {}, {}, {}, {}, {}, {}
 
-        terms = {}
-        lap_banks = {}
-        z_turned = {}
-        z_grouped = {}
-        o_grouped = {}
+        def first_product(t, halves, index):
+            y_bank = bank(index, [P, HALF * len(halves)], "y_bank%d_%d" % (t, halves[0]))
+            for n, h in enumerate(halves):
+                nc.tensor.matmul_mx(
+                    out=y_bank[:, half_cols(n)],
+                    lhsT=w1_codes[:, block_cols(t)].bitcast(FP8X4),
+                    lhsT_scale=w1_scales[:, block_cols(t)],
+                    rhs=x_picked[:, half_cols(h)].bitcast(FP8X4),
+                    rhs_scale=xs_plane[:, half_cols(h)],
+                    start=True,
+                    stop=True,
+                )
+            return y_bank, slice(HALF * halves[0], HALF * (halves[-1] + 1))
 
-        half = {}
+        def take_y(t, product):
+            y_bank, cols = product
+            nc.scalar.copy(y[t][:, cols], y_bank[:])
+            nc.scalar.activation(minus2y[t][:, cols], y_bank[:], COPY, scale=-2.0)
+
+        def make_rest(b, u):
+            rest_bank = bank(4 + (len(rest) + 1) % 4, [P, 2, P], "rest_bank%d_%d" % (b, u))
+            for e in range(2):
+                t = 2 * u + e
+                prev_part = prev_sb[:, b // 2, t, block_cols(b % 2)]
+                dst = rest_bank[:, e, :]
+                nc.tensor.matmul(dst, prev_part, ident[:], start=True, stop=False, is_transpose=True)
+                nc.tensor.matmul(dst, minus2y[t][:, block_cols(b)], ident[:], start=False, stop=True, is_transpose=True)
+            tag = "rest%d_%d" % (b, u)
+            rest[b, u] = keep.tile([P, P, 2], F32, name=tag, tag=tag, align_bytes=64)
+            nc.scalar.copy(rest[b, u][:], rest_bank[:].rearrange("j e p -> j p e"))
 
         def gather_east(h, t, tag):
-            j0, j1 = 256 * h, 256 * (h + 1)
-            half[h, t] = keep.tile(
-                [P, 256], F32, name="half%d_%d" % (h, t), tag=tag, align_bytes=64
-            )
+            east_sum[h, t] = keep.tile([P, HALF], F32, name="east_sum%d_%d" % (h, t), tag=tag, align_bytes=64)
             nc.vector.tensor_tensor(
-                half[h, t][:], y[t][:].indirect(east_sb[:, j0 // 16 : j1 // 16]), minus2y[t][:, j0:j1], ADD
+                east_sum[h, t][:], y[t][:].indirect(east_sb[:, list_cols(h)]), minus2y[t][:, half_cols(h)], ADD
             )
 
-        def gather_west(b0, b1, t, tag):
-            j0, j1 = P * b0, P * b1
-            h = j0 // 256
-            lap = keep.tile([P, j1 - j0], F32, name="lap_sb%d_%d" % (b0, t), tag=tag, align_bytes=64)
-            nc.vector.tensor_tensor(
-                lap[:],
-                y[t][:].indirect(west_sb[:, j0 // 16 : j1 // 16]),
-                half[h, t][:, j0 - 256 * h : j1 - 256 * h],
-                ADD,
-            )
-            for b in range(b0, b1):
-                terms[b, t] = [lap[:, P * (b - b0) : P * (b - b0 + 1)]]
+        def gather_west(h, t, tag):
+            lap[h, t] = keep.tile([P, HALF], F32, name="lap%d_%d" % (h, t), tag=tag, align_bytes=64)
+            nc.vector.tensor_tensor(lap[h, t][:], y[t][:].indirect(west_sb[:, list_cols(h)]), east_sum[h, t][:], ADD)
 
         def turn(b, u):
-            lap_banks[b, u] = bank((2 * b + u) % 4, [P, 2, P], "lap%d_%d" % (b, u))
+            lap_turned[b, u] = bank((2 * b + u) % 4, [P, 2, P], "lap_turned%d_%d" % (b, u))
             for e in range(2):
-                add_transposed(lap_banks[b, u][:, e, :], terms[b, 2 * u + e])
+                nc.tensor.matmul(
+                    lap_turned[b, u][:, e, :],
+                    lap[b // 2, 2 * u + e][:, block_cols(b % 2)],
+                    ident[:],
+                    start=True,
+                    stop=True,
+                    is_transpose=True,
+                )
+
+        def new_z_turned(b, tag):
+            z_turned[b] = keep.tile([P, 2, P, 2], BF16, name="z_turned%d" % b, tag=tag, align_bytes=64)
 
         def combine(b, u):
-            if u == 0:
-                z_turned[b] = keep.tile([P, 2, P, 2], BF16, name="z_turned%d" % b, tag=["z_turned0", "z_turned1", "half1_2", "half0_3"][b], align_bytes=64)
             nc.vector.scalar_tensor_tensor(
                 z_turned[b][:, u],
-                lap_banks[b, u][:].rearrange("j e p -> j p e"),
+                lap_turned[b, u][:].rearrange("j e p -> j p e"),
                 c_col[:, b : b + 1],
                 rest[b, u][:],
                 MULT,
@@ -215,11 +202,12 @@ def tile_picked_waveeq_none_po_kernel(
             )
 
         def turn_back(b):
-            words = z_turned[b][:].rearrange("j u p e -> j (u p e)").bitcast(F32)
+            pairs = z_turned[b][:].rearrange("j u p e -> j (u p e)").bitcast(F32)
             back = bank(4 + b % 2, [P, 2, P], "back%d" % b)
             for u in range(2):
-                nc.tensor.transpose(back[:, u, :], words[:, P * u : P * (u + 1)], ident[:])
-            z_grouped[b] = keep.tile([P, P * PACK], BF16, name="z_grouped%d" % b, tag="z_grouped%d" % b, align_bytes=64)
+                nc.tensor.transpose(back[:, u, :], pairs[:, block_cols(u)], ident[:])
+            tag = "z_grouped%d" % b
+            z_grouped[b] = keep.tile([P, P * PACK], BF16, name=tag, tag=tag, align_bytes=64)
             nc.scalar.copy(
                 z_grouped[b][:].bitcast(F32).rearrange("p (j u) -> p j u", u=2), back[:].rearrange("p u j -> p j u")
             )
@@ -233,91 +221,94 @@ def tile_picked_waveeq_none_po_kernel(
                 nc.tensor.matmul_mx(
                     out=out_bank[:, t, :],
                     lhsT=w2_codes[:, t, :].bitcast(FP8X4),
-                    lhsT_scale=w2_planes[:, t, :],
+                    lhsT_scale=w2_plane[:, t, :],
                     rhs=z_codes[:].bitcast(FP8X4),
                     rhs_scale=z_scales[:],
                     start=True,
                     stop=True,
                 )
-            o_grouped[b] = keep.tile([P, P * PACK], BF16, name="o_grouped%d" % b, tag="o_grouped%d" % b, align_bytes=64)
+            out_grouped[b] = keep.tile([P, P * PACK], BF16, name="out_grouped%d" % b, align_bytes=64)
             nc.scalar.copy(
-                o_grouped[b][:].rearrange("p (j t) -> p j t", t=PACK), out_bank[:].rearrange("p t j -> p j t")
+                out_grouped[b][:].rearrange("p (j t) -> p j t", t=PACK), out_bank[:].rearrange("p t j -> p j t")
             )
-            o_sb = keep.tile([P, PACK, P], F32, name="o_sb%d" % b)
-            if b in (1, 2):
-                nc.vector.tensor_copy(o_sb[:], out_bank[:])
+            out_sb = keep.tile([P, PACK, P], F32, name="out_sb%d" % b)
+            if 0 < b < LAST:
+                nc.vector.tensor_copy(out_sb[:], out_bank[:])
             else:
-                nc.scalar.copy(o_sb[:], out_bank[:])
-            queue = nc.scalar if b == BLOCKS - 1 else nc.sync
-            queue.dma_start(out_rows[:, :, P * b : P * (b + 1)], o_sb[:])
+                nc.scalar.copy(out_sb[:], out_bank[:])
+            queue = nc.scalar if b == LAST else nc.sync
+            queue.dma_start(out_rows[:, :, block_cols(b)], out_sb[:])
 
-        def planes(b):
-            cols = slice(P * b, P * (b + 1))
-            nc.vector.quantize_mx(out=out_words[:, cols].bitcast(FP8X4), scales=out_scales[:, cols], in_=o_grouped[b][:])
+        def hand_on(b):
+            cols = block_cols(b)
+            nc.vector.quantize_mx(
+                out=out_words[:, cols].bitcast(FP8X4), scales=out_scales[:, cols], in_=out_grouped[b][:]
+            )
             nc.sync.dma_start(out_word_rows[:, cols], out_words[:, cols].bitcast(I32))
 
-        first_product(0, [0], 4)
-        first_product(0, [1], 0)
-        for t in range(1, PACK):
-            first_product(t, [0, 1], t)
-        for h in range(2):
-            take_y(0, h)
-            take_u(0, h)
-        take_y(1, 0)
-        take_u(1, 0)
-        take_y(2, 0)
-        make_rest(0, 0)
-        make_rest(1, 0)
-        take_u(2, 0)
-        take_y(3, 0)
-        take_u(3, 0)
-        make_rest(0, 1)
-        make_rest(1, 1)
-        for b in range(2, 4):
-            for u in range(2):
-                make_rest(b, u)
-        for t in range(PACK):
-            gather_east(0, t, "half0_%d" % t)
-            gather_west(0, 2, t, "lap_first%d" % t)
-            if t < 3:
-                gather_east(1, t, "half1_%d" % t)
-            if t == 1:
-                turn(0, 0)
-                turn(1, 0)
-                combine(0, 0)
-                combine(1, 0)
-        turn(0, 1)
-        turn(1, 1)
-        gather_east(1, 3, "half0_3")
-        combine(0, 1)
-        turn_back(0)
-        combine(1, 1)
-        turn_back(1)
-        gather_west(2, 4, 0, "rest0_1")
-        gather_west(2, 4, 1, "rest1_1")
-        turn(2, 0)
-        turn(3, 0)
-        gather_west(2, 4, 2, "z_turned1")
-        second_product(0)
-        second_product(1)
-        gather_west(2, 4, 3, "z_grouped0")
-        turn(2, 1)
-        turn(3, 1)
-        combine(2, 0)
-        combine(3, 0)
-        combine(2, 1)
-        turn_back(2)
-        combine(3, 1)
-        turn_back(3)
-        planes(0)
-        second_product(2)
-        second_product(3)
-        planes(1)
-        planes(2)
-        planes(3)
+        plane0 = [first_product(0, [0], 4), first_product(0, [1], 0)]
+        later_planes = {t: first_product(t, [0, 1], t) for t in range(1, PACK)}
 
-        for q in range(4):
-            queue = nc.sync if q < 3 else nc.scalar
+        w2_plane = keep.tile([P, PACK, P], U8, name="w2_plane", tag="xs_plane", align_bytes=64)
+        nc.gpsimd.memset(w2_plane[:].bitcast(I32), 0)
+        place_rows(w2_plane, w2s_dealt)
+
+        for product in plane0:
+            take_y(0, product)
+        take_y(1, later_planes[1])
+        take_y(2, later_planes[2])
+        for b in (0, 1):
+            make_rest(b, 0)
+        take_y(3, later_planes[3])
+        for b in (2, 3):
+            make_rest(b, 0)
+        for b in range(BLOCKS):
+            make_rest(b, 1)
+
+        for t in range(PACK):
+            gather_east(0, t, "east_sum0_%d" % t)
+            gather_west(0, t, "lap0_%d" % t)
+            if t < LAST:
+                gather_east(1, t, "east_sum1_%d" % t)
+            if t == LAST - 1:
+                for b in (0, 1):
+                    turn(b, 0)
+                for b in (0, 1):
+                    new_z_turned(b, "z_turned%d" % b)
+                    combine(b, 0)
+        for b in (0, 1):
+            turn(b, 1)
+        gather_east(1, LAST, "east_sum0_%d" % LAST)
+        for b in (0, 1):
+            combine(b, 1)
+            turn_back(b)
+
+        gather_west(1, 0, "rest0_1")
+        gather_west(1, 1, "rest1_1")
+        for b in (2, 3):
+            turn(b, 0)
+        gather_west(1, 2, "z_turned1")
+        for b in (0, 1):
+            second_product(b)
+        gather_west(1, 3, "z_grouped0")
+        for b in (2, 3):
+            turn(b, 1)
+        new_z_turned(2, "east_sum1_2")
+        combine(2, 0)
+        new_z_turned(3, "east_sum0_%d" % LAST)
+        combine(3, 0)
+        for b in (2, 3):
+            combine(b, 1)
+            turn_back(b)
+        hand_on(0)
+        for b in (2, 3):
+            second_product(b)
+        for b in range(1, BLOCKS):
+            hand_on(b)
+
+        for q in range(P // QUAD):
+            queue = nc.scalar if q == LAST else nc.sync
             queue.dma_start(
-                out_2[0, 4 * q : 4 * q + 4, :].bitcast(I32), out_scales[32 * q : 32 * q + 4, :].bitcast(I32)
+                out_2[0, PACK * q : PACK * (q + 1), :].bitcast(I32),
+                out_scales[QUAD * q : QUAD * q + PACK, :].bitcast(I32),
             )

@@ -26,8 +26,9 @@ ROWS = 16
 SPREAD = P // ROWS
 BLOCKS = S // P
 HALF = S // 2
-W1_ON_VECTOR = 72
 LAST = PACK - 1
+TURNED = 3
+AB = TURNED * P
 
 
 def tile_picked_waveeq_none_po_kernel(
@@ -37,173 +38,153 @@ def tile_picked_waveeq_none_po_kernel(
     with ExitStack() as ctx:
         lists = ctx.enter_context(tc.tile_pool(name="lists", bufs=1))
         keep = ctx.enter_context(tc.tile_pool(name="keep", bufs=1))
+        shared = ctx.enter_context(tc.tile_pool(name="shared", bufs=1))
         psum = ctx.enter_context(tc.psum_pool(name="psum", bufs=1))
 
         def bank(index, shape, name):
             return psum.tile(shape, F32, name=name, tag="bank%d" % index)
 
-        def half_cols(h):
-            return slice(HALF * h, HALF * (h + 1))
+        def cols(first, count):
+            return slice(first, first + count)
 
         def block_cols(b):
-            return slice(P * b, P * (b + 1))
+            return cols(P * b, P)
 
-        def list_cols(h):
-            return slice(HALF * h // GROUP, HALF * (h + 1) // GROUP)
-
-        def spread_rows(scales):
-            rows = scales[0].bitcast(I32)
-            return rows.unsqueeze(1).to_broadcast([ROWS, SPREAD, rows.shape[1]])
-
-        def place_rows(plane, spread):
-            for a in range(PACK):
-                nc.sync.dma_start(plane[a:P:QUAD].bitcast(I32), spread[SPREAD * a : P : QUAD].bitcast(I32))
+        def list_cols(span):
+            return slice(span.start // GROUP, span.stop // GROUP)
 
         offs_sb = lists.tile([P, S // GROUP], U16, name="offs_sb")
         east_sb = lists.tile([P, S // GROUP], U16, name="east_sb")
         west_sb = lists.tile([P, S // GROUP], U16, name="west_sb")
-        nc.sync.dma_start(offs_sb[:], offs)
         xs_window = keep.tile([P, T], U8, name="xs_window", tag="xs_window", align_bytes=64)
-        nc.sync.dma_start(xs_window[:].bitcast(I32), spread_rows(x_scales))
-        w2s_raw = keep.tile([P, N], U8, name="w2s_raw", align_bytes=64)
-        nc.sync.dma_start(w2s_raw[:].bitcast(I32), spread_rows(w2_scales))
-        w1_raw = keep.tile([P, PACK, H], F32, name="w1_raw", tag="w1_raw")
-        nc.sync.dma_start(w1_raw[:], w1.rearrange("(p j) c -> p j c", j=PACK))
-        x_window = keep.tile([P, T], I32, name="x_window", align_bytes=64)
-        nc.sync.dma_start(x_window[:], x_words[0].rearrange("p n t -> p (n t)").bitcast(I32))
+        nc.gpsimd.memset(xs_window[:].bitcast(I32), 0)
+        nc.sync.dma_start(offs_sb[:], offs)
         nc.sync.dma_start(east_sb[:], east)
         nc.sync.dma_start(west_sb[:], west)
-
+        nc.sync.dma_start(xs_window[0:P:SPREAD].bitcast(I32), x_scales[0].bitcast(I32))
+        w1_raw = keep.tile([P, PACK, H], F32, name="w1_raw", tag="w1_raw")
+        nc.sync.dma_start(w1_raw[:], w1.rearrange("(p j) c -> p j c", j=PACK))
+        x_window = shared.tile([P, T], I32, name="x_window", offset=0, align_bytes=64)
+        nc.sync.dma_start(x_window[:], x_words[0].rearrange("p n t -> p (n t)").bitcast(I32))
+        w2_raw = keep.tile([P, N], I32, name="w2_raw", align_bytes=64)
+        nc.sync.dma_start(w2_raw[:], w2_words[0].rearrange("p n t -> p (n t)").bitcast(I32))
+        w2s_raw = keep.tile([P, N], U8, name="w2s_raw", align_bytes=64)
+        w2s_rows = w2_scales[0].bitcast(I32)
+        nc.sync.dma_start(w2s_raw[:].bitcast(I32), w2s_rows.unsqueeze(1).to_broadcast([ROWS, SPREAD, N // 4]))
         ident = keep.tile([P, P], F32, name="ident")
         make_identity(nc, ident[:])
-        c_rows = keep.tile([P, P], F32, name="c_rows")
-        nc.gpsimd.memset(c_rows[:], 0.0)
-        nc.gpsimd.dma_start(c_rows[0:BLOCKS, :], c2[0:1, :].rearrange("a (b j) -> (a b) j", j=P))
-        c_bank = bank(7, [P, P], "c_bank")
-        nc.tensor.transpose(c_bank[:], c_rows[:], ident[:])
-        c_col = keep.tile([P, BLOCKS], F32, name="c_col")
-        nc.scalar.copy(c_col[:], c_bank[:, 0:BLOCKS])
+        w2_plane = keep.tile([P, PACK, P], U8, name="w2_plane", align_bytes=64)
+        nc.gpsimd.memset(w2_plane[:].bitcast(I32), 0)
 
-        xs_plane = keep.tile([P, S], U8, name="xs_plane", tag="xs_plane", align_bytes=64)
+        xs_plane = keep.tile([P, S], U8, name="xs_plane", align_bytes=64)
         nc.vector.memset(xs_plane[:].bitcast(I32), 0)
         xs_picked = keep.tile([P, S], U8, name="xs_picked", align_bytes=64)
         nc.vector.tensor_copy(xs_picked[:], xs_window[:].indirect(offs_sb[:]))
-        place_rows(xs_plane, xs_picked)
-
-        w2s_dealt = keep.tile([P, PACK, P], U8, name="w2s_dealt", align_bytes=64)
-        nc.vector.tensor_copy(
-            w2s_dealt[:].rearrange("p t (g i) -> p g t i", i=16),
-            w2s_raw[:].rearrange("p (g i t) -> p g t i", i=16, t=PACK),
-        )
-
-        w2_raw = keep.tile([P, N], I32, name="w2_raw", tag="xs_window", align_bytes=64)
-        nc.sync.dma_start(w2_raw[:], w2_words[0].rearrange("p n t -> p (n t)").bitcast(I32))
+        for a in range(PACK):
+            nc.scalar.dma_start(xs_plane[a:P:QUAD].bitcast(I32), xs_picked[SPREAD * a : P : QUAD].bitcast(I32))
 
         w1_grouped = keep.tile([P, PACK, P, PACK], BF16, name="w1_grouped", tag="w1_grouped", align_bytes=64)
-        w1_dst = w1_grouped[:].rearrange("p t m j -> p m t j")
-        w1_src = w1_raw[:].rearrange("p j (m t) -> p m t j", t=PACK)
-        nc.vector.tensor_copy(w1_dst[:, 0:W1_ON_VECTOR], w1_src[:, 0:W1_ON_VECTOR])
-        nc.scalar.copy(w1_dst[:, W1_ON_VECTOR:P], w1_src[:, W1_ON_VECTOR:P])
+        nc.vector.tensor_copy(
+            w1_grouped[:].rearrange("p t m j -> p m t j"), w1_raw[:].rearrange("p j (m t) -> p m t j", t=PACK)
+        )
         w1_codes = keep.tile([P, H], U32, name="w1_codes", align_bytes=64)
         w1_scales = keep.tile([P, H], U8, name="w1_scales", align_bytes=64)
         nc.vector.quantize_mx(
             out=w1_codes[:].bitcast(FP8X4), scales=w1_scales[:], in_=w1_grouped[:].rearrange("p t m j -> p (t m j)")
         )
 
-        prev_sb = keep.tile([P, 2, PACK, HALF], F32, name="prev_sb", tag="w1_raw")
-        prev_rows = prev.rearrange("(p t) (h j) -> p h t j", t=PACK, h=2)
-        for h in range(2):
-            nc.sync.dma_start(prev_sb[:, h], prev_rows[:, h])
+        prev_sb = keep.tile([P, PACK, S], F32, name="prev_sb", tag="w1_raw")
+        nc.sync.dma_start(prev_sb[:], prev.rearrange("(p t) j -> p t j", t=PACK))
 
         x_picked = keep.tile([P, S], U32, name="x_picked", tag="w1_grouped", align_bytes=64)
         for h in range(2):
-            nc.vector.tensor_copy(
-                x_picked[:, half_cols(h)], x_window[:].bitcast(U32).indirect(offs_sb[:, list_cols(h)])
-            )
+            span = cols(HALF * h, HALF)
+            nc.vector.tensor_copy(x_picked[:, span], x_window[:].bitcast(U32).indirect(offs_sb[:, list_cols(span)]))
 
-        w2_codes = keep.tile([P, PACK, P], I32, name="w2_codes", align_bytes=64)
+        w2_codes = shared.tile([P, PACK, P], I32, name="w2_codes", offset=0, align_bytes=64)
         nc.vector.tensor_copy(
             w2_codes[:].rearrange("p t (g i) -> p g t i", i=4),
             w2_raw[:].rearrange("p (g i t) -> p g t i", i=4, t=PACK),
         )
+        w2s_dealt = shared.tile([P, PACK, P], U8, name="w2s_dealt", offset=2048, align_bytes=64)
+        nc.vector.tensor_copy(
+            w2s_dealt[:].rearrange("p t (g i) -> p g t i", i=16),
+            w2s_raw[:].rearrange("p (g i t) -> p g t i", i=16, t=PACK),
+        )
+        c_rows = shared.tile([P, P], F32, name="c_rows", offset=5120, align_bytes=64)
+        nc.sync.dma_start(c_rows[:], c2.rearrange("r (b j) -> (r b) j", j=P)[0:P, :])
+        c_last = shared.tile([P, P], F32, name="c_last", offset=4096, align_bytes=64)
+        nc.sync.dma_start(c_last[:], c2[:, block_cols(LAST)])
+
+        for a in range(PACK):
+            nc.sync.dma_start(w2_plane[a:P:QUAD].bitcast(I32), w2s_dealt[SPREAD * a : P : QUAD].bitcast(I32))
+
+        c_bank = bank(7, [P, P], "c_bank")
+        nc.tensor.transpose(c_bank[:], c_rows[:], ident[:])
+        c_col = keep.tile([P, BLOCKS], F32, name="c_col")
+        nc.scalar.copy(c_col[:], c_bank[:, 0:BLOCKS])
 
         y = [keep.tile([P, S], F32, name="y%d" % t) for t in range(PACK)]
-        minus2y = [keep.tile([P, S], F32, name="minus2y%d" % t) for t in range(PACK)]
+        m2y = [keep.tile([P, AB], F32, name="m2y%d" % t, tag="m2y%d" % t, align_bytes=64) for t in range(PACK)]
+        m2y_last = keep.tile([P, PACK, P], F32, name="m2y_last")
         out_words = keep.tile([P, S], U32, name="out_words", align_bytes=64)
         out_scales = keep.tile([P, S], U8, name="out_scales", align_bytes=64)
         out_rows = out_0.rearrange("(p t) j -> p t j", t=PACK)
         out_word_rows = out_1[0].rearrange("p n t -> p (n t)").bitcast(I32)
-        rest, east_sum, lap, lap_turned, z_turned, z_grouped, out_grouped = {}, {}, {}, {}, {}, {}, {}
+        rest, lap_turned, z_turned, z_grouped, out_grouped = {}, {}, {}, {}, {}
 
-        def first_product(t, halves, index):
-            y_bank = bank(index, [P, HALF * len(halves)], "y_bank%d_%d" % (t, halves[0]))
-            for n, h in enumerate(halves):
-                nc.tensor.matmul_mx(
-                    out=y_bank[:, half_cols(n)],
-                    lhsT=w1_codes[:, block_cols(t)].bitcast(FP8X4),
-                    lhsT_scale=w1_scales[:, block_cols(t)],
-                    rhs=x_picked[:, half_cols(h)].bitcast(FP8X4),
-                    rhs_scale=xs_plane[:, half_cols(h)],
-                    start=True,
-                    stop=True,
-                )
-            return y_bank, slice(HALF * halves[0], HALF * (halves[-1] + 1))
+        def first_product(t, span, index):
+            y_bank = bank(index, [P, span.stop - span.start], "y_bank%d_%d" % (t, span.start))
+            nc.tensor.matmul_mx(
+                out=y_bank[:],
+                lhsT=w1_codes[:, block_cols(t)].bitcast(FP8X4),
+                lhsT_scale=w1_scales[:, block_cols(t)],
+                rhs=x_picked[:, span].bitcast(FP8X4),
+                rhs_scale=xs_plane[:, span],
+                start=True,
+                stop=True,
+            )
+            return y_bank
 
-        def take_y(t, product):
-            y_bank, cols = product
-            nc.scalar.copy(y[t][:, cols], y_bank[:])
-            nc.scalar.activation(minus2y[t][:, cols], y_bank[:], COPY, scale=-2.0)
+        def take_y(t, span, y_bank):
+            nc.scalar.copy(y[t][:, span], y_bank[:])
+            width = min(span.stop, AB) - span.start
+            nc.scalar.activation(m2y[t][:, cols(span.start, width)], y_bank[:, 0:width], COPY, scale=-2.0)
+            if span.stop > AB:
+                nc.scalar.activation(m2y_last[:, t, :], y_bank[:, cols(width, P)], COPY, scale=-2.0)
 
-        def make_rest(b, u):
-            rest_bank = bank(4 + (len(rest) + 1) % 4, [P, 2, P], "rest_bank%d_%d" % (b, u))
+        def turn_into(dst, src, start, stop):
+            nc.tensor.matmul(dst, src, ident[:], start=start, stop=stop, is_transpose=True)
+
+        def make_rest(blocks, u, index):
+            rest_bank = bank(index, [P, len(blocks), 2, P], "rest_bank%d_%d" % (blocks[0], u))
             for e in range(2):
                 t = 2 * u + e
-                prev_part = prev_sb[:, b // 2, t, block_cols(b % 2)]
-                dst = rest_bank[:, e, :]
-                nc.tensor.matmul(dst, prev_part, ident[:], start=True, stop=False, is_transpose=True)
-                nc.tensor.matmul(dst, minus2y[t][:, block_cols(b)], ident[:], start=False, stop=True, is_transpose=True)
-            tag = "rest%d_%d" % (b, u)
-            rest[b, u] = keep.tile([P, P, 2], F32, name=tag, tag=tag, align_bytes=64)
-            nc.scalar.copy(rest[b, u][:], rest_bank[:].rearrange("j e p -> j p e"))
+                for n, b in enumerate(blocks):
+                    turn_into(rest_bank[:, n, e, :], prev_sb[:, t, block_cols(b)], True, False)
+                    turn_into(rest_bank[:, n, e, :], m2y[t][:, block_cols(b)], False, True)
+            tag = "rest%d_%d" % (blocks[0], u)
+            tile = keep.tile([P, len(blocks), P, 2], F32, name=tag, tag=tag, align_bytes=64)
+            nc.scalar.copy(tile[:], rest_bank[:].rearrange("j b e p -> j b p e"))
+            for n, b in enumerate(blocks):
+                rest[b, u] = tile[:, n]
 
-        def gather_east(h, t, tag):
-            east_sum[h, t] = keep.tile([P, HALF], F32, name="east_sum%d_%d" % (h, t), tag=tag, align_bytes=64)
-            nc.vector.tensor_tensor(
-                east_sum[h, t][:], y[t][:].indirect(east_sb[:, list_cols(h)]), minus2y[t][:, half_cols(h)], ADD
-            )
-
-        def gather_west(h, t, tag):
-            lap[h, t] = keep.tile([P, HALF], F32, name="lap%d_%d" % (h, t), tag=tag, align_bytes=64)
-            nc.vector.tensor_tensor(lap[h, t][:], y[t][:].indirect(west_sb[:, list_cols(h)]), east_sum[h, t][:], ADD)
-
-        def turn(b, u):
-            lap_turned[b, u] = bank((2 * b + u) % 4, [P, 2, P], "lap_turned%d_%d" % (b, u))
-            for e in range(2):
-                nc.tensor.matmul(
-                    lap_turned[b, u][:, e, :],
-                    lap[b // 2, 2 * u + e][:, block_cols(b % 2)],
-                    ident[:],
-                    start=True,
-                    stop=True,
-                    is_transpose=True,
-                )
-
-        def new_z_turned(b, tag):
-            z_turned[b] = keep.tile([P, 2, P, 2], BF16, name="z_turned%d" % b, tag=tag, align_bytes=64)
+        def gather(dst, t, lists_sb, span, other):
+            nc.vector.tensor_tensor(dst, y[t][:].indirect(lists_sb[:, list_cols(span)]), other, ADD)
 
         def combine(b, u):
             nc.vector.scalar_tensor_tensor(
                 z_turned[b][:, u],
-                lap_turned[b, u][:].rearrange("j e p -> j p e"),
+                lap_turned[b][:, 2 * u : 2 * u + 2, :].rearrange("j e p -> j p e"),
                 c_col[:, b : b + 1],
-                rest[b, u][:],
+                rest[b, u],
                 MULT,
                 SUB,
             )
 
-        def turn_back(b):
+        def turn_back(b, index):
             pairs = z_turned[b][:].rearrange("j u p e -> j (u p e)").bitcast(F32)
-            back = bank(4 + b % 2, [P, 2, P], "back%d" % b)
+            back = bank(index, [P, 2, P], "back%d" % b)
             for u in range(2):
                 nc.tensor.transpose(back[:, u, :], pairs[:, block_cols(u)], ident[:])
             tag = "z_grouped%d" % b
@@ -212,11 +193,11 @@ def tile_picked_waveeq_none_po_kernel(
                 z_grouped[b][:].bitcast(F32).rearrange("p (j u) -> p j u", u=2), back[:].rearrange("p u j -> p j u")
             )
 
-        def second_product(b):
+        def second_product(b, index):
             z_codes = keep.tile([P, P], U32, name="z_codes%d" % b, align_bytes=64)
             z_scales = keep.tile([P, P], U8, name="z_scales%d" % b, align_bytes=64)
             nc.vector.quantize_mx(out=z_codes[:].bitcast(FP8X4), scales=z_scales[:], in_=z_grouped[b][:])
-            out_bank = bank(6 + b % 2, [P, PACK, P], "out_bank%d" % b)
+            out_bank = bank(index, [P, PACK, P], "out_bank%d" % b)
             for t in range(PACK):
                 nc.tensor.matmul_mx(
                     out=out_bank[:, t, :],
@@ -228,87 +209,95 @@ def tile_picked_waveeq_none_po_kernel(
                     stop=True,
                 )
             out_grouped[b] = keep.tile([P, P * PACK], BF16, name="out_grouped%d" % b, align_bytes=64)
-            nc.scalar.copy(
-                out_grouped[b][:].rearrange("p (j t) -> p j t", t=PACK), out_bank[:].rearrange("p t j -> p j t")
-            )
-            out_sb = keep.tile([P, PACK, P], F32, name="out_sb%d" % b)
-            if 0 < b < LAST:
-                nc.vector.tensor_copy(out_sb[:], out_bank[:])
+            rounded = out_grouped[b][:].rearrange("p (j t) -> p j t", t=PACK)
+            if b == LAST:
+                nc.vector.tensor_copy(rounded, out_bank[:].rearrange("p t j -> p j t"))
             else:
-                nc.scalar.copy(out_sb[:], out_bank[:])
+                nc.scalar.copy(rounded, out_bank[:].rearrange("p t j -> p j t"))
+            out_sb = keep.tile([P, PACK, P], F32, name="out_sb%d" % b)
+            nc.scalar.copy(out_sb[:], out_bank[:])
             queue = nc.scalar if b == LAST else nc.sync
             queue.dma_start(out_rows[:, :, block_cols(b)], out_sb[:])
 
         def hand_on(b):
-            cols = block_cols(b)
+            span = block_cols(b)
             nc.vector.quantize_mx(
-                out=out_words[:, cols].bitcast(FP8X4), scales=out_scales[:, cols], in_=out_grouped[b][:]
+                out=out_words[:, span].bitcast(FP8X4), scales=out_scales[:, span], in_=out_grouped[b][:]
             )
-            nc.sync.dma_start(out_word_rows[:, cols], out_words[:, cols].bitcast(I32))
+            nc.sync.dma_start(out_word_rows[:, span], out_words[:, span].bitcast(I32))
 
-        plane0 = [first_product(0, [0], 4), first_product(0, [1], 0)]
-        later_planes = {t: first_product(t, [0, 1], t) for t in range(1, PACK)}
+        span_a, span_b, span_c = cols(0, HALF), block_cols(2), block_cols(LAST)
+        parts = [(0, cols(0, HALF), 0), (0, cols(HALF, HALF), 1)] + [(t, cols(0, S), t + 1) for t in range(1, PACK)]
+        banks = [first_product(*part) for part in parts]
+        for (t, span, index), y_bank in zip(parts, banks):
+            take_y(t, span, y_bank)
+        make_rest([0, 1], 0, 5)
+        make_rest([2], 0, 6)
+        make_rest([0, 1], 1, 2)
+        make_rest([2], 1, 3)
 
-        w2_plane = keep.tile([P, PACK, P], U8, name="w2_plane", tag="xs_plane", align_bytes=64)
-        nc.gpsimd.memset(w2_plane[:].bitcast(I32), 0)
-        place_rows(w2_plane, w2s_dealt)
-
-        for product in plane0:
-            take_y(0, product)
-        take_y(1, later_planes[1])
-        take_y(2, later_planes[2])
-        for b in (0, 1):
-            make_rest(b, 0)
-        take_y(3, later_planes[3])
-        for b in (2, 3):
-            make_rest(b, 0)
-        for b in range(BLOCKS):
-            make_rest(b, 1)
-
+        east_a = [keep.tile([P, HALF], F32, name="east_a%d" % t) for t in range(PACK)]
+        east_b = [keep.tile([P, P], F32, name="east_b%d" % t) for t in range(PACK)]
+        lap_a = [keep.tile([P, HALF], F32, name="lap_a%d" % t) for t in range(PACK)]
         for t in range(PACK):
-            gather_east(0, t, "east_sum0_%d" % t)
-            gather_west(0, t, "lap0_%d" % t)
-            if t < LAST:
-                gather_east(1, t, "east_sum1_%d" % t)
-            if t == LAST - 1:
-                for b in (0, 1):
-                    turn(b, 0)
-                for b in (0, 1):
-                    new_z_turned(b, "z_turned%d" % b)
-                    combine(b, 0)
+            gather(east_a[t][:], t, east_sb, span_a, m2y[t][:, span_a])
+            gather(east_b[t][:], t, east_sb, span_b, m2y[t][:, span_b])
+            gather(lap_a[t][:], t, west_sb, span_a, east_a[t][:])
+        lap_b = keep.tile([P, PACK, P], F32, name="lap_b", tag="m2y%d" % LAST, align_bytes=64)
+        for t in range(PACK):
+            gather(lap_b[:, t, :], t, west_sb, span_b, east_b[t][:])
         for b in (0, 1):
-            turn(b, 1)
-        gather_east(1, LAST, "east_sum0_%d" % LAST)
-        for b in (0, 1):
-            combine(b, 1)
-            turn_back(b)
+            lap_turned[b] = bank(5 + b, [P, PACK, P], "lap_turned%d" % b)
+        for t in range(PACK):
+            for b in (0, 1):
+                turn_into(lap_turned[b][:, t, :], lap_a[t][:, block_cols(b)], True, True)
+        lap_turned[2] = bank(4, [P, PACK, P], "lap_turned2")
+        for t in range(PACK):
+            turn_into(lap_turned[2][:, t, :], lap_b[:, t, :], True, True)
 
-        gather_west(1, 0, "rest0_1")
-        gather_west(1, 1, "rest1_1")
-        for b in (2, 3):
-            turn(b, 0)
-        gather_west(1, 2, "z_turned1")
-        for b in (0, 1):
-            second_product(b)
-        gather_west(1, 3, "z_grouped0")
-        for b in (2, 3):
-            turn(b, 1)
-        new_z_turned(2, "east_sum1_2")
-        combine(2, 0)
-        new_z_turned(3, "east_sum0_%d" % LAST)
-        combine(3, 0)
-        for b in (2, 3):
-            combine(b, 1)
-            turn_back(b)
+        rest_last = keep.tile([P, PACK, P], F32, name="rest_last")
+        nc.vector.tensor_tensor(rest_last[:], prev_sb[:, :, span_c], m2y_last[:], ADD)
+
+        for b in range(TURNED):
+            z_turned[b] = keep.tile([P, 2, P, 2], BF16, name="z_turned%d" % b, align_bytes=64)
+            for u in range(2):
+                combine(b, u)
+            turn_back(b, b)
+
+        east_c0 = keep.tile([P, 2, P], F32, name="east_c0", tag="rest2_0", align_bytes=64)
+        for t in (0, 1):
+            gather(east_c0[:, t, :], t, east_sb, span_c, m2y_last[:, t, :])
+        second_product(0, 7)
+        east_c1 = keep.tile([P, 2, P], F32, name="east_c1", tag="z_grouped0", align_bytes=64)
+        for t in (2, 3):
+            gather(east_c1[:, t - 2, :], t, east_sb, span_c, m2y_last[:, t, :])
+        second_product(1, 3)
+        second_product(2, 5)
+        lap_c = keep.tile([P, PACK, P], F32, name="lap_c", tag="z_grouped2", align_bytes=64)
+        for t in range(PACK):
+            gather(lap_c[:, t, :], t, west_sb, span_c, (east_c0, east_c1)[t // 2][:, t % 2, :])
+        scaled = keep.tile([P, PACK, P], F32, name="scaled")
+        for u in range(2):
+            pair = slice(2 * u, 2 * u + 2)
+            nc.vector.tensor_tensor(
+                scaled[:, pair, :], lap_c[:, pair, :], c_last[:].unsqueeze(1).to_broadcast([P, 2, P]), MULT
+            )
+        z_grouped[LAST] = keep.tile([P, P * PACK], BF16, name="z_grouped%d" % LAST, align_bytes=64)
+        for u in range(2):
+            pair = slice(2 * u, 2 * u + 2)
+            nc.vector.tensor_tensor(
+                z_grouped[LAST][:].rearrange("p (j t) -> p j t", t=PACK)[:, :, pair],
+                scaled[:, pair, :].rearrange("p e j -> p j e"),
+                rest_last[:, pair, :].rearrange("p e j -> p j e"),
+                SUB,
+            )
         hand_on(0)
-        for b in (2, 3):
-            second_product(b)
+        second_product(LAST, 6)
         for b in range(1, BLOCKS):
             hand_on(b)
 
         for q in range(P // QUAD):
-            queue = nc.scalar if q == LAST else nc.sync
+            queue = nc.scalar if q % 2 else nc.sync
             queue.dma_start(
-                out_2[0, PACK * q : PACK * (q + 1), :].bitcast(I32),
-                out_scales[QUAD * q : QUAD * q + PACK, :].bitcast(I32),
+                out_2[0, cols(PACK * q, PACK), :].bitcast(I32), out_scales[cols(QUAD * q, PACK), :].bitcast(I32)
             )

@@ -119,14 +119,8 @@ def tile_picked_waveeq_none_po_kernel(
         for a in range(PACK):
             nc.sync.dma_start(w2_plane[a:P:QUAD].bitcast(I32), w2s_dealt[SPREAD * a : P : QUAD].bitcast(I32))
 
-        c_bank = bank(7, [P, P], "c_bank")
-        nc.tensor.transpose(c_bank[:], c_rows[:], ident[:])
-        c_col = keep.tile([P, BLOCKS], F32, name="c_col")
-        nc.scalar.copy(c_col[:], c_bank[:, 0:BLOCKS])
-
         y = [keep.tile([P, S], F32, name="y%d" % t) for t in range(PACK)]
-        m2y = [keep.tile([P, AB], F32, name="m2y%d" % t, tag="m2y%d" % t, align_bytes=64) for t in range(PACK)]
-        m2y_last = keep.tile([P, PACK, P], F32, name="m2y_last")
+        m2y = keep.tile([P, PACK, S], F32, name="m2y")
         out_words = keep.tile([P, S], U32, name="out_words", align_bytes=64)
         out_scales = keep.tile([P, S], U8, name="out_scales", align_bytes=64)
         out_rows = out_0.rearrange("(p t) j -> p t j", t=PACK)
@@ -148,26 +142,15 @@ def tile_picked_waveeq_none_po_kernel(
 
         def take_y(t, span, y_bank):
             nc.scalar.copy(y[t][:, span], y_bank[:])
-            width = min(span.stop, AB) - span.start
-            nc.scalar.activation(m2y[t][:, cols(span.start, width)], y_bank[:, 0:width], COPY, scale=-2.0)
-            if span.stop > AB:
-                nc.scalar.activation(m2y_last[:, t, :], y_bank[:, cols(width, P)], COPY, scale=-2.0)
+            nc.scalar.activation(m2y[:, t, span], y_bank[:], COPY, scale=-2.0)
 
         def turn_into(dst, src, start, stop):
             nc.tensor.matmul(dst, src, ident[:], start=start, stop=stop, is_transpose=True)
 
-        def make_rest(blocks, u, index):
-            rest_bank = bank(index, [P, len(blocks), 2, P], "rest_bank%d_%d" % (blocks[0], u))
-            for e in range(2):
-                t = 2 * u + e
-                for n, b in enumerate(blocks):
-                    turn_into(rest_bank[:, n, e, :], prev_sb[:, t, block_cols(b)], True, False)
-                    turn_into(rest_bank[:, n, e, :], m2y[t][:, block_cols(b)], False, True)
-            tag = "rest%d_%d" % (blocks[0], u)
-            tile = keep.tile([P, len(blocks), P, 2], F32, name=tag, tag=tag, align_bytes=64)
-            nc.scalar.copy(tile[:], rest_bank[:].rearrange("j b e p -> j b p e"))
-            for n, b in enumerate(blocks):
-                rest[b, u] = tile[:, n]
+        def take_rest(b):
+            tag = "rest%d" % b
+            rest[b] = keep.tile([P, 2, P, 2], F32, name=tag, tag=tag, align_bytes=64)
+            nc.scalar.copy(rest[b][:], rest_bank[b][:].rearrange("j (u e) p -> j u p e", e=2))
 
         def gather(dst, t, lists_sb, span, other):
             nc.vector.tensor_tensor(dst, y[t][:].indirect(lists_sb[:, list_cols(span)]), other, ADD)
@@ -175,9 +158,9 @@ def tile_picked_waveeq_none_po_kernel(
         def combine(b, u):
             nc.vector.scalar_tensor_tensor(
                 z_turned[b][:, u],
-                lap_turned[b][:, 2 * u : 2 * u + 2, :].rearrange("j e p -> j p e"),
+                lap_turned[b, u].rearrange("j e p -> j p e"),
                 c_col[:, b : b + 1],
-                rest[b, u],
+                rest[b][:, u],
                 MULT,
                 SUB,
             )
@@ -193,14 +176,15 @@ def tile_picked_waveeq_none_po_kernel(
                 z_grouped[b][:].bitcast(F32).rearrange("p (j u) -> p j u", u=2), back[:].rearrange("p u j -> p j u")
             )
 
-        def second_product(b, index):
+        def second_product(b, *indices):
             z_codes = keep.tile([P, P], U32, name="z_codes%d" % b, align_bytes=64)
             z_scales = keep.tile([P, P], U8, name="z_scales%d" % b, align_bytes=64)
             nc.vector.quantize_mx(out=z_codes[:].bitcast(FP8X4), scales=z_scales[:], in_=z_grouped[b][:])
-            out_bank = bank(index, [P, PACK, P], "out_bank%d" % b)
+            step = PACK // len(indices)
+            out_banks = [bank(index, [P, step, P], "out_bank%d_%d" % (b, index)) for index in indices]
             for t in range(PACK):
                 nc.tensor.matmul_mx(
-                    out=out_bank[:, t, :],
+                    out=out_banks[t // step][:, t % step, :],
                     lhsT=w2_codes[:, t, :].bitcast(FP8X4),
                     lhsT_scale=w2_plane[:, t, :],
                     rhs=z_codes[:].bitcast(FP8X4),
@@ -209,13 +193,19 @@ def tile_picked_waveeq_none_po_kernel(
                     stop=True,
                 )
             out_grouped[b] = keep.tile([P, P * PACK], BF16, name="out_grouped%d" % b, align_bytes=64)
-            rounded = out_grouped[b][:].rearrange("p (j t) -> p j t", t=PACK)
-            if b == LAST:
-                nc.vector.tensor_copy(rounded, out_bank[:].rearrange("p t j -> p j t"))
-            else:
-                nc.scalar.copy(rounded, out_bank[:].rearrange("p t j -> p j t"))
             out_sb = keep.tile([P, PACK, P], F32, name="out_sb%d" % b)
-            nc.scalar.copy(out_sb[:], out_bank[:])
+            if b < LAST:
+                nc.scalar.copy(
+                    out_grouped[b][:].rearrange("p (j t) -> p j t", t=PACK),
+                    out_banks[0][:].rearrange("p t j -> p j t"),
+                )
+            for n, out_bank in enumerate(out_banks):
+                nc.scalar.copy(out_sb[:, cols(step * n, step), :], out_bank[:])
+            if b == LAST:
+                nc.vector.tensor_copy(
+                    out_grouped[b][:].rearrange("p (g i t) -> p g t i", i=2, t=PACK),
+                    out_sb[:].rearrange("p t (g i) -> p g t i", i=2),
+                )
             queue = nc.scalar if b == LAST else nc.sync
             queue.dma_start(out_rows[:, :, block_cols(b)], out_sb[:])
 
@@ -231,48 +221,62 @@ def tile_picked_waveeq_none_po_kernel(
         banks = [first_product(*part) for part in parts]
         for (t, span, index), y_bank in zip(parts, banks):
             take_y(t, span, y_bank)
-        make_rest([0, 1], 0, 5)
-        make_rest([2], 0, 6)
-        make_rest([0, 1], 1, 2)
-        make_rest([2], 1, 3)
+        rest_bank = [bank(5 + b, [P, PACK, P], "rest_bank%d" % b) for b in range(TURNED)]
+        for b in range(TURNED):
+            for t in range(PACK):
+                turn_into(rest_bank[b][:, t, :], prev_sb[:, t, block_cols(b)], t == 0, False)
+        for t in range(PACK):
+            for b in range(TURNED):
+                turn_into(rest_bank[b][:, t, :], m2y[:, t, block_cols(b)], False, t == LAST)
+        c_bank = bank(0, [P, P], "c_bank")
+        nc.tensor.transpose(c_bank[:], c_rows[:], ident[:])
+        c_col = keep.tile([P, BLOCKS], F32, name="c_col")
+        nc.scalar.copy(c_col[:], c_bank[:, 0:BLOCKS])
 
-        east_a = [keep.tile([P, HALF], F32, name="east_a%d" % t) for t in range(PACK)]
+        for b in range(TURNED):
+            take_rest(b)
+
+        east_a = [keep.tile([P, HALF], F32, name="east_a%d" % t, tag="east_a%d" % t) for t in range(PACK)]
         east_b = [keep.tile([P, P], F32, name="east_b%d" % t) for t in range(PACK)]
         lap_a = [keep.tile([P, HALF], F32, name="lap_a%d" % t) for t in range(PACK)]
         for t in range(PACK):
-            gather(east_a[t][:], t, east_sb, span_a, m2y[t][:, span_a])
-            gather(east_b[t][:], t, east_sb, span_b, m2y[t][:, span_b])
+            gather(east_a[t][:], t, east_sb, span_a, m2y[:, t, span_a])
+            gather(east_b[t][:], t, east_sb, span_b, m2y[:, t, span_b])
             gather(lap_a[t][:], t, west_sb, span_a, east_a[t][:])
-        lap_b = keep.tile([P, PACK, P], F32, name="lap_b", tag="m2y%d" % LAST, align_bytes=64)
+        lap_b = keep.tile([P, PACK, P], F32, name="lap_b", tag="east_a%d" % (LAST - 1))
         for t in range(PACK):
             gather(lap_b[:, t, :], t, west_sb, span_b, east_b[t][:])
-        for b in (0, 1):
-            lap_turned[b] = bank(5 + b, [P, PACK, P], "lap_turned%d" % b)
-        for t in range(PACK):
+        for u in range(2):
+            pair_bank = bank(3 + u, [P, 2, 2, P], "lap_turned_a%d" % u)
+            for e in range(2):
+                for b in (0, 1):
+                    turn_into(pair_bank[:, b, e, :], lap_a[2 * u + e][:, block_cols(b)], True, True)
             for b in (0, 1):
-                turn_into(lap_turned[b][:, t, :], lap_a[t][:, block_cols(b)], True, True)
-        lap_turned[2] = bank(4, [P, PACK, P], "lap_turned2")
+                lap_turned[b, u] = pair_bank[:, b]
+        block_bank = bank(2, [P, 2, 2, P], "lap_turned_b")
         for t in range(PACK):
-            turn_into(lap_turned[2][:, t, :], lap_b[:, t, :], True, True)
+            turn_into(block_bank[:, t // 2, t % 2, :], lap_b[:, t, :], True, True)
+        for u in range(2):
+            lap_turned[2, u] = block_bank[:, u]
 
         rest_last = keep.tile([P, PACK, P], F32, name="rest_last")
-        nc.vector.tensor_tensor(rest_last[:], prev_sb[:, :, span_c], m2y_last[:], ADD)
+        nc.vector.tensor_tensor(rest_last[:], prev_sb[:, :, span_c], m2y[:, :, span_c], ADD)
 
         for b in range(TURNED):
             z_turned[b] = keep.tile([P, 2, P, 2], BF16, name="z_turned%d" % b, align_bytes=64)
             for u in range(2):
                 combine(b, u)
-            turn_back(b, b)
+            turn_back(b, (1, 0, 2)[b])
 
-        east_c0 = keep.tile([P, 2, P], F32, name="east_c0", tag="rest2_0", align_bytes=64)
+        east_c0 = keep.tile([P, 2, P], F32, name="east_c0", tag="rest1", align_bytes=64)
         for t in (0, 1):
-            gather(east_c0[:, t, :], t, east_sb, span_c, m2y_last[:, t, :])
-        second_product(0, 7)
+            gather(east_c0[:, t, :], t, east_sb, span_c, m2y[:, t, span_c])
+        second_product(0, 5)
         east_c1 = keep.tile([P, 2, P], F32, name="east_c1", tag="z_grouped0", align_bytes=64)
         for t in (2, 3):
-            gather(east_c1[:, t - 2, :], t, east_sb, span_c, m2y_last[:, t, :])
-        second_product(1, 3)
-        second_product(2, 5)
+            gather(east_c1[:, t - 2, :], t, east_sb, span_c, m2y[:, t, span_c])
+        second_product(1, 6)
+        second_product(2, 7)
         lap_c = keep.tile([P, PACK, P], F32, name="lap_c", tag="z_grouped2", align_bytes=64)
         for t in range(PACK):
             gather(lap_c[:, t, :], t, west_sb, span_c, (east_c0, east_c1)[t // 2][:, t % 2, :])
@@ -283,16 +287,14 @@ def tile_picked_waveeq_none_po_kernel(
                 scaled[:, pair, :], lap_c[:, pair, :], c_last[:].unsqueeze(1).to_broadcast([P, 2, P]), MULT
             )
         z_grouped[LAST] = keep.tile([P, P * PACK], BF16, name="z_grouped%d" % LAST, align_bytes=64)
-        for u in range(2):
-            pair = slice(2 * u, 2 * u + 2)
-            nc.vector.tensor_tensor(
-                z_grouped[LAST][:].rearrange("p (j t) -> p j t", t=PACK)[:, :, pair],
-                scaled[:, pair, :].rearrange("p e j -> p j e"),
-                rest_last[:, pair, :].rearrange("p e j -> p j e"),
-                SUB,
-            )
+        nc.vector.tensor_tensor(
+            z_grouped[LAST][:].rearrange("p (g i t) -> p g t i", i=2, t=PACK),
+            scaled[:].rearrange("p t (g i) -> p g t i", i=2),
+            rest_last[:].rearrange("p t (g i) -> p g t i", i=2),
+            SUB,
+        )
         hand_on(0)
-        second_product(LAST, 6)
+        second_product(LAST, 3, 4)
         for b in range(1, BLOCKS):
             hand_on(b)
 

@@ -26,6 +26,7 @@ ROWS = 16
 SPREAD = P // ROWS
 BLOCKS = S // P
 HALF = S // 2
+W1_ON_VECTOR = 80
 LAST = PACK - 1
 TURNED = 3
 AB = TURNED * P
@@ -62,7 +63,7 @@ def tile_picked_waveeq_none_po_kernel(
         nc.sync.dma_start(east_sb[:], east)
         nc.sync.dma_start(west_sb[:], west)
         nc.sync.dma_start(xs_window[0:P:SPREAD].bitcast(I32), x_scales[0].bitcast(I32))
-        w1_raw = keep.tile([P, PACK, H], F32, name="w1_raw", tag="w1_raw")
+        w1_raw = shared.tile([P, PACK, H], F32, name="w1_raw", offset=8192, align_bytes=64)
         nc.sync.dma_start(w1_raw[:], w1.rearrange("(p j) c -> p j c", j=PACK))
         x_window = shared.tile([P, T], I32, name="x_window", offset=0, align_bytes=64)
         nc.sync.dma_start(x_window[:], x_words[0].rearrange("p n t -> p (n t)").bitcast(I32))
@@ -73,28 +74,36 @@ def tile_picked_waveeq_none_po_kernel(
         nc.sync.dma_start(w2s_raw[:].bitcast(I32), w2s_rows.unsqueeze(1).to_broadcast([ROWS, SPREAD, N // 4]))
         ident = keep.tile([P, P], F32, name="ident")
         make_identity(nc, ident[:])
+        warm = keep.tile([P, 2], F32, name="warm")
+        nc.vector.memset(warm[:, 0:1], 0.0)
+        nc.scalar.copy(warm[:, 1:2], warm[:, 0:1])
         w2_plane = keep.tile([P, PACK, P], U8, name="w2_plane", align_bytes=64)
         nc.gpsimd.memset(w2_plane[:].bitcast(I32), 0)
 
         xs_plane = keep.tile([P, S], U8, name="xs_plane", align_bytes=64)
-        nc.vector.memset(xs_plane[:].bitcast(I32), 0)
         xs_picked = keep.tile([P, S], U8, name="xs_picked", align_bytes=64)
         nc.vector.tensor_copy(xs_picked[:], xs_window[:].indirect(offs_sb[:]))
-        for a in range(PACK):
+        nc.vector.tensor_copy(xs_plane[:].bitcast(I32), xs_picked[:].bitcast(I32))
+        for a in range(1, PACK):
             nc.scalar.dma_start(xs_plane[a:P:QUAD].bitcast(I32), xs_picked[SPREAD * a : P : QUAD].bitcast(I32))
 
         w1_grouped = keep.tile([P, PACK, P, PACK], BF16, name="w1_grouped", tag="w1_grouped", align_bytes=64)
-        nc.vector.tensor_copy(
-            w1_grouped[:].rearrange("p t m j -> p m t j"), w1_raw[:].rearrange("p j (m t) -> p m t j", t=PACK)
-        )
+        w1_dst = w1_grouped[:].rearrange("p t m j -> p m t j")
+        w1_src = w1_raw[:].rearrange("p j (m t) -> p m t j", t=PACK)
+        nc.vector.tensor_copy(w1_dst[:, 0:W1_ON_VECTOR], w1_src[:, 0:W1_ON_VECTOR])
+        nc.scalar.copy(w1_dst[:, W1_ON_VECTOR:P], w1_src[:, W1_ON_VECTOR:P])
         w1_codes = keep.tile([P, H], U32, name="w1_codes", align_bytes=64)
         w1_scales = keep.tile([P, H], U8, name="w1_scales", align_bytes=64)
         nc.vector.quantize_mx(
             out=w1_codes[:].bitcast(FP8X4), scales=w1_scales[:], in_=w1_grouped[:].rearrange("p t m j -> p (t m j)")
         )
 
-        prev_sb = keep.tile([P, PACK, S], F32, name="prev_sb", tag="w1_raw")
-        nc.sync.dma_start(prev_sb[:], prev.rearrange("(p t) j -> p t j", t=PACK))
+        prev_rows = prev.rearrange("(p t) j -> p t j", t=PACK)
+        prev_half = []
+        for h in range(2):
+            tile = shared.tile([P, PACK, HALF], F32, name="prev%d" % h, offset=8192 + 4096 * h, align_bytes=64)
+            nc.sync.dma_start(tile[:], prev_rows[:, :, cols(HALF * h, HALF)])
+            prev_half.append(tile)
 
         x_picked = keep.tile([P, S], U32, name="x_picked", tag="w1_grouped", align_bytes=64)
         for h in range(2):
@@ -224,7 +233,7 @@ def tile_picked_waveeq_none_po_kernel(
         rest_bank = [bank(5 + b, [P, PACK, P], "rest_bank%d" % b) for b in range(TURNED)]
         for b in range(TURNED):
             for t in range(PACK):
-                turn_into(rest_bank[b][:, t, :], prev_sb[:, t, block_cols(b)], t == 0, False)
+                turn_into(rest_bank[b][:, t, :], prev_half[b // 2][:, t, block_cols(b % 2)], t == 0, False)
         for t in range(PACK):
             for b in range(TURNED):
                 turn_into(rest_bank[b][:, t, :], m2y[:, t, block_cols(b)], False, t == LAST)
@@ -259,9 +268,6 @@ def tile_picked_waveeq_none_po_kernel(
         for u in range(2):
             lap_turned[2, u] = block_bank[:, u]
 
-        rest_last = keep.tile([P, PACK, P], F32, name="rest_last")
-        nc.vector.tensor_tensor(rest_last[:], prev_sb[:, :, span_c], m2y[:, :, span_c], ADD)
-
         for b in range(TURNED):
             z_turned[b] = keep.tile([P, 2, P, 2], BF16, name="z_turned%d" % b, align_bytes=64)
             for u in range(2):
@@ -276,6 +282,9 @@ def tile_picked_waveeq_none_po_kernel(
         for t in (2, 3):
             gather(east_c1[:, t - 2, :], t, east_sb, span_c, m2y[:, t, span_c])
         second_product(1, 6)
+        rest_last = keep.tile([P, PACK, P], F32, name="rest_last", tag="rest2", align_bytes=64)
+        nc.vector.tensor_tensor(rest_last[:], prev_half[1][:, :, block_cols(1)], m2y[:, :, span_c], ADD)
+
         second_product(2, 7)
         lap_c = keep.tile([P, PACK, P], F32, name="lap_c", tag="z_grouped2", align_bytes=64)
         for t in range(PACK):

@@ -27,6 +27,7 @@ SPREAD = P // ROWS
 BLOCKS = S // P
 HALF = S // 2
 W1_ON_VECTOR = 80
+ROUNDED_ON_SCALAR = 2
 LAST = PACK - 1
 TURNED = 3
 AB = TURNED * P
@@ -134,7 +135,7 @@ def tile_picked_waveeq_none_po_kernel(
         out_scales = keep.tile([P, S], U8, name="out_scales", align_bytes=64)
         out_rows = out_0.rearrange("(p t) j -> p t j", t=PACK)
         out_word_rows = out_1[0].rearrange("p n t -> p (n t)").bitcast(I32)
-        rest, lap_turned, z_turned, z_grouped, out_grouped = {}, {}, {}, {}, {}
+        rest, lap_turned, z_turned, z_grouped, out_grouped, out_sb = {}, {}, {}, {}, {}, {}
 
         def first_product(t, span, index):
             y_bank = bank(index, [P, span.stop - span.start], "y_bank%d_%d" % (t, span.start))
@@ -202,24 +203,24 @@ def tile_picked_waveeq_none_po_kernel(
                     stop=True,
                 )
             out_grouped[b] = keep.tile([P, P * PACK], BF16, name="out_grouped%d" % b, align_bytes=64)
-            out_sb = keep.tile([P, PACK, P], F32, name="out_sb%d" % b)
-            if b < LAST:
+            out_sb[b] = keep.tile([P, PACK, P], F32, name="out_sb%d" % b)
+            if b < ROUNDED_ON_SCALAR:
                 nc.scalar.copy(
                     out_grouped[b][:].rearrange("p (j t) -> p j t", t=PACK),
                     out_banks[0][:].rearrange("p t j -> p j t"),
                 )
             for n, out_bank in enumerate(out_banks):
-                nc.scalar.copy(out_sb[:, cols(step * n, step), :], out_bank[:])
-            if b == LAST:
-                nc.vector.tensor_copy(
-                    out_grouped[b][:].rearrange("p (g i t) -> p g t i", i=2, t=PACK),
-                    out_sb[:].rearrange("p t (g i) -> p g t i", i=2),
-                )
+                nc.scalar.copy(out_sb[b][:, cols(step * n, step), :], out_bank[:])
             queue = nc.scalar if b == LAST else nc.sync
-            queue.dma_start(out_rows[:, :, block_cols(b)], out_sb[:])
+            queue.dma_start(out_rows[:, :, block_cols(b)], out_sb[b][:])
 
         def hand_on(b):
             span = block_cols(b)
+            if b >= ROUNDED_ON_SCALAR:
+                nc.vector.tensor_copy(
+                    out_grouped[b][:].rearrange("p (g i t) -> p g t i", i=2, t=PACK),
+                    out_sb[b][:].rearrange("p t (g i) -> p g t i", i=2),
+                )
             nc.vector.quantize_mx(
                 out=out_words[:, span].bitcast(FP8X4), scales=out_scales[:, span], in_=out_grouped[b][:]
             )
@@ -245,65 +246,60 @@ def tile_picked_waveeq_none_po_kernel(
         for b in range(TURNED):
             take_rest(b)
 
+        span_bc = cols(HALF, HALF)
         east_a = [keep.tile([P, HALF], F32, name="east_a%d" % t, tag="east_a%d" % t) for t in range(PACK)]
-        east_b = [keep.tile([P, P], F32, name="east_b%d" % t) for t in range(PACK)]
-        lap_a = [keep.tile([P, HALF], F32, name="lap_a%d" % t) for t in range(PACK)]
+        east_bc = [keep.tile([P, HALF], F32, name="east_bc%d" % t) for t in range(PACK)]
+        lap_ab = [keep.tile([P, TURNED * P], F32, name="lap_ab%d" % t) for t in range(PACK)]
         for t in range(PACK):
             gather(east_a[t][:], t, east_sb, span_a, m2y[:, t, span_a])
-            gather(east_b[t][:], t, east_sb, span_b, m2y[:, t, span_b])
-            gather(lap_a[t][:], t, west_sb, span_a, east_a[t][:])
-        lap_b = keep.tile([P, PACK, P], F32, name="lap_b", tag="east_a%d" % (LAST - 1))
-        for t in range(PACK):
-            gather(lap_b[:, t, :], t, west_sb, span_b, east_b[t][:])
+            gather(east_bc[t][:], t, east_sb, span_bc, m2y[:, t, span_bc])
+            gather(lap_ab[t][:, span_a], t, west_sb, span_a, east_a[t][:])
+            gather(lap_ab[t][:, span_b], t, west_sb, span_b, east_bc[t][:, block_cols(0)])
         for u in range(2):
-            pair_bank = bank(3 + u, [P, 2, 2, P], "lap_turned_a%d" % u)
-            for e in range(2):
-                for b in (0, 1):
-                    turn_into(pair_bank[:, b, e, :], lap_a[2 * u + e][:, block_cols(b)], True, True)
-            for b in (0, 1):
-                lap_turned[b, u] = pair_bank[:, b]
-        block_bank = bank(2, [P, 2, 2, P], "lap_turned_b")
-        for t in range(PACK):
-            turn_into(block_bank[:, t // 2, t % 2, :], lap_b[:, t, :], True, True)
-        for u in range(2):
-            lap_turned[2, u] = block_bank[:, u]
+            for blocks, index in (((0, 1), 3 + u), ((2,), (2, 5)[u])):
+                pair_bank = bank(index, [P, len(blocks), 2, P], "lap_turned%d_%d" % (blocks[0], u))
+                for e in range(2):
+                    for n, b in enumerate(blocks):
+                        turn_into(pair_bank[:, n, e, :], lap_ab[2 * u + e][:, block_cols(b)], True, True)
+                for n, b in enumerate(blocks):
+                    lap_turned[b, u] = pair_bank[:, n]
 
         for b in range(TURNED):
             z_turned[b] = keep.tile([P, 2, P, 2], BF16, name="z_turned%d" % b, align_bytes=64)
-            for u in range(2):
-                combine(b, u)
-            turn_back(b, (1, 0, 2)[b])
+            combine(b, 0)
+        for b in range(TURNED):
+            combine(b, 1)
+            turn_back(b, (1, 0, 6)[b])
 
-        east_c0 = keep.tile([P, 2, P], F32, name="east_c0", tag="rest1", align_bytes=64)
+        last_terms = keep.tile([P, PACK + 1, P], F32, name="last_terms", tag="east_a%d" % LAST)
+        rest_last, east_scaled = last_terms[:, 0:PACK, :], last_terms[:, PACK, :]
+        nc.gpsimd.tensor_tensor(rest_last, prev_half[1][:, :, block_cols(1)], m2y[:, :, span_c], ADD)
+        nc.gpsimd.tensor_tensor(east_scaled, east_bc[LAST][:, block_cols(1)], c_last[:], MULT)
+        nc.gpsimd.tensor_tensor(last_terms[:, LAST, :], last_terms[:, LAST, :], east_scaled, SUB)
+
+        lap_c = keep.tile([P, 2, P], F32, name="lap_c", tag="rest1", align_bytes=64)
         for t in (0, 1):
-            gather(east_c0[:, t, :], t, east_sb, span_c, m2y[:, t, span_c])
-        second_product(0, 5)
-        east_c1 = keep.tile([P, 2, P], F32, name="east_c1", tag="z_grouped0", align_bytes=64)
-        for t in (2, 3):
-            gather(east_c1[:, t - 2, :], t, east_sb, span_c, m2y[:, t, span_c])
-        second_product(1, 6)
-        rest_last = keep.tile([P, PACK, P], F32, name="rest_last", tag="rest2", align_bytes=64)
-        nc.vector.tensor_tensor(rest_last[:], prev_half[1][:, :, block_cols(1)], m2y[:, :, span_c], ADD)
-
-        second_product(2, 7)
-        lap_c = keep.tile([P, PACK, P], F32, name="lap_c", tag="z_grouped2", align_bytes=64)
-        for t in range(PACK):
-            gather(lap_c[:, t, :], t, west_sb, span_c, (east_c0, east_c1)[t // 2][:, t % 2, :])
-        scaled = keep.tile([P, PACK, P], F32, name="scaled")
-        for u in range(2):
-            pair = slice(2 * u, 2 * u + 2)
-            nc.vector.tensor_tensor(
-                scaled[:, pair, :], lap_c[:, pair, :], c_last[:].unsqueeze(1).to_broadcast([P, 2, P]), MULT
-            )
+            gather(lap_c[:, t, :], t, west_sb, span_c, east_bc[t][:, block_cols(1)])
+        second_product(0, 7)
+        second_product(1, 2)
+        lap_c2 = keep.tile([P, P], F32, name="lap_c2", tag="z_grouped1", align_bytes=64)
+        gather(lap_c2[:], 2, west_sb, span_c, east_bc[2][:, block_cols(1)])
+        second_product(2, 3)
+        scaled = keep.tile([P, PACK, P], F32, name="scaled", tag="z_grouped2", align_bytes=64)
+        nc.vector.tensor_tensor(scaled[:, 0:2, :], lap_c[:], c_last[:].unsqueeze(1).to_broadcast([P, 2, P]), MULT)
+        nc.vector.tensor_tensor(scaled[:, 2, :], lap_c2[:], c_last[:], MULT)
+        nc.vector.tensor_tensor(
+            scaled[:, LAST, :], y[LAST][:].indirect(west_sb[:, list_cols(span_c)]), c_last[:], MULT
+        )
+        hand_on(0)
         z_grouped[LAST] = keep.tile([P, P * PACK], BF16, name="z_grouped%d" % LAST, align_bytes=64)
         nc.vector.tensor_tensor(
             z_grouped[LAST][:].rearrange("p (g i t) -> p g t i", i=2, t=PACK),
             scaled[:].rearrange("p t (g i) -> p g t i", i=2),
-            rest_last[:].rearrange("p t (g i) -> p g t i", i=2),
+            rest_last.rearrange("p t (g i) -> p g t i", i=2),
             SUB,
         )
-        hand_on(0)
-        second_product(LAST, 3, 4)
+        second_product(LAST, 4, 5)
         for b in range(1, BLOCKS):
             hand_on(b)
 

@@ -27,7 +27,7 @@ SPREAD = P // ROWS
 BLOCKS = S // P
 HALF = S // 2
 W1_ON_VECTOR = 80
-ROUNDED_ON_SCALAR = 2
+ROUNDED_ON_SCALAR = 1
 LAST = PACK - 1
 TURNED = 3
 AB = TURNED * P
@@ -71,8 +71,8 @@ def tile_picked_waveeq_none_po_kernel(
         w2_raw = keep.tile([P, N], I32, name="w2_raw", align_bytes=64)
         nc.sync.dma_start(w2_raw[:], w2_words[0].rearrange("p n t -> p (n t)").bitcast(I32))
         w2s_raw = keep.tile([P, N], U8, name="w2s_raw", align_bytes=64)
-        w2s_rows = w2_scales[0].bitcast(I32)
-        nc.sync.dma_start(w2s_raw[:].bitcast(I32), w2s_rows.unsqueeze(1).to_broadcast([ROWS, SPREAD, N // 4]))
+        nc.gpsimd.memset(w2s_raw[:].bitcast(I32), 0)
+        nc.sync.dma_start(w2s_raw[0:P:SPREAD].bitcast(I32), w2_scales[0].bitcast(I32))
         ident = keep.tile([P, P], F32, name="ident")
         make_identity(nc, ident[:])
         warm = keep.tile([P, 2], F32, name="warm")
@@ -224,7 +224,9 @@ def tile_picked_waveeq_none_po_kernel(
             nc.vector.quantize_mx(
                 out=out_words[:, span].bitcast(FP8X4), scales=out_scales[:, span], in_=out_grouped[b][:]
             )
-            nc.sync.dma_start(out_word_rows[:, span], out_words[:, span].bitcast(I32))
+            if b >= LAST - 1:
+                stored = span if b == LAST else cols(0, AB)
+                nc.sync.dma_start(out_word_rows[:, stored], out_words[:, stored].bitcast(I32))
 
         span_a, span_b, span_c = cols(0, HALF), block_cols(2), block_cols(LAST)
         parts = [(0, cols(0, HALF), 0), (0, cols(HALF, HALF), 1)] + [(t, cols(0, S), t + 1) for t in range(1, PACK)]
@@ -277,17 +279,16 @@ def tile_picked_waveeq_none_po_kernel(
         nc.gpsimd.tensor_tensor(east_scaled, east_bc[LAST][:, block_cols(1)], c_last[:], MULT)
         nc.gpsimd.tensor_tensor(last_terms[:, LAST, :], last_terms[:, LAST, :], east_scaled, SUB)
 
-        lap_c = keep.tile([P, 2, P], F32, name="lap_c", tag="rest1", align_bytes=64)
-        for t in (0, 1):
+        lap_c = keep.tile([P, LAST, P], F32, name="lap_c", tag="rest1", align_bytes=64)
+        for t in range(LAST):
             gather(lap_c[:, t, :], t, west_sb, span_c, east_bc[t][:, block_cols(1)])
         second_product(0, 7)
         second_product(1, 2)
-        lap_c2 = keep.tile([P, P], F32, name="lap_c2", tag="z_grouped1", align_bytes=64)
-        gather(lap_c2[:], 2, west_sb, span_c, east_bc[2][:, block_cols(1)])
+        scaled = keep.tile([P, PACK, P], F32, name="scaled", tag="z_grouped1", align_bytes=64)
+        nc.vector.tensor_tensor(
+            scaled[:, 0:LAST, :], lap_c[:], c_last[:].unsqueeze(1).to_broadcast([P, LAST, P]), MULT
+        )
         second_product(2, 3)
-        scaled = keep.tile([P, PACK, P], F32, name="scaled", tag="z_grouped2", align_bytes=64)
-        nc.vector.tensor_tensor(scaled[:, 0:2, :], lap_c[:], c_last[:].unsqueeze(1).to_broadcast([P, 2, P]), MULT)
-        nc.vector.tensor_tensor(scaled[:, 2, :], lap_c2[:], c_last[:], MULT)
         nc.vector.tensor_tensor(
             scaled[:, LAST, :], y[LAST][:].indirect(west_sb[:, list_cols(span_c)]), c_last[:], MULT
         )

@@ -27,7 +27,6 @@ SPREAD = P // ROWS
 BLOCKS = S // P
 HALF = S // 2
 W1_ON_VECTOR = 80
-ROUNDED_ON_SCALAR = 1
 LAST = PACK - 1
 TURNED = 3
 AB = TURNED * P
@@ -135,7 +134,7 @@ def tile_picked_waveeq_none_po_kernel(
         out_scales = keep.tile([P, S], U8, name="out_scales", align_bytes=64)
         out_rows = out_0.rearrange("(p t) j -> p t j", t=PACK)
         out_word_rows = out_1[0].rearrange("p n t -> p (n t)").bitcast(I32)
-        rest, lap_turned, z_turned, z_grouped, out_grouped, out_sb = {}, {}, {}, {}, {}, {}
+        rest, lap_turned, z_turned, z_grouped, out_sb = {}, {}, {}, {}, {}
 
         def first_product(t, span, index):
             y_bank = bank(index, [P, span.stop - span.start], "y_bank%d_%d" % (t, span.start))
@@ -202,13 +201,7 @@ def tile_picked_waveeq_none_po_kernel(
                     start=True,
                     stop=True,
                 )
-            out_grouped[b] = keep.tile([P, P * PACK], BF16, name="out_grouped%d" % b, align_bytes=64)
             out_sb[b] = keep.tile([P, PACK, P], F32, name="out_sb%d" % b)
-            if b < ROUNDED_ON_SCALAR:
-                nc.scalar.copy(
-                    out_grouped[b][:].rearrange("p (j t) -> p j t", t=PACK),
-                    out_banks[0][:].rearrange("p t j -> p j t"),
-                )
             for n, out_bank in enumerate(out_banks):
                 nc.scalar.copy(out_sb[b][:, cols(step * n, step), :], out_bank[:])
             queue = nc.scalar if b == LAST else nc.sync
@@ -216,13 +209,12 @@ def tile_picked_waveeq_none_po_kernel(
 
         def hand_on(b):
             span = block_cols(b)
-            if b >= ROUNDED_ON_SCALAR:
-                nc.vector.tensor_copy(
-                    out_grouped[b][:].rearrange("p (g i t) -> p g t i", i=2, t=PACK),
-                    out_sb[b][:].rearrange("p t (g i) -> p g t i", i=2),
-                )
+            nc.vector.tensor_copy(
+                out_grouped[:, b, :].rearrange("p (g i t) -> p g t i", i=2, t=PACK),
+                out_sb[b][:].rearrange("p t (g i) -> p g t i", i=2),
+            )
             nc.vector.quantize_mx(
-                out=out_words[:, span].bitcast(FP8X4), scales=out_scales[:, span], in_=out_grouped[b][:]
+                out=out_words[:, span].bitcast(FP8X4), scales=out_scales[:, span], in_=out_grouped[:, b, :]
             )
             if b >= LAST - 1:
                 stored = span if b == LAST else cols(0, AB)
@@ -249,7 +241,7 @@ def tile_picked_waveeq_none_po_kernel(
             take_rest(b)
 
         span_bc = cols(HALF, HALF)
-        east_a = [keep.tile([P, HALF], F32, name="east_a%d" % t, tag="east_a%d" % t) for t in range(PACK)]
+        east_a = [keep.tile([P, HALF], F32, name="east_a%d" % t, tag="east_a%d" % t, align_bytes=64) for t in range(PACK)]
         east_bc = [keep.tile([P, HALF], F32, name="east_bc%d" % t) for t in range(PACK)]
         lap_ab = [keep.tile([P, TURNED * P], F32, name="lap_ab%d" % t) for t in range(PACK)]
         for t in range(PACK):
@@ -258,7 +250,7 @@ def tile_picked_waveeq_none_po_kernel(
             gather(lap_ab[t][:, span_a], t, west_sb, span_a, east_a[t][:])
             gather(lap_ab[t][:, span_b], t, west_sb, span_b, east_bc[t][:, block_cols(0)])
         for u in range(2):
-            for blocks, index in (((0, 1), 3 + u), ((2,), (2, 5)[u])):
+            for blocks, index in (((0, 1), 4 + 2 * u), ((2,), 5 + 2 * u)):
                 pair_bank = bank(index, [P, len(blocks), 2, P], "lap_turned%d_%d" % (blocks[0], u))
                 for e in range(2):
                     for n, b in enumerate(blocks):
@@ -271,9 +263,9 @@ def tile_picked_waveeq_none_po_kernel(
             combine(b, 0)
         for b in range(TURNED):
             combine(b, 1)
-            turn_back(b, (1, 0, 6)[b])
+            turn_back(b, (1, 0, 7)[b])
 
-        last_terms = keep.tile([P, PACK + 1, P], F32, name="last_terms", tag="east_a%d" % LAST)
+        last_terms = keep.tile([P, PACK + 1, P], F32, name="last_terms", tag="east_a%d" % LAST, align_bytes=64)
         rest_last, east_scaled = last_terms[:, 0:PACK, :], last_terms[:, PACK, :]
         nc.gpsimd.tensor_tensor(rest_last, prev_half[1][:, :, block_cols(1)], m2y[:, :, span_c], ADD)
         nc.gpsimd.tensor_tensor(east_scaled, east_bc[LAST][:, block_cols(1)], c_last[:], MULT)
@@ -282,17 +274,16 @@ def tile_picked_waveeq_none_po_kernel(
         lap_c = keep.tile([P, LAST, P], F32, name="lap_c", tag="rest1", align_bytes=64)
         for t in range(LAST):
             gather(lap_c[:, t, :], t, west_sb, span_c, east_bc[t][:, block_cols(1)])
-        second_product(0, 7)
-        second_product(1, 2)
+        second_product(0, 2)
+        second_product(1, 3)
         scaled = keep.tile([P, PACK, P], F32, name="scaled", tag="z_grouped1", align_bytes=64)
         nc.vector.tensor_tensor(
             scaled[:, 0:LAST, :], lap_c[:], c_last[:].unsqueeze(1).to_broadcast([P, LAST, P]), MULT
         )
-        second_product(2, 3)
+        second_product(2, 4)
         nc.vector.tensor_tensor(
             scaled[:, LAST, :], y[LAST][:].indirect(west_sb[:, list_cols(span_c)]), c_last[:], MULT
         )
-        hand_on(0)
         z_grouped[LAST] = keep.tile([P, P * PACK], BF16, name="z_grouped%d" % LAST, align_bytes=64)
         nc.vector.tensor_tensor(
             z_grouped[LAST][:].rearrange("p (g i t) -> p g t i", i=2, t=PACK),
@@ -300,8 +291,9 @@ def tile_picked_waveeq_none_po_kernel(
             rest_last.rearrange("p t (g i) -> p g t i", i=2),
             SUB,
         )
-        second_product(LAST, 4, 5)
-        for b in range(1, BLOCKS):
+        second_product(LAST, 5, 6)
+        out_grouped = keep.tile([P, BLOCKS, P * PACK], BF16, name="out_grouped", tag="east_a%d" % LAST, align_bytes=64)
+        for b in range(BLOCKS):
             hand_on(b)
 
         for q in range(P // QUAD):

@@ -265,30 +265,22 @@ def tile_picked_waveeq_none_po_kernel(
             combine(b, 1)
             turn_back(b, (1, 0, 7)[b])
 
-        last_terms = keep.tile([P, PACK + 1, P], F32, name="last_terms", tag="east_a%d" % LAST, align_bytes=64)
-        rest_last, east_scaled = last_terms[:, 0:PACK, :], last_terms[:, PACK, :]
-        nc.gpsimd.tensor_tensor(rest_last, prev_half[1][:, :, block_cols(1)], m2y[:, :, span_c], ADD)
-        nc.gpsimd.tensor_tensor(east_scaled, east_bc[LAST][:, block_cols(1)], c_last[:], MULT)
-        nc.gpsimd.tensor_tensor(last_terms[:, LAST, :], last_terms[:, LAST, :], east_scaled, SUB)
+        rest_last = keep.tile([P, PACK, P], F32, name="rest_last", tag="east_a%d" % LAST, align_bytes=64)
+        nc.gpsimd.tensor_tensor(rest_last[:], prev_half[1][:, :, block_cols(1)], m2y[:, :, span_c], ADD)
 
-        lap_c = keep.tile([P, LAST, P], F32, name="lap_c", tag="rest1", align_bytes=64)
-        for t in range(LAST):
+        lap_c = keep.tile([P, PACK, P], F32, name="lap_c", tag="rest1", align_bytes=64)
+        for t in range(PACK):
             gather(lap_c[:, t, :], t, west_sb, span_c, east_bc[t][:, block_cols(1)])
         second_product(0, 2)
         second_product(1, 3)
-        scaled = keep.tile([P, PACK, P], F32, name="scaled", tag="z_grouped1", align_bytes=64)
-        nc.vector.tensor_tensor(
-            scaled[:, 0:LAST, :], lap_c[:], c_last[:].unsqueeze(1).to_broadcast([P, LAST, P]), MULT
-        )
+        scaled = keep.tile([P, PACK, P], F32, name="scaled", tag="z_grouped0", align_bytes=64)
+        nc.vector.tensor_tensor(scaled[:], lap_c[:], c_last[:].unsqueeze(1).to_broadcast([P, PACK, P]), MULT)
         second_product(2, 4)
-        nc.vector.tensor_tensor(
-            scaled[:, LAST, :], y[LAST][:].indirect(west_sb[:, list_cols(span_c)]), c_last[:], MULT
-        )
         z_grouped[LAST] = keep.tile([P, P * PACK], BF16, name="z_grouped%d" % LAST, align_bytes=64)
         nc.vector.tensor_tensor(
             z_grouped[LAST][:].rearrange("p (g i t) -> p g t i", i=2, t=PACK),
             scaled[:].rearrange("p t (g i) -> p g t i", i=2),
-            rest_last.rearrange("p t (g i) -> p g t i", i=2),
+            rest_last[:].rearrange("p t (g i) -> p g t i", i=2),
             SUB,
         )
         second_product(LAST, 5, 6)

@@ -156,10 +156,12 @@ def tile_picked_waveeq_none_po_kernel(
         def turn_into(dst, src, start, stop):
             nc.tensor.matmul(dst, src, ident[:], start=start, stop=stop, is_transpose=True)
 
-        def take_rest(b):
-            tag = "rest%d" % b
-            rest[b] = keep.tile([P, 2, P, 2], F32, name=tag, tag=tag, align_bytes=64)
-            nc.scalar.copy(rest[b][:], rest_bank[b][:].rearrange("j (u e) p -> j u p e", e=2))
+        def take_rest(b, pairs):
+            tag = "rest%d_%d" % (b, pairs.start)
+            tile = keep.tile([P, pairs.stop - pairs.start, P, 2], F32, name=tag, tag=tag, align_bytes=64)
+            nc.scalar.copy(tile[:], rest_bank[b][:].rearrange("j (u e) p -> j u p e", e=2)[:, pairs])
+            for u in range(pairs.start, pairs.stop):
+                rest[b, u] = tile[:, u - pairs.start]
 
         def gather(dst, t, lists_sb, span, other):
             nc.vector.tensor_tensor(dst, y[t][:].indirect(lists_sb[:, list_cols(span)]), other, ADD)
@@ -169,7 +171,7 @@ def tile_picked_waveeq_none_po_kernel(
                 z_turned[b][:, u],
                 lap_turned[b, u].rearrange("j e p -> j p e"),
                 c_col[:, b : b + 1],
-                rest[b][:, u],
+                rest[b, u],
                 MULT,
                 SUB,
             )
@@ -216,8 +218,8 @@ def tile_picked_waveeq_none_po_kernel(
             nc.vector.quantize_mx(
                 out=out_words[:, span].bitcast(FP8X4), scales=out_scales[:, span], in_=out_grouped[:, b, :]
             )
-            if b >= LAST - 1:
-                stored = span if b == LAST else cols(0, AB)
+            if b % 2:
+                stored = cols(P * (b - 1), HALF)
                 nc.sync.dma_start(out_word_rows[:, stored], out_words[:, stored].bitcast(I32))
 
         span_a, span_b, span_c = cols(0, HALF), block_cols(2), block_cols(LAST)
@@ -237,8 +239,10 @@ def tile_picked_waveeq_none_po_kernel(
         c_col = keep.tile([P, BLOCKS], F32, name="c_col")
         nc.scalar.copy(c_col[:], c_bank[:, 0:BLOCKS])
 
-        for b in range(TURNED):
-            take_rest(b)
+        for b in (0, 1):
+            take_rest(b, cols(0, 2))
+        for u in range(2):
+            take_rest(2, cols(u, 1))
 
         span_bc = cols(HALF, HALF)
         east_a = [keep.tile([P, HALF], F32, name="east_a%d" % t, tag="east_a%d" % t, align_bytes=64) for t in range(PACK)]
@@ -260,19 +264,23 @@ def tile_picked_waveeq_none_po_kernel(
 
         for b in range(TURNED):
             z_turned[b] = keep.tile([P, 2, P, 2], BF16, name="z_turned%d" % b, align_bytes=64)
+        for b in (0, 1):
             combine(b, 0)
-        for b in range(TURNED):
+        for b in (0, 1):
             combine(b, 1)
-            turn_back(b, (1, 0, 7)[b])
+            turn_back(b, 1 - b)
+        for u in range(2):
+            combine(2, u)
+        turn_back(2, 7)
 
         rest_last = keep.tile([P, PACK, P], F32, name="rest_last", tag="east_a%d" % LAST, align_bytes=64)
         nc.gpsimd.tensor_tensor(rest_last[:], prev_half[1][:, :, block_cols(1)], m2y[:, :, span_c], ADD)
 
-        lap_c = keep.tile([P, PACK, P], F32, name="lap_c", tag="rest1", align_bytes=64)
-        for t in range(PACK):
-            gather(lap_c[:, t, :], t, west_sb, span_c, east_bc[t][:, block_cols(1)])
         second_product(0, 2)
         second_product(1, 3)
+        lap_c = keep.tile([P, PACK, P], F32, name="lap_c", tag="rest2_0", align_bytes=64)
+        for t in range(PACK):
+            gather(lap_c[:, t, :], t, west_sb, span_c, east_bc[t][:, block_cols(1)])
         scaled = keep.tile([P, PACK, P], F32, name="scaled", tag="z_grouped0", align_bytes=64)
         nc.vector.tensor_tensor(scaled[:], lap_c[:], c_last[:].unsqueeze(1).to_broadcast([P, PACK, P]), MULT)
         second_product(2, 4)

@@ -59,19 +59,19 @@ def tile_picked_waveeq_none_po_kernel(
         west_sb = lists.tile([P, S // GROUP], U16, name="west_sb")
         xs_window = keep.tile([P, T], U8, name="xs_window", tag="xs_window", align_bytes=64)
         nc.gpsimd.memset(xs_window[:].bitcast(I32), 0)
+        w1_raw = shared.tile([P, PACK, H], F32, name="w1_raw", offset=8192, align_bytes=64)
+        w1_rows = w1.rearrange("(p j) c -> p j c", j=PACK)
+        nc.sync.dma_start(w1_raw[:, 0, :], w1_rows[:, 0, :])
         nc.sync.dma_start(offs_sb[:], offs)
         nc.sync.dma_start(east_sb[:], east)
-        nc.sync.dma_start(west_sb[:], west)
         nc.sync.dma_start(xs_window[0:P:SPREAD].bitcast(I32), x_scales[0].bitcast(I32))
-        w1_raw = shared.tile([P, PACK, H], F32, name="w1_raw", offset=8192, align_bytes=64)
-        nc.sync.dma_start(w1_raw[:], w1.rearrange("(p j) c -> p j c", j=PACK))
+        nc.sync.dma_start(w1_raw[:, 1:PACK, :], w1_rows[:, 1:PACK, :])
         x_window = shared.tile([P, T], I32, name="x_window", offset=0, align_bytes=64)
         nc.sync.dma_start(x_window[:], x_words[0].rearrange("p n t -> p (n t)").bitcast(I32))
-        w2_raw = keep.tile([P, N], I32, name="w2_raw", align_bytes=64)
-        nc.sync.dma_start(w2_raw[:], w2_words[0].rearrange("p n t -> p (n t)").bitcast(I32))
+        nc.sync.dma_start(west_sb[:], west)
         w2s_raw = keep.tile([P, N], U8, name="w2s_raw", align_bytes=64)
         nc.gpsimd.memset(w2s_raw[:].bitcast(I32), 0)
-        nc.sync.dma_start(w2s_raw[0:P:SPREAD].bitcast(I32), w2_scales[0].bitcast(I32))
+        nc.scalar.dma_start(w2s_raw[0:P:SPREAD].bitcast(I32), w2_scales[0].bitcast(I32))
         ident = keep.tile([P, P], F32, name="ident")
         make_identity(nc, ident[:])
         warm = keep.tile([P, 2], F32, name="warm")
@@ -84,6 +84,8 @@ def tile_picked_waveeq_none_po_kernel(
         xs_picked = keep.tile([P, S], U8, name="xs_picked", align_bytes=64)
         nc.vector.tensor_copy(xs_picked[:], xs_window[:].indirect(offs_sb[:]))
         nc.vector.tensor_copy(xs_plane[:].bitcast(I32), xs_picked[:].bitcast(I32))
+        w2_raw = keep.tile([P, N], I32, name="w2_raw", tag="xs_window", align_bytes=64)
+        nc.scalar.dma_start(w2_raw[:], w2_words[0].rearrange("p n t -> p (n t)").bitcast(I32))
         for a in range(1, PACK):
             nc.scalar.dma_start(xs_plane[a:P:QUAD].bitcast(I32), xs_picked[SPREAD * a : P : QUAD].bitcast(I32))
 
@@ -225,7 +227,9 @@ def tile_picked_waveeq_none_po_kernel(
         span_a, span_b, span_c = cols(0, HALF), block_cols(2), block_cols(LAST)
         parts = [(0, cols(0, HALF), 0), (0, cols(HALF, HALF), 1)] + [(t, cols(0, S), t + 1) for t in range(1, PACK)]
         banks = [first_product(*part) for part in parts]
-        for (t, span, index), y_bank in zip(parts, banks):
+        nc.scalar.copy(y[0][:, span_a], banks[0][:])
+        nc.vector.tensor_scalar(m2y[:, 0, span_a], banks[0][:], -2.0, None, MULT)
+        for (t, span, index), y_bank in list(zip(parts, banks))[1:]:
             take_y(t, span, y_bank)
         rest_bank = [bank(5 + b, [P, PACK, P], "rest_bank%d" % b) for b in range(TURNED)]
         for b in range(TURNED):

@@ -72,6 +72,8 @@ def tile_picked_waveeq_none_po_kernel(
         w2s_raw = keep.tile([P, N], U8, name="w2s_raw", align_bytes=64)
         nc.gpsimd.memset(w2s_raw[:].bitcast(I32), 0)
         nc.scalar.dma_start(w2s_raw[0:P:SPREAD].bitcast(I32), w2_scales[0].bitcast(I32))
+        xs_plane = keep.tile([P, S], U8, name="xs_plane", align_bytes=64)
+        nc.gpsimd.memset(xs_plane[:].bitcast(I32), 0)
         ident = keep.tile([P, P], F32, name="ident")
         make_identity(nc, ident[:])
         warm = keep.tile([P, 2], F32, name="warm")
@@ -80,14 +82,13 @@ def tile_picked_waveeq_none_po_kernel(
         w2_plane = keep.tile([P, PACK, P], U8, name="w2_plane", align_bytes=64)
         nc.gpsimd.memset(w2_plane[:].bitcast(I32), 0)
 
-        xs_plane = keep.tile([P, S], U8, name="xs_plane", align_bytes=64)
         xs_picked = keep.tile([P, S], U8, name="xs_picked", align_bytes=64)
         nc.vector.tensor_copy(xs_picked[:], xs_window[:].indirect(offs_sb[:]))
-        nc.vector.tensor_copy(xs_plane[:].bitcast(I32), xs_picked[:].bitcast(I32))
+        for a in range(PACK):
+            queue = nc.scalar if a % 2 else nc.sync
+            queue.dma_start(xs_plane[a:P:QUAD].bitcast(I32), xs_picked[SPREAD * a : P : QUAD].bitcast(I32))
         w2_raw = keep.tile([P, N], I32, name="w2_raw", tag="xs_window", align_bytes=64)
         nc.scalar.dma_start(w2_raw[:], w2_words[0].rearrange("p n t -> p (n t)").bitcast(I32))
-        for a in range(1, PACK):
-            nc.scalar.dma_start(xs_plane[a:P:QUAD].bitcast(I32), xs_picked[SPREAD * a : P : QUAD].bitcast(I32))
 
         w1_grouped = keep.tile([P, PACK, P, PACK], BF16, name="w1_grouped", tag="w1_grouped", align_bytes=64)
         w1_dst = w1_grouped[:].rearrange("p t m j -> p m t j")

@@ -26,7 +26,7 @@ ROWS = 16
 SPREAD = P // ROWS
 BLOCKS = S // P
 HALF = S // 2
-W1_ON_VECTOR = 80
+W1_ON_VECTOR = 84
 LAST = PACK - 1
 TURNED = 3
 AB = TURNED * P
@@ -79,8 +79,6 @@ def tile_picked_waveeq_none_po_kernel(
         warm = keep.tile([P, 2], F32, name="warm")
         nc.vector.memset(warm[:, 0:1], 0.0)
         nc.scalar.copy(warm[:, 1:2], warm[:, 0:1])
-        w2_plane = keep.tile([P, PACK, P], U8, name="w2_plane", align_bytes=64)
-        nc.gpsimd.memset(w2_plane[:].bitcast(I32), 0)
 
         xs_picked = keep.tile([P, S], U8, name="xs_picked", align_bytes=64)
         nc.vector.tensor_copy(xs_picked[:], xs_window[:].indirect(offs_sb[:]))
@@ -90,16 +88,20 @@ def tile_picked_waveeq_none_po_kernel(
         w2_raw = keep.tile([P, N], I32, name="w2_raw", tag="xs_window", align_bytes=64)
         nc.scalar.dma_start(w2_raw[:], w2_words[0].rearrange("p n t -> p (n t)").bitcast(I32))
 
-        w1_grouped = keep.tile([P, PACK, P, PACK], BF16, name="w1_grouped", tag="w1_grouped", align_bytes=64)
+        w1_grouped = keep.tile([P, PACK, P, PACK], BF16, name="w1_grouped", align_bytes=64)
         w1_dst = w1_grouped[:].rearrange("p t m j -> p m t j")
         w1_src = w1_raw[:].rearrange("p j (m t) -> p m t j", t=PACK)
         nc.vector.tensor_copy(w1_dst[:, 0:W1_ON_VECTOR], w1_src[:, 0:W1_ON_VECTOR])
         nc.scalar.copy(w1_dst[:, W1_ON_VECTOR:P], w1_src[:, W1_ON_VECTOR:P])
-        w1_codes = keep.tile([P, H], U32, name="w1_codes", align_bytes=64)
-        w1_scales = keep.tile([P, H], U8, name="w1_scales", align_bytes=64)
-        nc.vector.quantize_mx(
-            out=w1_codes[:].bitcast(FP8X4), scales=w1_scales[:], in_=w1_grouped[:].rearrange("p t m j -> p (t m j)")
-        )
+        w1_codes, w1_scales = {}, {}
+
+        def quantise_w1(u, codes):
+            w1_codes[u] = codes
+            w1_scales[u] = keep.tile([P, HALF], U8, name="w1_scales%d" % u, align_bytes=64)
+            pair = w1_grouped[:, cols(2 * u, 2)].rearrange("p t m j -> p (t m j)")
+            nc.vector.quantize_mx(out=codes[:].bitcast(FP8X4), scales=w1_scales[u][:], in_=pair)
+
+        quantise_w1(0, keep.tile([P, HALF], U32, name="w1_codes0", align_bytes=64))
 
         prev_rows = prev.rearrange("(p t) j -> p t j", t=PACK)
         prev_half = []
@@ -108,17 +110,18 @@ def tile_picked_waveeq_none_po_kernel(
             nc.sync.dma_start(tile[:], prev_rows[:, :, cols(HALF * h, HALF)])
             prev_half.append(tile)
 
-        x_picked = keep.tile([P, S], U32, name="x_picked", tag="w1_grouped", align_bytes=64)
+        x_picked = shared.tile([P, S], U32, name="x_picked", offset=16384, align_bytes=64)
         for h in range(2):
             span = cols(HALF * h, HALF)
             nc.vector.tensor_copy(x_picked[:, span], x_window[:].bitcast(U32).indirect(offs_sb[:, list_cols(span)]))
 
+        quantise_w1(1, shared.tile([P, HALF], U32, name="w1_codes1", offset=6144, align_bytes=64))
         w2_codes = shared.tile([P, PACK, P], I32, name="w2_codes", offset=0, align_bytes=64)
         nc.vector.tensor_copy(
             w2_codes[:].rearrange("p t (g i) -> p g t i", i=4),
             w2_raw[:].rearrange("p (g i t) -> p g t i", i=4, t=PACK),
         )
-        w2s_dealt = shared.tile([P, PACK, P], U8, name="w2s_dealt", offset=2048, align_bytes=64)
+        w2s_dealt = keep.tile([P, PACK, P], U8, name="w2s_dealt", align_bytes=64)
         nc.vector.tensor_copy(
             w2s_dealt[:].rearrange("p t (g i) -> p g t i", i=16),
             w2s_raw[:].rearrange("p (g i t) -> p g t i", i=16, t=PACK),
@@ -128,6 +131,8 @@ def tile_picked_waveeq_none_po_kernel(
         c_last = shared.tile([P, P], F32, name="c_last", offset=4096, align_bytes=64)
         nc.sync.dma_start(c_last[:], c2[:, block_cols(LAST)])
 
+        w2_plane = shared.tile([P, PACK, P], U8, name="w2_plane", offset=2048, align_bytes=64)
+        nc.gpsimd.memset(w2_plane[:].bitcast(I32), 0)
         for a in range(PACK):
             nc.sync.dma_start(w2_plane[a:P:QUAD].bitcast(I32), w2s_dealt[SPREAD * a : P : QUAD].bitcast(I32))
 
@@ -143,8 +148,8 @@ def tile_picked_waveeq_none_po_kernel(
             y_bank = bank(index, [P, span.stop - span.start], "y_bank%d_%d" % (t, span.start))
             nc.tensor.matmul_mx(
                 out=y_bank[:],
-                lhsT=w1_codes[:, block_cols(t)].bitcast(FP8X4),
-                lhsT_scale=w1_scales[:, block_cols(t)],
+                lhsT=w1_codes[t // 2][:, block_cols(t % 2)].bitcast(FP8X4),
+                lhsT_scale=w1_scales[t // 2][:, block_cols(t % 2)],
                 rhs=x_picked[:, span].bitcast(FP8X4),
                 rhs_scale=xs_plane[:, span],
                 start=True,
@@ -190,8 +195,8 @@ def tile_picked_waveeq_none_po_kernel(
                 z_grouped[b][:].bitcast(F32).rearrange("p (j u) -> p j u", u=2), back[:].rearrange("p u j -> p j u")
             )
 
-        def second_product(b, *indices):
-            z_codes = keep.tile([P, P], U32, name="z_codes%d" % b, align_bytes=64)
+        def second_product(b, *indices, tag=None):
+            z_codes = keep.tile([P, P], U32, name="z_codes%d" % b, tag=tag or "z_codes%d" % b, align_bytes=64)
             z_scales = keep.tile([P, P], U8, name="z_scales%d" % b, align_bytes=64)
             nc.vector.quantize_mx(out=z_codes[:].bitcast(FP8X4), scales=z_scales[:], in_=z_grouped[b][:])
             step = PACK // len(indices)
@@ -212,25 +217,20 @@ def tile_picked_waveeq_none_po_kernel(
             queue = nc.scalar if b == LAST else nc.sync
             queue.dma_start(out_rows[:, :, block_cols(b)], out_sb[b][:])
 
-        def hand_on(b):
-            span = block_cols(b)
+        def round_out(b, grouped):
             nc.vector.tensor_copy(
-                out_grouped[:, b, :].rearrange("p (g i t) -> p g t i", i=2, t=PACK),
+                grouped.rearrange("p (g i t) -> p g t i", i=2, t=PACK),
                 out_sb[b][:].rearrange("p t (g i) -> p g t i", i=2),
             )
-            nc.vector.quantize_mx(
-                out=out_words[:, span].bitcast(FP8X4), scales=out_scales[:, span], in_=out_grouped[:, b, :]
-            )
-            if b % 2:
-                stored = cols(P * (b - 1), HALF)
-                nc.sync.dma_start(out_word_rows[:, stored], out_words[:, stored].bitcast(I32))
+
+        def hand_on(blocks, grouped):
+            span = slice(P * blocks.start, P * blocks.stop)
+            nc.vector.quantize_mx(out=out_words[:, span].bitcast(FP8X4), scales=out_scales[:, span], in_=grouped)
 
         span_a, span_b, span_c = cols(0, HALF), block_cols(2), block_cols(LAST)
-        parts = [(0, cols(0, HALF), 0), (0, cols(HALF, HALF), 1)] + [(t, cols(0, S), t + 1) for t in range(1, PACK)]
+        parts = [(0, span_a, 0), (0, cols(HALF, HALF), 1)] + [(t, cols(0, S), t + 1) for t in range(1, PACK)]
         banks = [first_product(*part) for part in parts]
-        nc.scalar.copy(y[0][:, span_a], banks[0][:])
-        nc.vector.tensor_scalar(m2y[:, 0, span_a], banks[0][:], -2.0, None, MULT)
-        for (t, span, index), y_bank in list(zip(parts, banks))[1:]:
+        for (t, span, index), y_bank in zip(parts, banks):
             take_y(t, span, y_bank)
         rest_bank = [bank(5 + b, [P, PACK, P], "rest_bank%d" % b) for b in range(TURNED)]
         for b in range(TURNED):
@@ -281,14 +281,19 @@ def tile_picked_waveeq_none_po_kernel(
         rest_last = keep.tile([P, PACK, P], F32, name="rest_last", tag="east_a%d" % LAST, align_bytes=64)
         nc.gpsimd.tensor_tensor(rest_last[:], prev_half[1][:, :, block_cols(1)], m2y[:, :, span_c], ADD)
 
+        lap_c = [
+            keep.tile([P, planes, P], F32, name="lap_c%d" % planes, tag=tag, align_bytes=64)
+            for planes, tag in ((LAST, "rest2_0"), (1, "z_grouped0"))
+        ]
+        for t in range(LAST):
+            gather(lap_c[0][:, t, :], t, west_sb, span_c, east_bc[t][:, block_cols(1)])
         second_product(0, 2)
         second_product(1, 3)
-        lap_c = keep.tile([P, PACK, P], F32, name="lap_c", tag="rest2_0", align_bytes=64)
-        for t in range(PACK):
-            gather(lap_c[:, t, :], t, west_sb, span_c, east_bc[t][:, block_cols(1)])
-        scaled = keep.tile([P, PACK, P], F32, name="scaled", tag="z_grouped0", align_bytes=64)
-        nc.vector.tensor_tensor(scaled[:], lap_c[:], c_last[:].unsqueeze(1).to_broadcast([P, PACK, P]), MULT)
-        second_product(2, 4)
+        gather(lap_c[1][:, 0, :], LAST, west_sb, span_c, east_bc[LAST][:, block_cols(1)])
+        scaled = keep.tile([P, PACK, P], F32, name="scaled", tag="z_grouped1", align_bytes=64)
+        nc.vector.tensor_tensor(scaled[:, 0:LAST], lap_c[0][:], c_last[:].unsqueeze(1).to_broadcast([P, LAST, P]), MULT)
+        nc.vector.tensor_tensor(scaled[:, LAST], lap_c[1][:, 0], c_last[:], MULT)
+        second_product(2, 4, tag="rest2_0")
         z_grouped[LAST] = keep.tile([P, P * PACK], BF16, name="z_grouped%d" % LAST, align_bytes=64)
         nc.vector.tensor_tensor(
             z_grouped[LAST][:].rearrange("p (g i t) -> p g t i", i=2, t=PACK),
@@ -296,10 +301,18 @@ def tile_picked_waveeq_none_po_kernel(
             rest_last[:].rearrange("p t (g i) -> p g t i", i=2),
             SUB,
         )
+        first_grouped = keep.tile([P, P * PACK], BF16, name="first_grouped", tag="z_grouped2", align_bytes=64)
+        round_out(0, first_grouped[:])
         second_product(LAST, 5, 6)
-        out_grouped = keep.tile([P, BLOCKS, P * PACK], BF16, name="out_grouped", tag="east_a%d" % LAST, align_bytes=64)
-        for b in range(BLOCKS):
-            hand_on(b)
+        hand_on(cols(0, 1), first_grouped[:])
+        late_grouped = keep.tile([P, LAST, P * PACK], BF16, name="late_grouped", tag="east_a%d" % LAST, align_bytes=64)
+        for b in (1, 2):
+            round_out(b, late_grouped[:, b - 1, :])
+            hand_on(cols(b, 1), late_grouped[:, b - 1, :])
+        nc.sync.dma_start(out_word_rows[:, 0:AB], out_words[:, 0:AB].bitcast(I32))
+        round_out(LAST, late_grouped[:, 2, :])
+        hand_on(cols(LAST, 1), late_grouped[:, 2, :])
+        nc.sync.dma_start(out_word_rows[:, span_c], out_words[:, span_c].bitcast(I32))
 
         for q in range(P // QUAD):
             queue = nc.scalar if q % 2 else nc.sync

@@ -26,7 +26,7 @@ ROWS = 16
 SPREAD = P // ROWS
 BLOCKS = S // P
 HALF = S // 2
-W1_ON_VECTOR = 84
+W1_ON_VECTOR = 92
 LAST = PACK - 1
 TURNED = 3
 AB = TURNED * P
@@ -57,21 +57,22 @@ def tile_picked_waveeq_none_po_kernel(
         offs_sb = lists.tile([P, S // GROUP], U16, name="offs_sb")
         east_sb = lists.tile([P, S // GROUP], U16, name="east_sb")
         west_sb = lists.tile([P, S // GROUP], U16, name="west_sb")
-        xs_window = keep.tile([P, T], U8, name="xs_window", tag="xs_window", align_bytes=64)
+        xs_window = shared.tile([P, T], U8, name="xs_window", offset=26624, align_bytes=64)
         nc.gpsimd.memset(xs_window[:].bitcast(I32), 0)
-        w1_raw = shared.tile([P, PACK, H], F32, name="w1_raw", offset=8192, align_bytes=64)
-        w1_rows = w1.rearrange("(p j) c -> p j c", j=PACK)
-        nc.sync.dma_start(w1_raw[:, 0, :], w1_rows[:, 0, :])
+        w2s_raw = keep.tile([P, N], U8, name="w2s_raw", align_bytes=64)
+        nc.gpsimd.memset(w2s_raw[:].bitcast(I32), 0)
+        w1_raw = shared.tile([P, PACK, H], F32, name="w1_raw", offset=16384, align_bytes=64)
+        w1_rows = w1.rearrange("(p j) c -> p (j c)", j=PACK)
+        w1_flat = w1_raw[:].rearrange("p j c -> p (j c)")
+        nc.sync.dma_start(w1_flat[:, 0:768], w1_rows[:, 0:768])
         nc.sync.dma_start(offs_sb[:], offs)
         nc.sync.dma_start(east_sb[:], east)
         nc.sync.dma_start(xs_window[0:P:SPREAD].bitcast(I32), x_scales[0].bitcast(I32))
-        nc.sync.dma_start(w1_raw[:, 1:PACK, :], w1_rows[:, 1:PACK, :])
-        x_window = shared.tile([P, T], I32, name="x_window", offset=0, align_bytes=64)
+        nc.sync.dma_start(w2s_raw[0:P:SPREAD].bitcast(I32), w2_scales[0].bitcast(I32))
+        nc.sync.dma_start(w1_flat[:, 768 : PACK * H], w1_rows[:, 768 : PACK * H])
+        x_window = shared.tile([P, T], I32, name="x_window", offset=4096, align_bytes=64)
         nc.sync.dma_start(x_window[:], x_words[0].rearrange("p n t -> p (n t)").bitcast(I32))
         nc.sync.dma_start(west_sb[:], west)
-        w2s_raw = keep.tile([P, N], U8, name="w2s_raw", align_bytes=64)
-        nc.gpsimd.memset(w2s_raw[:].bitcast(I32), 0)
-        nc.scalar.dma_start(w2s_raw[0:P:SPREAD].bitcast(I32), w2_scales[0].bitcast(I32))
         xs_plane = keep.tile([P, S], U8, name="xs_plane", align_bytes=64)
         nc.gpsimd.memset(xs_plane[:].bitcast(I32), 0)
         ident = keep.tile([P, P], F32, name="ident")
@@ -85,10 +86,8 @@ def tile_picked_waveeq_none_po_kernel(
         for a in range(PACK):
             queue = nc.scalar if a % 2 else nc.sync
             queue.dma_start(xs_plane[a:P:QUAD].bitcast(I32), xs_picked[SPREAD * a : P : QUAD].bitcast(I32))
-        w2_raw = keep.tile([P, N], I32, name="w2_raw", tag="xs_window", align_bytes=64)
-        nc.scalar.dma_start(w2_raw[:], w2_words[0].rearrange("p n t -> p (n t)").bitcast(I32))
 
-        w1_grouped = keep.tile([P, PACK, P, PACK], BF16, name="w1_grouped", align_bytes=64)
+        w1_grouped = shared.tile([P, PACK, P, PACK], BF16, name="w1_grouped", offset=27136, align_bytes=64)
         w1_dst = w1_grouped[:].rearrange("p t m j -> p m t j")
         w1_src = w1_raw[:].rearrange("p j (m t) -> p m t j", t=PACK)
         nc.vector.tensor_copy(w1_dst[:, 0:W1_ON_VECTOR], w1_src[:, 0:W1_ON_VECTOR])
@@ -103,35 +102,37 @@ def tile_picked_waveeq_none_po_kernel(
 
         quantise_w1(0, keep.tile([P, HALF], U32, name="w1_codes0", align_bytes=64))
 
+        w2_raw = shared.tile([P, N], I32, name="w2_raw", offset=16384, align_bytes=64)
+        nc.scalar.dma_start(w2_raw[:], w2_words[0].rearrange("p n t -> p (n t)").bitcast(I32))
         prev_rows = prev.rearrange("(p t) j -> p t j", t=PACK)
         prev_half = []
         for h in range(2):
-            tile = shared.tile([P, PACK, HALF], F32, name="prev%d" % h, offset=8192 + 4096 * h, align_bytes=64)
+            tile = shared.tile([P, PACK, HALF], F32, name="prev%d" % h, offset=1024 + 10240 * h, align_bytes=64)
             nc.sync.dma_start(tile[:], prev_rows[:, :, cols(HALF * h, HALF)])
             prev_half.append(tile)
 
-        x_picked = shared.tile([P, S], U32, name="x_picked", offset=16384, align_bytes=64)
+        x_picked = shared.tile([P, S], U32, name="x_picked", offset=24576, align_bytes=64)
         for h in range(2):
             span = cols(HALF * h, HALF)
             nc.vector.tensor_copy(x_picked[:, span], x_window[:].bitcast(U32).indirect(offs_sb[:, list_cols(span)]))
 
-        quantise_w1(1, shared.tile([P, HALF], U32, name="w1_codes1", offset=6144, align_bytes=64))
-        w2_codes = shared.tile([P, PACK, P], I32, name="w2_codes", offset=0, align_bytes=64)
+        quantise_w1(1, shared.tile([P, HALF], U32, name="w1_codes1", offset=8704, align_bytes=64))
+        w2_codes = shared.tile([P, PACK, P], I32, name="w2_codes", offset=5120, align_bytes=64)
         nc.vector.tensor_copy(
             w2_codes[:].rearrange("p t (g i) -> p g t i", i=4),
             w2_raw[:].rearrange("p (g i t) -> p g t i", i=4, t=PACK),
         )
-        w2s_dealt = keep.tile([P, PACK, P], U8, name="w2s_dealt", align_bytes=64)
+        w2s_dealt = shared.tile([P, PACK, P], U8, name="w2s_dealt", offset=26624, align_bytes=64)
         nc.vector.tensor_copy(
             w2s_dealt[:].rearrange("p t (g i) -> p g t i", i=16),
             w2s_raw[:].rearrange("p (g i t) -> p g t i", i=16, t=PACK),
         )
-        c_rows = shared.tile([P, P], F32, name="c_rows", offset=5120, align_bytes=64)
+        c_rows = shared.tile([P, P], F32, name="c_rows", offset=8192, align_bytes=64)
         nc.sync.dma_start(c_rows[:], c2.rearrange("r (b j) -> (r b) j", j=P)[0:P, :])
-        c_last = shared.tile([P, P], F32, name="c_last", offset=4096, align_bytes=64)
+        c_last = shared.tile([P, P], F32, name="c_last", offset=7680, align_bytes=64)
         nc.sync.dma_start(c_last[:], c2[:, block_cols(LAST)])
 
-        w2_plane = shared.tile([P, PACK, P], U8, name="w2_plane", offset=2048, align_bytes=64)
+        w2_plane = shared.tile([P, PACK, P], U8, name="w2_plane", offset=7168, align_bytes=64)
         nc.gpsimd.memset(w2_plane[:].bitcast(I32), 0)
         for a in range(PACK):
             nc.sync.dma_start(w2_plane[a:P:QUAD].bitcast(I32), w2s_dealt[SPREAD * a : P : QUAD].bitcast(I32))
@@ -303,7 +304,7 @@ def tile_picked_waveeq_none_po_kernel(
         )
         first_grouped = keep.tile([P, P * PACK], BF16, name="first_grouped", tag="z_grouped2", align_bytes=64)
         round_out(0, first_grouped[:])
-        second_product(LAST, 5, 6)
+        second_product(LAST, 5, 6, 0, 1)
         hand_on(cols(0, 1), first_grouped[:])
         late_grouped = keep.tile([P, LAST, P * PACK], BF16, name="late_grouped", tag="east_a%d" % LAST, align_bytes=64)
         for b in (1, 2):

@@ -167,7 +167,10 @@ def tile_picked_waveeq_none_po_kernel(
 
         def take_rest(b, pairs):
             tag = "rest%d_%d" % (b, pairs.start)
-            tile = keep.tile([P, pairs.stop - pairs.start, P, 2], F32, name=tag, tag=tag, align_bytes=64)
+            if b < 2:
+                tile = shared.tile([P, 2, P, 2], F32, name=tag, offset=32768 + 2048 * b, align_bytes=64)
+            else:
+                tile = keep.tile([P, 1, P, 2], F32, name=tag, tag=tag, align_bytes=64)
             nc.scalar.copy(tile[:], rest_bank[b][:].rearrange("j (u e) p -> j u p e", e=2)[:, pairs])
             for u in range(pairs.start, pairs.stop):
                 rest[b, u] = tile[:, u - pairs.start]
@@ -235,11 +238,13 @@ def tile_picked_waveeq_none_po_kernel(
             take_y(t, span, y_bank)
         rest_bank = [bank(5 + b, [P, PACK, P], "rest_bank%d" % b) for b in range(TURNED)]
         for b in range(TURNED):
-            for t in range(PACK):
+            for t in range(PACK if b == 2 else LAST):
                 turn_into(rest_bank[b][:, t, :], prev_half[b // 2][:, t, block_cols(b % 2)], t == 0, False)
         for t in range(PACK):
             for b in range(TURNED):
-                turn_into(rest_bank[b][:, t, :], m2y[:, t, block_cols(b)], False, t == LAST)
+                turn_into(rest_bank[b][:, t, :], m2y[:, t, block_cols(b)], False, t == LAST and b == 2)
+                if t == LAST and b < 2:
+                    turn_into(rest_bank[b][:, t, :], prev_half[0][:, t, block_cols(b)], False, True)
         c_bank = bank(0, [P, P], "c_bank")
         nc.tensor.transpose(c_bank[:], c_rows[:], ident[:])
         c_col = keep.tile([P, BLOCKS], F32, name="c_col")
@@ -252,48 +257,67 @@ def tile_picked_waveeq_none_po_kernel(
 
         span_bc = cols(HALF, HALF)
         east_a = [keep.tile([P, HALF], F32, name="east_a%d" % t, tag="east_a%d" % t, align_bytes=64) for t in range(PACK)]
-        east_bc = [keep.tile([P, HALF], F32, name="east_bc%d" % t) for t in range(PACK)]
-        lap_ab = [keep.tile([P, TURNED * P], F32, name="lap_ab%d" % t) for t in range(PACK)]
+        east_bc = [keep.tile([P, HALF], F32, name="east_bc%d" % t) for t in range(LAST)]
+        east_b = [tile[:, block_cols(0)] for tile in east_bc] + [keep.tile([P, P], F32, name="east_b")[:]]
+        east_c = [tile[:, block_cols(1)] for tile in east_bc]
+        lap_a = [keep.tile([P, HALF], F32, name="lap_a%d" % t) for t in range(PACK)]
+        lap_b = [keep.tile([P, P], F32, name="lap_b%d" % t) for t in (0, 1)]
+        lap_b.append(shared.tile([P, P], F32, name="lap_b2", offset=1024, align_bytes=64))
+
+        def turn_lap(pair_bank, t, blocks):
+            for n, b in enumerate(blocks):
+                lap = lap_b[t][:] if b == 2 else lap_a[t][:, block_cols(b)]
+                turn_into(pair_bank[:, n, t % 2, :], lap, True, True)
+                lap_turned[b, t // 2] = pair_bank[:, n]
+
         for t in range(PACK):
             gather(east_a[t][:], t, east_sb, span_a, m2y[:, t, span_a])
-            gather(east_bc[t][:], t, east_sb, span_bc, m2y[:, t, span_bc])
-            gather(lap_ab[t][:, span_a], t, west_sb, span_a, east_a[t][:])
-            gather(lap_ab[t][:, span_b], t, west_sb, span_b, east_bc[t][:, block_cols(0)])
-        for u in range(2):
-            for blocks, index in (((0, 1), 4 + 2 * u), ((2,), 5 + 2 * u)):
-                pair_bank = bank(index, [P, len(blocks), 2, P], "lap_turned%d_%d" % (blocks[0], u))
-                for e in range(2):
-                    for n, b in enumerate(blocks):
-                        turn_into(pair_bank[:, n, e, :], lap_ab[2 * u + e][:, block_cols(b)], True, True)
-                for n, b in enumerate(blocks):
-                    lap_turned[b, u] = pair_bank[:, n]
+            if t < LAST:
+                gather(east_bc[t][:], t, east_sb, span_bc, m2y[:, t, span_bc])
+            else:
+                gather(east_b[t], t, east_sb, span_b, m2y[:, t, span_b])
+            gather(lap_a[t][:], t, west_sb, span_a, east_a[t][:])
+            if t < 2:
+                gather(lap_b[t][:], t, west_sb, span_b, east_b[t])
+        gather(lap_b[2][:], 2, west_sb, span_b, east_b[2])
+        pair_banks = {}
+        for u, blocks, index in ((0, (0, 1), 4), (0, (2,), 5), (1, (0, 1), 6), (1, (2,), 7)):
+            pair_banks[u, blocks] = bank(index, [P, len(blocks), 2, P], "lap_turned%d_%d" % (blocks[0], u))
+            for t in range(2 * u, min(2 * u + 2, LAST if blocks == (2,) else PACK)):
+                turn_lap(pair_banks[u, blocks], t, blocks)
 
-        for b in range(TURNED):
+        for b in (0, 1):
             z_turned[b] = keep.tile([P, 2, P, 2], BF16, name="z_turned%d" % b, align_bytes=64)
         for b in (0, 1):
             combine(b, 0)
         for b in (0, 1):
             combine(b, 1)
             turn_back(b, 1 - b)
-        for u in range(2):
-            combine(2, u)
-        turn_back(2, 7)
 
         rest_last = keep.tile([P, PACK, P], F32, name="rest_last", tag="east_a%d" % LAST, align_bytes=64)
         nc.gpsimd.tensor_tensor(rest_last[:], prev_half[1][:, :, block_cols(1)], m2y[:, :, span_c], ADD)
 
+        lap_b.append(shared.tile([P, P], F32, name="lap_b3", offset=32768, align_bytes=64))
+        gather(lap_b[LAST][:], LAST, west_sb, span_b, east_b[LAST])
+        turn_lap(pair_banks[1, (2,)], LAST, (2,))
+        z_turned[2] = shared.tile([P, 2, P, 2], BF16, name="z_turned2", offset=32768 + 512, align_bytes=64)
+        combine(2, 0)
+        east_c.append(shared.tile([P, P], F32, name="east_c", offset=32768 + 2048, align_bytes=64)[:])
+        gather(east_c[LAST], LAST, east_sb, span_c, m2y[:, LAST, span_c])
         lap_c = [
             keep.tile([P, planes, P], F32, name="lap_c%d" % planes, tag=tag, align_bytes=64)
-            for planes, tag in ((LAST, "rest2_0"), (1, "z_grouped0"))
+            for planes, tag in ((1, "rest2_0"), (LAST, "z_grouped0"))
         ]
-        for t in range(LAST):
-            gather(lap_c[0][:, t, :], t, west_sb, span_c, east_bc[t][:, block_cols(1)])
+        gather(lap_c[0][:, 0, :], 0, west_sb, span_c, east_c[0])
+        combine(2, 1)
+        turn_back(2, 7)
         second_product(0, 2)
         second_product(1, 3)
-        gather(lap_c[1][:, 0, :], LAST, west_sb, span_c, east_bc[LAST][:, block_cols(1)])
+        for t in range(1, PACK):
+            gather(lap_c[1][:, t - 1, :], t, west_sb, span_c, east_c[t])
         scaled = keep.tile([P, PACK, P], F32, name="scaled", tag="z_grouped1", align_bytes=64)
-        nc.vector.tensor_tensor(scaled[:, 0:LAST], lap_c[0][:], c_last[:].unsqueeze(1).to_broadcast([P, LAST, P]), MULT)
-        nc.vector.tensor_tensor(scaled[:, LAST], lap_c[1][:, 0], c_last[:], MULT)
+        nc.vector.tensor_tensor(scaled[:, 0], lap_c[0][:, 0], c_last[:], MULT)
+        nc.vector.tensor_tensor(scaled[:, 1:PACK], lap_c[1][:], c_last[:].unsqueeze(1).to_broadcast([P, LAST, P]), MULT)
         second_product(2, 4, tag="rest2_0")
         z_grouped[LAST] = keep.tile([P, P * PACK], BF16, name="z_grouped%d" % LAST, align_bytes=64)
         nc.vector.tensor_tensor(

@@ -28,8 +28,6 @@ BLOCKS = S // P
 HALF = S // 2
 W1_ON_VECTOR = 92
 LAST = PACK - 1
-TURNED = 3
-AB = TURNED * P
 
 
 def tile_picked_waveeq_none_po_kernel(
@@ -104,6 +102,11 @@ def tile_picked_waveeq_none_po_kernel(
 
         w2_raw = shared.tile([P, N], I32, name="w2_raw", offset=16384, align_bytes=64)
         nc.scalar.dma_start(w2_raw[:], w2_words[0].rearrange("p n t -> p (n t)").bitcast(I32))
+        c_col = shared.tile([P, BLOCKS], F32, name="c_col", offset=8192, align_bytes=64)
+        with nc.allow_non_contiguous_dma(reason="one value of c2 for each partition and block"):
+            nc.sync.dma_start(c_col[:], c2[0].rearrange("(b p) -> p b", p=P))
+        d_col = keep.tile([P, BLOCKS], F32, name="d_col")
+        nc.gpsimd.tensor_scalar(d_col[:], c_col[:], -2.0, 2.0, MULT, ADD)
         prev_rows = prev.rearrange("(p t) j -> p t j", t=PACK)
         prev_half = []
         for h in range(2):
@@ -127,217 +130,154 @@ def tile_picked_waveeq_none_po_kernel(
             w2s_dealt[:].rearrange("p t (g i) -> p g t i", i=16),
             w2s_raw[:].rearrange("p (g i t) -> p g t i", i=16, t=PACK),
         )
-        c_rows = shared.tile([P, P], F32, name="c_rows", offset=8192, align_bytes=64)
-        nc.sync.dma_start(c_rows[:], c2.rearrange("r (b j) -> (r b) j", j=P)[0:P, :])
-        c_last = shared.tile([P, P], F32, name="c_last", offset=7680, align_bytes=64)
-        nc.sync.dma_start(c_last[:], c2[:, block_cols(LAST)])
-
         w2_plane = shared.tile([P, PACK, P], U8, name="w2_plane", offset=7168, align_bytes=64)
         nc.gpsimd.memset(w2_plane[:].bitcast(I32), 0)
         for a in range(PACK):
             nc.sync.dma_start(w2_plane[a:P:QUAD].bitcast(I32), w2s_dealt[SPREAD * a : P : QUAD].bitcast(I32))
 
         y = [keep.tile([P, S], F32, name="y%d" % t) for t in range(PACK)]
-        m2y = keep.tile([P, PACK, S], F32, name="m2y")
         out_words = keep.tile([P, S], U32, name="out_words", align_bytes=64)
         out_scales = keep.tile([P, S], U8, name="out_scales", align_bytes=64)
         out_rows = out_0.rearrange("(p t) j -> p t j", t=PACK)
         out_word_rows = out_1[0].rearrange("p n t -> p (n t)").bitcast(I32)
-        rest, lap_turned, z_turned, z_grouped, out_sb = {}, {}, {}, {}, {}
+        y_turned, sum_turned, own_term, z_bank, z_grouped, out_sb, out_grouped = {}, {}, {}, {}, {}, {}, {}
 
-        def first_product(t, span, index):
-            y_bank = bank(index, [P, span.stop - span.start], "y_bank%d_%d" % (t, span.start))
+        def product(dst, lhs, lhs_scale, rhs, rhs_scale):
             nc.tensor.matmul_mx(
-                out=y_bank[:],
-                lhsT=w1_codes[t // 2][:, block_cols(t % 2)].bitcast(FP8X4),
-                lhsT_scale=w1_scales[t // 2][:, block_cols(t % 2)],
-                rhs=x_picked[:, span].bitcast(FP8X4),
-                rhs_scale=xs_plane[:, span],
+                out=dst,
+                lhsT=lhs.bitcast(FP8X4),
+                lhsT_scale=lhs_scale,
+                rhs=rhs.bitcast(FP8X4),
+                rhs_scale=rhs_scale,
                 start=True,
                 stop=True,
             )
+
+        def first_product(t, span, index):
+            y_bank = bank(index, [P, span.stop - span.start], "y_bank%d_%d" % (t, span.start))
+            w_cols = block_cols(t % 2)
+            product(y_bank[:], w1_codes[t // 2][:, w_cols], w1_scales[t // 2][:, w_cols], x_picked[:, span], xs_plane[:, span])
             return y_bank
 
-        def take_y(t, span, y_bank):
-            nc.scalar.copy(y[t][:, span], y_bank[:])
-            nc.scalar.activation(m2y[:, t, span], y_bank[:], COPY, scale=-2.0)
+        def first_product_turned(b, index):
+            y_turned[b] = bank(index, [P, PACK, P], "y_turned%d" % b)
+            for u in range(2):
+                dst = y_turned[b][:, cols(2 * u, 2), :].rearrange("j t p -> j (t p)")
+                product(dst, x_picked[:, block_cols(b)], xs_plane[:, block_cols(b)], w1_codes[u][:], w1_scales[u][:])
 
         def turn_into(dst, src, start, stop):
             nc.tensor.matmul(dst, src, ident[:], start=start, stop=stop, is_transpose=True)
 
-        def take_rest(b, pairs):
-            tag = "rest%d_%d" % (b, pairs.start)
-            if b < 2:
-                tile = shared.tile([P, 2, P, 2], F32, name=tag, offset=32768 + 2048 * b, align_bytes=64)
+        def turn_y(b, index):
+            y_turned[b] = bank(index, [P, PACK, P], "y_turned%d" % b)
+            for t in range(PACK):
+                turn_into(y_turned[b][:, t, :], y[t][:, block_cols(b)], True, True)
+
+        def looked_up(t, lists_sb, span):
+            return y[t][:].indirect(lists_sb[:, list_cols(span)])
+
+        def neighbours(t, half, west_on_vector):
+            span = cols(HALF * half, HALF)
+            east_vals = keep.tile([P, HALF], F32, name="east%d_%d" % (t, half))
+            nc.scalar.activation(east_vals[:], looked_up(t, east_sb, span), COPY)
+            second = keep.tile([P, HALF], F32, name="west%d_%d" % (t, half))
+            if west_on_vector:
+                nc.vector.tensor_tensor(second[:], looked_up(t, west_sb, span), east_vals[:], ADD)
+                terms = [second]
             else:
-                tile = keep.tile([P, 1, P, 2], F32, name=tag, tag=tag, align_bytes=64)
-            nc.scalar.copy(tile[:], rest_bank[b][:].rearrange("j (u e) p -> j u p e", e=2)[:, pairs])
-            for u in range(pairs.start, pairs.stop):
-                rest[b, u] = tile[:, u - pairs.start]
+                nc.scalar.activation(second[:], looked_up(t, west_sb, span), COPY)
+                terms = [east_vals, second]
+            for n in range(2):
+                for k, term in enumerate(terms):
+                    turn_into(sum_turned[2 * half + n][:, t, :], term[:, block_cols(n)], k == 0, k == len(terms) - 1)
 
-        def gather(dst, t, lists_sb, span, other):
-            nc.vector.tensor_tensor(dst, y[t][:].indirect(lists_sb[:, list_cols(span)]), other, ADD)
+        def take_own_term(b):
+            own_term[b] = keep.tile([P, PACK, P], F32, name="own_term%d" % b)
+            nc.scalar.activation(own_term[b][:], y_turned[b][:], COPY, scale=d_col[:, b : b + 1])
 
-        def combine(b, u):
-            nc.vector.scalar_tensor_tensor(
-                z_turned[b][:, u],
-                lap_turned[b, u].rearrange("j e p -> j p e"),
-                c_col[:, b : b + 1],
-                rest[b, u],
-                MULT,
+        def combine(b, index):
+            turned = keep.tile([P, PACK, P], F32, name="combined%d" % b)
+            nc.vector.scalar_tensor_tensor(turned[:], sum_turned[b][:], c_col[:, b : b + 1], own_term[b][:], MULT, ADD)
+            z_bank[b] = bank(index, [P, PACK, P], "z_bank%d" % b)
+            for t in range(PACK):
+                turn_into(z_bank[b][:, t, :], turned[:, t, :], True, True)
+
+        def finish_z(b):
+            z_grouped[b] = keep.tile([P, P * PACK], BF16, name="z_grouped%d" % b, align_bytes=64)
+            nc.vector.tensor_tensor(
+                z_grouped[b][:].rearrange("p (g i t) -> p g t i", i=2, t=PACK),
+                z_bank[b][:].rearrange("p t (g i) -> p g t i", i=2),
+                prev_half[b // 2][:, :, block_cols(b % 2)].rearrange("p t (g i) -> p g t i", i=2),
                 SUB,
             )
 
-        def turn_back(b, index):
-            pairs = z_turned[b][:].rearrange("j u p e -> j (u p e)").bitcast(F32)
-            back = bank(index, [P, 2, P], "back%d" % b)
-            for u in range(2):
-                nc.tensor.transpose(back[:, u, :], pairs[:, block_cols(u)], ident[:])
-            tag = "z_grouped%d" % b
-            z_grouped[b] = keep.tile([P, P * PACK], BF16, name=tag, tag=tag, align_bytes=64)
-            nc.scalar.copy(
-                z_grouped[b][:].bitcast(F32).rearrange("p (j u) -> p j u", u=2), back[:].rearrange("p u j -> p j u")
-            )
-
-        def second_product(b, *indices, tag=None):
-            z_codes = keep.tile([P, P], U32, name="z_codes%d" % b, tag=tag or "z_codes%d" % b, align_bytes=64)
+        def second_product(b, index):
+            z_codes = keep.tile([P, P], U32, name="z_codes%d" % b, align_bytes=64)
             z_scales = keep.tile([P, P], U8, name="z_scales%d" % b, align_bytes=64)
             nc.vector.quantize_mx(out=z_codes[:].bitcast(FP8X4), scales=z_scales[:], in_=z_grouped[b][:])
-            step = PACK // len(indices)
-            out_banks = [bank(index, [P, step, P], "out_bank%d_%d" % (b, index)) for index in indices]
+            out_bank = bank(index, [P, PACK, P], "out_bank%d" % b)
             for t in range(PACK):
-                nc.tensor.matmul_mx(
-                    out=out_banks[t // step][:, t % step, :],
-                    lhsT=w2_codes[:, t, :].bitcast(FP8X4),
-                    lhsT_scale=w2_plane[:, t, :],
-                    rhs=z_codes[:].bitcast(FP8X4),
-                    rhs_scale=z_scales[:],
-                    start=True,
-                    stop=True,
-                )
+                product(out_bank[:, t, :], w2_codes[:, t, :], w2_plane[:, t, :], z_codes[:], z_scales[:])
             out_sb[b] = keep.tile([P, PACK, P], F32, name="out_sb%d" % b)
-            for n, out_bank in enumerate(out_banks):
-                nc.scalar.copy(out_sb[b][:, cols(step * n, step), :], out_bank[:])
+            nc.scalar.copy(out_sb[b][:], out_bank[:])
             queue = nc.scalar if b == LAST else nc.sync
             queue.dma_start(out_rows[:, :, block_cols(b)], out_sb[b][:])
 
-        def round_out(b, grouped):
+        def round_out(b):
+            out_grouped[b] = keep.tile([P, P * PACK], BF16, name="out_grouped%d" % b, align_bytes=64)
             nc.vector.tensor_copy(
-                grouped.rearrange("p (g i t) -> p g t i", i=2, t=PACK),
+                out_grouped[b][:].rearrange("p (g i t) -> p g t i", i=2, t=PACK),
                 out_sb[b][:].rearrange("p t (g i) -> p g t i", i=2),
             )
 
-        def hand_on(blocks, grouped):
-            span = slice(P * blocks.start, P * blocks.stop)
-            nc.vector.quantize_mx(out=out_words[:, span].bitcast(FP8X4), scales=out_scales[:, span], in_=grouped)
+        def hand_on(b):
+            span = block_cols(b)
+            nc.vector.quantize_mx(out=out_words[:, span].bitcast(FP8X4), scales=out_scales[:, span], in_=out_grouped[b][:])
 
-        span_a, span_b, span_c = cols(0, HALF), block_cols(2), block_cols(LAST)
-        parts = [(0, span_a, 0), (0, cols(HALF, HALF), 1)] + [(t, cols(0, S), t + 1) for t in range(1, PACK)]
+        halves = [cols(0, HALF), cols(HALF, HALF)]
+        parts = [(0, halves[0], 0), (0, halves[1], 1)] + [(t, cols(0, S), t + 1) for t in range(1, PACK)]
         banks = [first_product(*part) for part in parts]
-        for (t, span, index), y_bank in zip(parts, banks):
-            take_y(t, span, y_bank)
-        rest_bank = [bank(5 + b, [P, PACK, P], "rest_bank%d" % b) for b in range(TURNED)]
-        for b in range(TURNED):
-            for t in range(PACK if b == 2 else LAST):
-                turn_into(rest_bank[b][:, t, :], prev_half[b // 2][:, t, block_cols(b % 2)], t == 0, False)
-        for t in range(PACK):
-            for b in range(TURNED):
-                turn_into(rest_bank[b][:, t, :], m2y[:, t, block_cols(b)], False, t == LAST and b == 2)
-                if t == LAST and b < 2:
-                    turn_into(rest_bank[b][:, t, :], prev_half[0][:, t, block_cols(b)], False, True)
-        c_bank = bank(0, [P, P], "c_bank")
-        nc.tensor.transpose(c_bank[:], c_rows[:], ident[:])
-        c_col = keep.tile([P, BLOCKS], F32, name="c_col")
-        nc.scalar.copy(c_col[:], c_bank[:, 0:BLOCKS])
-
         for b in (0, 1):
-            take_rest(b, cols(0, 2))
-        for u in range(2):
-            take_rest(2, cols(u, 1))
-
-        span_bc = cols(HALF, HALF)
-        east_a = [keep.tile([P, HALF], F32, name="east_a%d" % t, tag="east_a%d" % t, align_bytes=64) for t in range(PACK)]
-        east_bc = [keep.tile([P, HALF], F32, name="east_bc%d" % t) for t in range(LAST)]
-        east_b = [tile[:, block_cols(0)] for tile in east_bc] + [keep.tile([P, P], F32, name="east_b")[:]]
-        east_c = [tile[:, block_cols(1)] for tile in east_bc]
-        lap_a = [keep.tile([P, HALF], F32, name="lap_a%d" % t) for t in range(PACK)]
-        lap_b = [keep.tile([P, P], F32, name="lap_b%d" % t) for t in (0, 1)]
-        lap_b.append(shared.tile([P, P], F32, name="lap_b2", offset=1024, align_bytes=64))
-
-        def turn_lap(pair_bank, t, blocks):
-            for n, b in enumerate(blocks):
-                lap = lap_b[t][:] if b == 2 else lap_a[t][:, block_cols(b)]
-                turn_into(pair_bank[:, n, t % 2, :], lap, True, True)
-                lap_turned[b, t // 2] = pair_bank[:, n]
-
-        for t in range(PACK):
-            gather(east_a[t][:], t, east_sb, span_a, m2y[:, t, span_a])
-            if t < LAST:
-                gather(east_bc[t][:], t, east_sb, span_bc, m2y[:, t, span_bc])
+            first_product_turned(b, 5 + b)
+        for n, ((t, span, index), y_bank) in enumerate(zip(parts, banks)):
+            if n in (0, 3):
+                nc.scalar.copy(y[t][:, span], y_bank[:])
             else:
-                gather(east_b[t], t, east_sb, span_b, m2y[:, t, span_b])
-            gather(lap_a[t][:], t, west_sb, span_a, east_a[t][:])
-            if t < 2:
-                gather(lap_b[t][:], t, west_sb, span_b, east_b[t])
-        gather(lap_b[2][:], 2, west_sb, span_b, east_b[2])
-        pair_banks = {}
-        for u, blocks, index in ((0, (0, 1), 4), (0, (2,), 5), (1, (0, 1), 6), (1, (2,), 7)):
-            pair_banks[u, blocks] = bank(index, [P, len(blocks), 2, P], "lap_turned%d_%d" % (blocks[0], u))
-            for t in range(2 * u, min(2 * u + 2, LAST if blocks == (2,) else PACK)):
-                turn_lap(pair_banks[u, blocks], t, blocks)
-
+                nc.vector.tensor_copy(y[t][:, span], y_bank[:])
+        for b in range(BLOCKS):
+            sum_turned[b] = bank(1 + b, [P, PACK, P], "sum_turned%d" % b)
+        for t in range(PACK):
+            neighbours(t, 0, True)
+        turn_y(2, 7)
+        turn_y(LAST, 0)
         for b in (0, 1):
-            z_turned[b] = keep.tile([P, 2, P, 2], BF16, name="z_turned%d" % b, align_bytes=64)
+            take_own_term(b)
         for b in (0, 1):
-            combine(b, 0)
+            combine(b, 5 + b)
         for b in (0, 1):
-            combine(b, 1)
-            turn_back(b, 1 - b)
-
-        rest_last = keep.tile([P, PACK, P], F32, name="rest_last", tag="east_a%d" % LAST, align_bytes=64)
-        nc.gpsimd.tensor_tensor(rest_last[:], prev_half[1][:, :, block_cols(1)], m2y[:, :, span_c], ADD)
-
-        lap_b.append(shared.tile([P, P], F32, name="lap_b3", offset=32768, align_bytes=64))
-        gather(lap_b[LAST][:], LAST, west_sb, span_b, east_b[LAST])
-        turn_lap(pair_banks[1, (2,)], LAST, (2,))
-        z_turned[2] = shared.tile([P, 2, P, 2], BF16, name="z_turned2", offset=32768 + 512, align_bytes=64)
-        combine(2, 0)
-        east_c.append(shared.tile([P, P], F32, name="east_c", offset=32768 + 2048, align_bytes=64)[:])
-        gather(east_c[LAST], LAST, east_sb, span_c, m2y[:, LAST, span_c])
-        lap_c = [
-            keep.tile([P, planes, P], F32, name="lap_c%d" % planes, tag=tag, align_bytes=64)
-            for planes, tag in ((1, "rest2_0"), (LAST, "z_grouped0"))
-        ]
-        gather(lap_c[0][:, 0, :], 0, west_sb, span_c, east_c[0])
-        combine(2, 1)
-        turn_back(2, 7)
-        second_product(0, 2)
-        second_product(1, 3)
-        for t in range(1, PACK):
-            gather(lap_c[1][:, t - 1, :], t, west_sb, span_c, east_c[t])
-        scaled = keep.tile([P, PACK, P], F32, name="scaled", tag="z_grouped1", align_bytes=64)
-        nc.vector.tensor_tensor(scaled[:, 0], lap_c[0][:, 0], c_last[:], MULT)
-        nc.vector.tensor_tensor(scaled[:, 1:PACK], lap_c[1][:], c_last[:].unsqueeze(1).to_broadcast([P, LAST, P]), MULT)
-        second_product(2, 4, tag="rest2_0")
-        z_grouped[LAST] = keep.tile([P, P * PACK], BF16, name="z_grouped%d" % LAST, align_bytes=64)
-        nc.vector.tensor_tensor(
-            z_grouped[LAST][:].rearrange("p (g i t) -> p g t i", i=2, t=PACK),
-            scaled[:].rearrange("p t (g i) -> p g t i", i=2),
-            rest_last[:].rearrange("p t (g i) -> p g t i", i=2),
-            SUB,
-        )
-        first_grouped = keep.tile([P, P * PACK], BF16, name="first_grouped", tag="z_grouped2", align_bytes=64)
-        round_out(0, first_grouped[:])
-        second_product(LAST, 5, 6, 0, 1)
-        hand_on(cols(0, 1), first_grouped[:])
-        late_grouped = keep.tile([P, LAST, P * PACK], BF16, name="late_grouped", tag="east_a%d" % LAST, align_bytes=64)
-        for b in (1, 2):
-            round_out(b, late_grouped[:, b - 1, :])
-            hand_on(cols(b, 1), late_grouped[:, b - 1, :])
-        nc.sync.dma_start(out_word_rows[:, 0:AB], out_words[:, 0:AB].bitcast(I32))
-        round_out(LAST, late_grouped[:, 2, :])
-        hand_on(cols(LAST, 1), late_grouped[:, 2, :])
-        nc.sync.dma_start(out_word_rows[:, span_c], out_words[:, span_c].bitcast(I32))
+            finish_z(b)
+        for t in range(PACK):
+            neighbours(t, 1, t < 2)
+        for b in (2, LAST):
+            take_own_term(b)
+        for b in (0, 1):
+            second_product(b, 1 + b)
+        for b in (2, LAST):
+            combine(b, (5 + b) % 8)
+        for b in (0, 1):
+            round_out(b)
+        for b in (0, 1):
+            hand_on(b)
+        nc.sync.dma_start(out_word_rows[:, halves[0]], out_words[:, halves[0]].bitcast(I32))
+        for b in (2, LAST):
+            finish_z(b)
+        for b in (2, LAST):
+            second_product(b, 1 + b)
+        for b in (2, LAST):
+            round_out(b)
+        for b in (2, LAST):
+            hand_on(b)
+        nc.sync.dma_start(out_word_rows[:, halves[1]], out_words[:, halves[1]].bitcast(I32))
 
         for q in range(P // QUAD):
             queue = nc.scalar if q % 2 else nc.sync

@@ -107,6 +107,10 @@ def tile_picked_waveeq_none_po_kernel(
             nc.sync.dma_start(c_col[:], c2[0].rearrange("(b p) -> p b", p=P))
         d_col = keep.tile([P, BLOCKS], F32, name="d_col")
         nc.gpsimd.tensor_scalar(d_col[:], c_col[:], -2.0, 2.0, MULT, ADD)
+        c_last = shared.tile([P, P], F32, name="c_last", offset=7680, align_bytes=64)
+        nc.sync.dma_start(c_last[:], c2[:, block_cols(LAST)])
+        d_last = keep.tile([P, P], F32, name="d_last")
+        nc.gpsimd.tensor_scalar(d_last[:], c_last[:], -2.0, 2.0, MULT, ADD)
         prev_rows = prev.rearrange("(p t) j -> p t j", t=PACK)
         prev_half = []
         for h in range(2):
@@ -141,6 +145,8 @@ def tile_picked_waveeq_none_po_kernel(
         out_rows = out_0.rearrange("(p t) j -> p t j", t=PACK)
         out_word_rows = out_1[0].rearrange("p n t -> p (n t)").bitcast(I32)
         y_turned, sum_turned, own_term, z_bank, z_grouped, out_sb, out_grouped = {}, {}, {}, {}, {}, {}, {}
+        east_vals, out_bank = {}, {}
+        HOLD = "east3_0"
 
         def product(dst, lhs, lhs_scale, rhs, rhs_scale):
             nc.tensor.matmul_mx(
@@ -176,20 +182,27 @@ def tile_picked_waveeq_none_po_kernel(
         def looked_up(t, lists_sb, span):
             return y[t][:].indirect(lists_sb[:, list_cols(span)])
 
-        def neighbours(t, half, west_on_vector):
-            span = cols(HALF * half, HALF)
-            east_vals = keep.tile([P, HALF], F32, name="east%d_%d" % (t, half))
-            nc.scalar.activation(east_vals[:], looked_up(t, east_sb, span), COPY)
-            second = keep.tile([P, HALF], F32, name="west%d_%d" % (t, half))
-            if west_on_vector:
-                nc.vector.tensor_tensor(second[:], looked_up(t, west_sb, span), east_vals[:], ADD)
-                terms = [second]
-            else:
-                nc.scalar.activation(second[:], looked_up(t, west_sb, span), COPY)
-                terms = [east_vals, second]
-            for n in range(2):
-                for k, term in enumerate(terms):
-                    turn_into(sum_turned[2 * half + n][:, t, :], term[:, block_cols(n)], k == 0, k == len(terms) - 1)
+        def gather_east(t, half):
+            tag = "east%d_%d" % (t, half)
+            east_vals[t, half] = keep.tile([P, PACK, P] if tag == HOLD else [P, HALF], F32, name=tag, tag=tag)
+            nc.scalar.activation(east_of(t, cols(HALF * half, HALF)), looked_up(t, east_sb, cols(HALF * half, HALF)), COPY)
+
+        def east_of(t, span):
+            tile = east_vals[t, span.start // HALF]
+            flat = tile[:].rearrange("p a j -> p (a j)") if len(tile.shape) == 3 else tile[:]
+            return flat[:, cols(span.start % HALF, span.stop - span.start)]
+
+        def west_added(t, span, dst):
+            nc.vector.tensor_tensor(dst, looked_up(t, west_sb, span), east_of(t, span), ADD)
+
+        def turn_sum(b, t, terms):
+            for k, term in enumerate(terms):
+                turn_into(sum_turned[b][:, t, :], term, k == 0, k == len(terms) - 1)
+
+        def west_on_scalar(t, b):
+            tile = keep.tile([P, P], F32, name="west%d_%d" % (t, b))
+            nc.scalar.activation(tile[:], looked_up(t, west_sb, block_cols(b)), COPY)
+            turn_sum(b, t, [east_of(t, block_cols(b)), tile[:]])
 
         def take_own_term(b):
             own_term[b] = keep.tile([P, PACK, P], F32, name="own_term%d" % b)
@@ -215,11 +228,13 @@ def tile_picked_waveeq_none_po_kernel(
             z_codes = keep.tile([P, P], U32, name="z_codes%d" % b, align_bytes=64)
             z_scales = keep.tile([P, P], U8, name="z_scales%d" % b, align_bytes=64)
             nc.vector.quantize_mx(out=z_codes[:].bitcast(FP8X4), scales=z_scales[:], in_=z_grouped[b][:])
-            out_bank = bank(index, [P, PACK, P], "out_bank%d" % b)
+            out_bank[b] = bank(index, [P, PACK, P], "out_bank%d" % b)
             for t in range(PACK):
-                product(out_bank[:, t, :], w2_codes[:, t, :], w2_plane[:, t, :], z_codes[:], z_scales[:])
+                product(out_bank[b][:, t, :], w2_codes[:, t, :], w2_plane[:, t, :], z_codes[:], z_scales[:])
+
+        def take_out(b):
             out_sb[b] = keep.tile([P, PACK, P], F32, name="out_sb%d" % b)
-            nc.scalar.copy(out_sb[b][:], out_bank[:])
+            nc.scalar.copy(out_sb[b][:], out_bank[b][:])
             queue = nc.scalar if b == LAST else nc.sync
             queue.dma_start(out_rows[:, :, block_cols(b)], out_sb[b][:])
 
@@ -228,6 +243,12 @@ def tile_picked_waveeq_none_po_kernel(
             nc.vector.tensor_copy(
                 out_grouped[b][:].rearrange("p (g i t) -> p g t i", i=2, t=PACK),
                 out_sb[b][:].rearrange("p t (g i) -> p g t i", i=2),
+            )
+
+        def round_out_of_bank(b):
+            out_grouped[b] = keep.tile([P, P * PACK], BF16, name="out_grouped%d" % b, align_bytes=64)
+            nc.scalar.copy(
+                out_grouped[b][:].rearrange("p (j t) -> p j t", t=PACK), out_bank[b][:].rearrange("p t j -> p j t")
             )
 
         def hand_on(b):
@@ -244,38 +265,61 @@ def tile_picked_waveeq_none_po_kernel(
                 nc.scalar.copy(y[t][:, span], y_bank[:])
             else:
                 nc.vector.tensor_copy(y[t][:, span], y_bank[:])
-        for b in range(BLOCKS):
-            sum_turned[b] = bank(1 + b, [P, PACK, P], "sum_turned%d" % b)
+        for b in range(LAST):
+            sum_turned[b] = bank(b, [P, PACK, P], "sum_turned%d" % b)
         for t in range(PACK):
-            neighbours(t, 0, True)
+            gather_east(t, 0)
+            both = keep.tile([P, HALF], F32, name="both%d" % t)
+            west_added(t, halves[0], both[:])
+            for b in (0, 1):
+                turn_sum(b, t, [both[:, block_cols(b)]])
         turn_y(2, 7)
-        turn_y(LAST, 0)
         for b in (0, 1):
             take_own_term(b)
+        own_last = keep.tile([P, PACK, P], F32, name="own_last")
+        for t in range(PACK):
+            nc.vector.tensor_tensor(own_last[:, t, :], y[t][:, block_cols(LAST)], d_last[:], MULT)
         for b in (0, 1):
             combine(b, 5 + b)
-        for b in (0, 1):
-            finish_z(b)
+        rest_last = keep.tile([P, PACK, P], F32, name="rest_last", tag=HOLD)
+        nc.gpsimd.tensor_tensor(rest_last[:], own_last[:], prev_half[1][:, :, block_cols(1)], SUB)
         for t in range(PACK):
-            neighbours(t, 1, t < 2)
-        for b in (2, LAST):
-            take_own_term(b)
+            gather_east(t, 1)
+        sum_last = keep.tile([P, PACK, P], F32, name="sum_last")
+        both_two = keep.tile([P, P], F32, name="both_two")
+        finish_z(0)
+        west_added(0, block_cols(2), both_two[:])
+        turn_sum(2, 0, [both_two[:]])
+        finish_z(1)
+        for t in range(1, PACK):
+            west_on_scalar(t, 2)
+        take_own_term(2)
         for b in (0, 1):
-            second_product(b, 1 + b)
-        for b in (2, LAST):
-            combine(b, (5 + b) % 8)
+            second_product(b, 3 + b)
+        for t in range(PACK):
+            west_added(t, block_cols(LAST), sum_last[:, t, :])
+        combine(2, 7)
+        scaled = keep.tile([P, PACK, P], F32, name="scaled")
+        nc.vector.tensor_tensor(scaled[:], sum_last[:], c_last[:].unsqueeze(1).to_broadcast([P, PACK, P]), MULT)
+        finish_z(2)
+        z_grouped[LAST] = keep.tile([P, P * PACK], BF16, name="z_grouped%d" % LAST, align_bytes=64)
+        nc.vector.tensor_tensor(
+            z_grouped[LAST][:].rearrange("p (g i t) -> p g t i", i=2, t=PACK),
+            scaled[:].rearrange("p t (g i) -> p g t i", i=2),
+            rest_last[:].rearrange("p t (g i) -> p g t i", i=2),
+            ADD,
+        )
+        second_product(2, 0)
+        second_product(LAST, 1)
         for b in (0, 1):
-            round_out(b)
+            take_out(b)
         for b in (0, 1):
+            round_out_of_bank(b)
             hand_on(b)
         nc.sync.dma_start(out_word_rows[:, halves[0]], out_words[:, halves[0]].bitcast(I32))
         for b in (2, LAST):
-            finish_z(b)
-        for b in (2, LAST):
-            second_product(b, 1 + b)
-        for b in (2, LAST):
+            take_out(b)
             round_out(b)
-        for b in (2, LAST):
             hand_on(b)
         nc.sync.dma_start(out_word_rows[:, halves[1]], out_words[:, halves[1]].bitcast(I32))
 

@@ -102,11 +102,14 @@ def tile_picked_waveeq_none_po_kernel(
 
         w2_raw = shared.tile([P, N], I32, name="w2_raw", offset=16384, align_bytes=64)
         nc.scalar.dma_start(w2_raw[:], w2_words[0].rearrange("p n t -> p (n t)").bitcast(I32))
-        c_col = shared.tile([P, BLOCKS], F32, name="c_col", offset=8192, align_bytes=64)
+        c_col = shared.tile([P, LAST], F32, name="c_col", offset=8192, align_bytes=64)
         with nc.allow_non_contiguous_dma(reason="one value of c2 for each partition and block"):
-            nc.sync.dma_start(c_col[:], c2[0].rearrange("(b p) -> p b", p=P))
-        d_col = keep.tile([P, BLOCKS], F32, name="d_col")
-        nc.gpsimd.tensor_scalar(d_col[:], c_col[:], -2.0, 2.0, MULT, ADD)
+            nc.sync.dma_start(c_col[:], c2[0, 0 : LAST * P].rearrange("(b p) -> p b", p=P))
+        d_first = shared.tile([P, 1], F32, name="d_first", offset=32768, align_bytes=64)
+        d_next = keep.tile([P, 2], F32, name="d_next")
+        nc.gpsimd.tensor_scalar(d_first[:], c_col[:, 0:1], -2.0, 2.0, MULT, ADD)
+        nc.gpsimd.tensor_scalar(d_next[:], c_col[:, 1:LAST], -2.0, 2.0, MULT, ADD)
+        d_col = [d_first[:], d_next[:, 0:1], d_next[:, 1:2]]
         c_last = shared.tile([P, P], F32, name="c_last", offset=7680, align_bytes=64)
         nc.sync.dma_start(c_last[:], c2[:, block_cols(LAST)])
         d_last = keep.tile([P, P], F32, name="d_last")
@@ -146,7 +149,6 @@ def tile_picked_waveeq_none_po_kernel(
         out_word_rows = out_1[0].rearrange("p n t -> p (n t)").bitcast(I32)
         y_turned, sum_turned, own_term, z_bank, z_grouped, out_sb, out_grouped = {}, {}, {}, {}, {}, {}, {}
         east_vals, out_bank = {}, {}
-        HOLD = "east3_0"
 
         def product(dst, lhs, lhs_scale, rhs, rhs_scale):
             nc.tensor.matmul_mx(
@@ -184,13 +186,11 @@ def tile_picked_waveeq_none_po_kernel(
 
         def gather_east(t, half):
             tag = "east%d_%d" % (t, half)
-            east_vals[t, half] = keep.tile([P, PACK, P] if tag == HOLD else [P, HALF], F32, name=tag, tag=tag)
+            east_vals[t, half] = keep.tile([P, HALF], F32, name=tag)
             nc.scalar.activation(east_of(t, cols(HALF * half, HALF)), looked_up(t, east_sb, cols(HALF * half, HALF)), COPY)
 
         def east_of(t, span):
-            tile = east_vals[t, span.start // HALF]
-            flat = tile[:].rearrange("p a j -> p (a j)") if len(tile.shape) == 3 else tile[:]
-            return flat[:, cols(span.start % HALF, span.stop - span.start)]
+            return east_vals[t, span.start // HALF][:, cols(span.start % HALF, span.stop - span.start)]
 
         def west_added(t, span, dst):
             nc.vector.tensor_tensor(dst, looked_up(t, west_sb, span), east_of(t, span), ADD)
@@ -205,11 +205,11 @@ def tile_picked_waveeq_none_po_kernel(
             turn_sum(b, t, [east_of(t, block_cols(b)), tile[:]])
 
         def take_own_term(b):
-            own_term[b] = keep.tile([P, PACK, P], F32, name="own_term%d" % b)
-            nc.scalar.activation(own_term[b][:], y_turned[b][:], COPY, scale=d_col[:, b : b + 1])
+            own_term[b] = keep.tile([P, PACK, P], F32, name="own_term%d" % b, tag="own_term%d" % b)
+            nc.scalar.activation(own_term[b][:], y_turned[b][:], COPY, scale=d_col[b])
 
         def combine(b, index):
-            turned = keep.tile([P, PACK, P], F32, name="combined%d" % b)
+            turned = keep.tile([P, PACK, P], F32, name="combined%d" % b, tag="combined%d" % b)
             nc.vector.scalar_tensor_tensor(turned[:], sum_turned[b][:], c_col[:, b : b + 1], own_term[b][:], MULT, ADD)
             z_bank[b] = bank(index, [P, PACK, P], "z_bank%d" % b)
             for t in range(PACK):
@@ -224,18 +224,21 @@ def tile_picked_waveeq_none_po_kernel(
                 SUB,
             )
 
-        def second_product(b, index):
+        def second_product(b, *indices):
             z_codes = keep.tile([P, P], U32, name="z_codes%d" % b, align_bytes=64)
             z_scales = keep.tile([P, P], U8, name="z_scales%d" % b, align_bytes=64)
             nc.vector.quantize_mx(out=z_codes[:].bitcast(FP8X4), scales=z_scales[:], in_=z_grouped[b][:])
-            out_bank[b] = bank(index, [P, PACK, P], "out_bank%d" % b)
+            step = PACK // len(indices)
+            out_bank[b] = [bank(index, [P, step, P], "out_bank%d_%d" % (b, index)) for index in indices]
             for t in range(PACK):
-                product(out_bank[b][:, t, :], w2_codes[:, t, :], w2_plane[:, t, :], z_codes[:], z_scales[:])
+                product(out_bank[b][t // step][:, t % step, :], w2_codes[:, t, :], w2_plane[:, t, :], z_codes[:], z_scales[:])
 
         def take_out(b):
             out_sb[b] = keep.tile([P, PACK, P], F32, name="out_sb%d" % b)
-            nc.scalar.copy(out_sb[b][:], out_bank[b][:])
-            queue = nc.scalar if b == LAST else nc.sync
+            step = PACK // len(out_bank[b])
+            for n, part in enumerate(out_bank[b]):
+                nc.scalar.copy(out_sb[b][:, cols(step * n, step), :], part[:])
+            queue = nc.scalar if b == 2 else nc.sync
             queue.dma_start(out_rows[:, :, block_cols(b)], out_sb[b][:])
 
         def round_out(b):
@@ -248,7 +251,7 @@ def tile_picked_waveeq_none_po_kernel(
         def round_out_of_bank(b):
             out_grouped[b] = keep.tile([P, P * PACK], BF16, name="out_grouped%d" % b, align_bytes=64)
             nc.scalar.copy(
-                out_grouped[b][:].rearrange("p (j t) -> p j t", t=PACK), out_bank[b][:].rearrange("p t j -> p j t")
+                out_grouped[b][:].rearrange("p (j t) -> p j t", t=PACK), out_bank[b][0][:].rearrange("p t j -> p j t")
             )
 
         def hand_on(b):
@@ -265,7 +268,7 @@ def tile_picked_waveeq_none_po_kernel(
                 nc.scalar.copy(y[t][:, span], y_bank[:])
             else:
                 nc.vector.tensor_copy(y[t][:, span], y_bank[:])
-        for b in range(LAST):
+        for b in (0, 1):
             sum_turned[b] = bank(b, [P, PACK, P], "sum_turned%d" % b)
         for t in range(PACK):
             gather_east(t, 0)
@@ -281,27 +284,27 @@ def tile_picked_waveeq_none_po_kernel(
             nc.vector.tensor_tensor(own_last[:, t, :], y[t][:, block_cols(LAST)], d_last[:], MULT)
         for b in (0, 1):
             combine(b, 5 + b)
-        rest_last = keep.tile([P, PACK, P], F32, name="rest_last", tag=HOLD)
+        rest_last = shared.tile([P, PACK, P], F32, name="rest_last", offset=32768, align_bytes=64)
         nc.gpsimd.tensor_tensor(rest_last[:], own_last[:], prev_half[1][:, :, block_cols(1)], SUB)
         for t in range(PACK):
             gather_east(t, 1)
-        sum_last = keep.tile([P, PACK, P], F32, name="sum_last")
-        both_two = keep.tile([P, P], F32, name="both_two")
+        sum_early = keep.tile([P, LAST, P], F32, name="sum_early", tag="own_term0")
+        for t in range(LAST):
+            west_added(t, block_cols(LAST), sum_early[:, t, :])
+        scaled = keep.tile([P, PACK, P], F32, name="scaled")
+        nc.gpsimd.tensor_tensor(scaled[:, 0:LAST], sum_early[:], c_last[:].unsqueeze(1).to_broadcast([P, LAST, P]), MULT)
         finish_z(0)
-        west_added(0, block_cols(2), both_two[:])
-        turn_sum(2, 0, [both_two[:]])
+        sum_turned[2] = bank(5, [P, PACK, P], "sum_turned2")
         finish_z(1)
-        for t in range(1, PACK):
+        for t in range(PACK):
             west_on_scalar(t, 2)
         take_own_term(2)
-        for b in (0, 1):
-            second_product(b, 3 + b)
-        for t in range(PACK):
-            west_added(t, block_cols(LAST), sum_last[:, t, :])
+        second_product(0, 3)
+        sum_late = shared.tile([P, P], F32, name="sum_late", offset=1024, align_bytes=64)
+        west_added(LAST, block_cols(LAST), sum_late[:])
+        second_product(1, 4)
+        nc.vector.tensor_tensor(scaled[:, LAST], sum_late[:], c_last[:], MULT)
         combine(2, 7)
-        scaled = keep.tile([P, PACK, P], F32, name="scaled")
-        nc.vector.tensor_tensor(scaled[:], sum_last[:], c_last[:].unsqueeze(1).to_broadcast([P, PACK, P]), MULT)
-        finish_z(2)
         z_grouped[LAST] = keep.tile([P, P * PACK], BF16, name="z_grouped%d" % LAST, align_bytes=64)
         nc.vector.tensor_tensor(
             z_grouped[LAST][:].rearrange("p (g i t) -> p g t i", i=2, t=PACK),
@@ -309,19 +312,20 @@ def tile_picked_waveeq_none_po_kernel(
             rest_last[:].rearrange("p t (g i) -> p g t i", i=2),
             ADD,
         )
-        second_product(2, 0)
-        second_product(LAST, 1)
         for b in (0, 1):
             take_out(b)
-        for b in (0, 1):
             round_out_of_bank(b)
-            hand_on(b)
+        hand_on(0)
+        second_product(LAST, 0)
+        finish_z(2)
+        hand_on(1)
+        second_product(2, 1, 2)
         nc.sync.dma_start(out_word_rows[:, halves[0]], out_words[:, halves[0]].bitcast(I32))
-        for b in (2, LAST):
+        for b in (LAST, 2):
             take_out(b)
             round_out(b)
             hand_on(b)
-        nc.sync.dma_start(out_word_rows[:, halves[1]], out_words[:, halves[1]].bitcast(I32))
+            nc.sync.dma_start(out_word_rows[:, block_cols(b)], out_words[:, block_cols(b)].bitcast(I32))
 
         for q in range(P // QUAD):
             queue = nc.scalar if q % 2 else nc.sync

@@ -102,14 +102,8 @@ def tile_picked_waveeq_none_po_kernel(
 
         w2_raw = shared.tile([P, N], I32, name="w2_raw", offset=16384, align_bytes=64)
         nc.scalar.dma_start(w2_raw[:], w2_words[0].rearrange("p n t -> p (n t)").bitcast(I32))
-        c_col = shared.tile([P, LAST], F32, name="c_col", offset=8192, align_bytes=64)
-        with nc.allow_non_contiguous_dma(reason="one value of c2 for each partition and block"):
-            nc.sync.dma_start(c_col[:], c2[0, 0 : LAST * P].rearrange("(b p) -> p b", p=P))
-        d_first = shared.tile([P, 1], F32, name="d_first", offset=32768, align_bytes=64)
-        d_next = keep.tile([P, 2], F32, name="d_next")
-        nc.gpsimd.tensor_scalar(d_first[:], c_col[:, 0:1], -2.0, 2.0, MULT, ADD)
-        nc.gpsimd.tensor_scalar(d_next[:], c_col[:, 1:LAST], -2.0, 2.0, MULT, ADD)
-        d_col = [d_first[:], d_next[:, 0:1], d_next[:, 1:2]]
+        c_rows = shared.tile([P, P], F32, name="c_rows", offset=8192, align_bytes=64)
+        nc.sync.dma_start(c_rows[:], c2.rearrange("r (b j) -> (r b) j", j=P)[0:P, :])
         c_last = shared.tile([P, P], F32, name="c_last", offset=7680, align_bytes=64)
         nc.sync.dma_start(c_last[:], c2[:, block_cols(LAST)])
         d_last = keep.tile([P, P], F32, name="d_last")
@@ -186,7 +180,7 @@ def tile_picked_waveeq_none_po_kernel(
 
         def gather_east(t, half):
             tag = "east%d_%d" % (t, half)
-            east_vals[t, half] = keep.tile([P, HALF], F32, name=tag)
+            east_vals[t, half] = keep.tile([P, HALF], F32, name=tag, tag=tag)
             nc.scalar.activation(east_of(t, cols(HALF * half, HALF)), looked_up(t, east_sb, cols(HALF * half, HALF)), COPY)
 
         def east_of(t, span):
@@ -206,7 +200,7 @@ def tile_picked_waveeq_none_po_kernel(
 
         def take_own_term(b):
             own_term[b] = keep.tile([P, PACK, P], F32, name="own_term%d" % b, tag="own_term%d" % b)
-            nc.scalar.activation(own_term[b][:], y_turned[b][:], COPY, scale=d_col[b])
+            nc.scalar.activation(own_term[b][:], y_turned[b][:], COPY, scale=d_col[:, b : b + 1])
 
         def combine(b, index):
             turned = keep.tile([P, PACK, P], F32, name="combined%d" % b, tag="combined%d" % b)
@@ -263,28 +257,36 @@ def tile_picked_waveeq_none_po_kernel(
         banks = [first_product(*part) for part in parts]
         for b in (0, 1):
             first_product_turned(b, 5 + b)
+        c_bank = bank(7, [P, P], "c_bank")
+        nc.tensor.transpose(c_bank[:], c_rows[:], ident[:])
+        c_col = keep.tile([P, LAST], F32, name="c_col")
+        d_col = keep.tile([P, LAST], F32, name="d_col")
         for n, ((t, span, index), y_bank) in enumerate(zip(parts, banks)):
             if n in (0, 3):
                 nc.scalar.copy(y[t][:, span], y_bank[:])
             else:
                 nc.vector.tensor_copy(y[t][:, span], y_bank[:])
+        nc.vector.tensor_copy(c_col[:], c_bank[:, 0:LAST])
+        nc.vector.tensor_scalar(d_col[:], c_bank[:, 0:LAST], -2.0, 2.0, MULT, ADD)
         for b in (0, 1):
             sum_turned[b] = bank(b, [P, PACK, P], "sum_turned%d" % b)
         for t in range(PACK):
             gather_east(t, 0)
             both = keep.tile([P, HALF], F32, name="both%d" % t)
-            west_added(t, halves[0], both[:])
+            nc.vector.tensor_copy(both[:], looked_up(t, west_sb, halves[0]))
             for b in (0, 1):
-                turn_sum(b, t, [both[:, block_cols(b)]])
+                turn_sum(b, t, [both[:, block_cols(b)], east_of(t, block_cols(b))])
         turn_y(2, 7)
         for b in (0, 1):
             take_own_term(b)
         own_last = keep.tile([P, PACK, P], F32, name="own_last")
         for t in range(PACK):
             nc.vector.tensor_tensor(own_last[:, t, :], y[t][:, block_cols(LAST)], d_last[:], MULT)
+        west_first = keep.tile([P, P], F32, name="west_first")
+        nc.vector.tensor_copy(west_first[:], looked_up(0, west_sb, block_cols(2)))
         for b in (0, 1):
             combine(b, 5 + b)
-        rest_last = shared.tile([P, PACK, P], F32, name="rest_last", offset=32768, align_bytes=64)
+        rest_last = keep.tile([P, PACK, P], F32, name="rest_last")
         nc.gpsimd.tensor_tensor(rest_last[:], own_last[:], prev_half[1][:, :, block_cols(1)], SUB)
         for t in range(PACK):
             gather_east(t, 1)
@@ -296,7 +298,8 @@ def tile_picked_waveeq_none_po_kernel(
         finish_z(0)
         sum_turned[2] = bank(5, [P, PACK, P], "sum_turned2")
         finish_z(1)
-        for t in range(PACK):
+        turn_sum(2, 0, [east_of(0, block_cols(2)), west_first[:]])
+        for t in range(1, PACK):
             west_on_scalar(t, 2)
         take_own_term(2)
         second_product(0, 3)

@@ -179,9 +179,13 @@ def tile_picked_waveeq_none_po_kernel(
             return y[t][:].indirect(lists_sb[:, list_cols(span)])
 
         def gather_east(t, half):
-            tag = "east%d_%d" % (t, half)
+            tag = "both%d" % t if half and t < 2 else "east%d_%d" % (t, half)
             east_vals[t, half] = keep.tile([P, HALF], F32, name=tag, tag=tag)
-            nc.scalar.activation(east_of(t, cols(HALF * half, HALF)), looked_up(t, east_sb, cols(HALF * half, HALF)), COPY)
+            span = cols(HALF * half, HALF)
+            if (t, half) == (2, 1):
+                nc.vector.tensor_copy(east_of(t, span), looked_up(t, east_sb, span))
+            else:
+                nc.scalar.activation(east_of(t, span), looked_up(t, east_sb, span), COPY)
 
         def east_of(t, span):
             return east_vals[t, span.start // HALF][:, cols(span.start % HALF, span.stop - span.start)]
@@ -272,7 +276,7 @@ def tile_picked_waveeq_none_po_kernel(
             sum_turned[b] = bank(b, [P, PACK, P], "sum_turned%d" % b)
         for t in range(PACK):
             gather_east(t, 0)
-            both = keep.tile([P, HALF], F32, name="both%d" % t)
+            both = keep.tile([P, HALF], F32, name="both%d" % t, tag="both%d" % t)
             nc.vector.tensor_copy(both[:], looked_up(t, west_sb, halves[0]))
             for b in (0, 1):
                 turn_sum(b, t, [both[:, block_cols(b)], east_of(t, block_cols(b))])
@@ -281,25 +285,23 @@ def tile_picked_waveeq_none_po_kernel(
             take_own_term(b)
         own_last = keep.tile([P, PACK, P], F32, name="own_last")
         for t in range(PACK):
-            nc.vector.tensor_tensor(own_last[:, t, :], y[t][:, block_cols(LAST)], d_last[:], MULT)
-        west_first = keep.tile([P, P], F32, name="west_first")
-        nc.vector.tensor_copy(west_first[:], looked_up(0, west_sb, block_cols(2)))
+            nc.gpsimd.tensor_tensor(own_last[:, t, :], y[t][:, block_cols(LAST)], d_last[:], MULT)
+        gather_east(2, 1)
         for b in (0, 1):
             combine(b, 5 + b)
         rest_last = keep.tile([P, PACK, P], F32, name="rest_last")
         nc.gpsimd.tensor_tensor(rest_last[:], own_last[:], prev_half[1][:, :, block_cols(1)], SUB)
-        for t in range(PACK):
+        for t in (0, 1, LAST):
             gather_east(t, 1)
         sum_early = keep.tile([P, LAST, P], F32, name="sum_early", tag="own_term0")
-        for t in range(LAST):
+        for t in (2, 0, 1):
             west_added(t, block_cols(LAST), sum_early[:, t, :])
         scaled = keep.tile([P, PACK, P], F32, name="scaled")
         nc.gpsimd.tensor_tensor(scaled[:, 0:LAST], sum_early[:], c_last[:].unsqueeze(1).to_broadcast([P, LAST, P]), MULT)
         finish_z(0)
         sum_turned[2] = bank(5, [P, PACK, P], "sum_turned2")
         finish_z(1)
-        turn_sum(2, 0, [east_of(0, block_cols(2)), west_first[:]])
-        for t in range(1, PACK):
+        for t in range(PACK):
             west_on_scalar(t, 2)
         take_own_term(2)
         second_product(0, 3)

@@ -131,7 +131,7 @@ def tile_picked_waveeq_none_po_kernel(
             w2s_dealt[:].rearrange("p t (g i) -> p g t i", i=16),
             w2s_raw[:].rearrange("p (g i t) -> p g t i", i=16, t=PACK),
         )
-        w2_plane = shared.tile([P, PACK, P], U8, name="w2_plane", offset=7168, align_bytes=64)
+        w2_plane = shared.tile([P, PACK, P], U8, name="w2_plane", offset=16384, align_bytes=64)
         nc.gpsimd.memset(w2_plane[:].bitcast(I32), 0)
         for a in range(PACK):
             nc.sync.dma_start(w2_plane[a:P:QUAD].bitcast(I32), w2s_dealt[SPREAD * a : P : QUAD].bitcast(I32))

from contextlib import ExitStack

import concourse.mybir as mybir
from concourse.masks import make_identity

K, T, S, H, N = 512, 2048, 512, 512, 512
FLOPS = 2 * K * H * S + 2 * H * N * S

F32 = mybir.dt.float32
BF16 = mybir.dt.bfloat16
I32 = mybir.dt.int32
U32 = mybir.dt.uint32
U16 = mybir.dt.uint16
U8 = mybir.dt.uint8
FP8X4 = mybir.dt.float8_e4m3fn_x4
COPY = mybir.ActivationFunctionType.Copy
MULT = mybir.AluOpType.mult
ADD = mybir.AluOpType.add
SUB = mybir.AluOpType.subtract

P = 128
PACK = 4
GROUP = 16
QUAD = 32
ROWS = 16
SPREAD = P // ROWS
BLOCKS = S // P
HALF = S // 2
W1_ON_VECTOR = 92
LAST = PACK - 1


def tile_picked_waveeq_none_po_kernel(
    tc, x_words, x_scales, w1, prev, c2, w2_words, w2_scales, offs, east, west, out_0, out_1, out_2
):
    nc = tc.nc
    with ExitStack() as ctx:
        lists = ctx.enter_context(tc.tile_pool(name="lists", bufs=1))
        keep = ctx.enter_context(tc.tile_pool(name="keep", bufs=1))
        shared = ctx.enter_context(tc.tile_pool(name="shared", bufs=1))
        psum = ctx.enter_context(tc.psum_pool(name="psum", bufs=1))

        def bank(index, shape, name):
            return psum.tile(shape, F32, name=name, tag="bank%d" % index)

        def cols(first, count):
            return slice(first, first + count)

        def block_cols(b):
            return cols(P * b, P)

        def list_cols(span):
            return slice(span.start // GROUP, span.stop // GROUP)

        offs_sb = lists.tile([P, S // GROUP], U16, name="offs_sb")
        east_sb = lists.tile([P, S // GROUP], U16, name="east_sb")
        west_sb = lists.tile([P, S // GROUP], U16, name="west_sb")
        xs_window = shared.tile([P, T], U8, name="xs_window", offset=26624, align_bytes=64)
        nc.gpsimd.memset(xs_window[:].bitcast(I32), 0)
        w2s_raw = keep.tile([P, N], U8, name="w2s_raw", align_bytes=64)
        nc.gpsimd.memset(w2s_raw[:].bitcast(I32), 0)
        w1_raw = shared.tile([P, PACK, H], F32, name="w1_raw", offset=16384, align_bytes=64)
        w1_rows = w1.rearrange("(p j) c -> p (j c)", j=PACK)
        w1_flat = w1_raw[:].rearrange("p j c -> p (j c)")
        nc.sync.dma_start(w1_flat[:, 0:768], w1_rows[:, 0:768])
        nc.sync.dma_start(offs_sb[:], offs)
        nc.sync.dma_start(east_sb[:], east)
        nc.sync.dma_start(xs_window[0:P:SPREAD].bitcast(I32), x_scales[0].bitcast(I32))
        nc.sync.dma_start(w2s_raw[0:P:SPREAD].bitcast(I32), w2_scales[0].bitcast(I32))
        nc.sync.dma_start(w1_flat[:, 768 : PACK * H], w1_rows[:, 768 : PACK * H])
        x_window = shared.tile([P, T], I32, name="x_window", offset=4096, align_bytes=64)
        nc.sync.dma_start(x_window[:], x_words[0].rearrange("p n t -> p (n t)").bitcast(I32))
        nc.sync.dma_start(west_sb[:], west)
        xs_plane = keep.tile([P, S], U8, name="xs_plane", align_bytes=64)
        nc.gpsimd.memset(xs_plane[:].bitcast(I32), 0)
        ident = keep.tile([P, P], F32, name="ident")
        make_identity(nc, ident[:])
        warm = keep.tile([P, 2], F32, name="warm")
        nc.vector.memset(warm[:, 0:1], 0.0)
        nc.scalar.copy(warm[:, 1:2], warm[:, 0:1])

        xs_picked = keep.tile([P, S], U8, name="xs_picked", align_bytes=64)
        nc.vector.tensor_copy(xs_picked[:], xs_window[:].indirect(offs_sb[:]))
        for a in range(PACK):
            queue = nc.scalar if a % 2 else nc.sync
            queue.dma_start(xs_plane[a:P:QUAD].bitcast(I32), xs_picked[SPREAD * a : P : QUAD].bitcast(I32))

        w1_grouped = shared.tile([P, PACK, P, PACK], BF16, name="w1_grouped", offset=27136, align_bytes=64)
        w1_dst = w1_grouped[:].rearrange("p t m j -> p m t j")
        w1_src = w1_raw[:].rearrange("p j (m t) -> p m t j", t=PACK)
        nc.vector.tensor_copy(w1_dst[:, 0:W1_ON_VECTOR], w1_src[:, 0:W1_ON_VECTOR])
        nc.scalar.copy(w1_dst[:, W1_ON_VECTOR:P], w1_src[:, W1_ON_VECTOR:P])
        w1_codes, w1_scales = {}, {}

        def quantise_w1(u, codes):
            w1_codes[u] = codes
            w1_scales[u] = keep.tile([P, HALF], U8, name="w1_scales%d" % u, align_bytes=64)
            pair = w1_grouped[:, cols(2 * u, 2)].rearrange("p t m j -> p (t m j)")
            nc.vector.quantize_mx(out=codes[:].bitcast(FP8X4), scales=w1_scales[u][:], in_=pair)

        quantise_w1(0, keep.tile([P, HALF], U32, name="w1_codes0", align_bytes=64))

        w2_raw = shared.tile([P, N], I32, name="w2_raw", offset=16384, align_bytes=64)
        nc.scalar.dma_start(w2_raw[:], w2_words[0].rearrange("p n t -> p (n t)").bitcast(I32))
        c_rows = shared.tile([P, P], F32, name="c_rows", offset=8192, align_bytes=64)
        nc.sync.dma_start(c_rows[:], c2.rearrange("r (b j) -> (r b) j", j=P)[0:P, :])
        c_last = shared.tile([P, P], F32, name="c_last", offset=7680, align_bytes=64)
        nc.sync.dma_start(c_last[:], c2[:, block_cols(LAST)])
        d_last = keep.tile([P, P], F32, name="d_last")
        nc.gpsimd.tensor_scalar(d_last[:], c_last[:], -2.0, 2.0, MULT, ADD)
        prev_rows = prev.rearrange("(p t) j -> p t j", t=PACK)
        prev_half = []
        for h in range(2):
            tile = shared.tile([P, PACK, HALF], F32, name="prev%d" % h, offset=1024 + 10240 * h, align_bytes=64)
            nc.sync.dma_start(tile[:], prev_rows[:, :, cols(HALF * h, HALF)])
            prev_half.append(tile)

        x_picked = shared.tile([P, S], U32, name="x_picked", offset=24576, align_bytes=64)
        for h in range(2):
            span = cols(HALF * h, HALF)
            nc.vector.tensor_copy(x_picked[:, span], x_window[:].bitcast(U32).indirect(offs_sb[:, list_cols(span)]))

        quantise_w1(1, shared.tile([P, HALF], U32, name="w1_codes1", offset=8704, align_bytes=64))
        w2_codes = shared.tile([P, PACK, P], I32, name="w2_codes", offset=5120, align_bytes=64)
        nc.vector.tensor_copy(
            w2_codes[:].rearrange("p t (g i) -> p g t i", i=4),
            w2_raw[:].rearrange("p (g i t) -> p g t i", i=4, t=PACK),
        )
        w2s_dealt = shared.tile([P, PACK, P], U8, name="w2s_dealt", offset=26624, align_bytes=64)
        nc.vector.tensor_copy(
            w2s_dealt[:].rearrange("p t (g i) -> p g t i", i=16),
            w2s_raw[:].rearrange("p (g i t) -> p g t i", i=16, t=PACK),
        )
        w2_plane = shared.tile([P, PACK, P], U8, name="w2_plane", offset=16384, align_bytes=64)
        nc.gpsimd.memset(w2_plane[:].bitcast(I32), 0)
        for a in range(PACK):
            nc.sync.dma_start(w2_plane[a:P:QUAD].bitcast(I32), w2s_dealt[SPREAD * a : P : QUAD].bitcast(I32))

        y = [keep.tile([P, S], F32, name="y%d" % t) for t in range(PACK)]
        out_words = keep.tile([P, S], U32, name="out_words", align_bytes=64)
        out_scales = keep.tile([P, S], U8, name="out_scales", align_bytes=64)
        out_rows = out_0.rearrange("(p t) j -> p t j", t=PACK)
        out_word_rows = out_1[0].rearrange("p n t -> p (n t)").bitcast(I32)
        y_turned, sum_turned, own_term, z_bank, z_grouped, out_sb, out_grouped = {}, {}, {}, {}, {}, {}, {}
        east_vals, out_bank = {}, {}

        def product(dst, lhs, lhs_scale, rhs, rhs_scale):
            nc.tensor.matmul_mx(
                out=dst,
                lhsT=lhs.bitcast(FP8X4),
                lhsT_scale=lhs_scale,
                rhs=rhs.bitcast(FP8X4),
                rhs_scale=rhs_scale,
                start=True,
                stop=True,
            )

        def first_product(t, span, index):
            y_bank = bank(index, [P, span.stop - span.start], "y_bank%d_%d" % (t, span.start))
            w_cols = block_cols(t % 2)
            product(y_bank[:], w1_codes[t // 2][:, w_cols], w1_scales[t // 2][:, w_cols], x_picked[:, span], xs_plane[:, span])
            return y_bank

        def first_product_turned(b, index):
            y_turned[b] = bank(index, [P, PACK, P], "y_turned%d" % b)
            for u in range(2):
                dst = y_turned[b][:, cols(2 * u, 2), :].rearrange("j t p -> j (t p)")
                product(dst, x_picked[:, block_cols(b)], xs_plane[:, block_cols(b)], w1_codes[u][:], w1_scales[u][:])

        def turn_into(dst, src, start, stop):
            nc.tensor.matmul(dst, src, ident[:], start=start, stop=stop, is_transpose=True)

        def turn_y(b, index):
            y_turned[b] = bank(index, [P, PACK, P], "y_turned%d" % b)
            for t in range(PACK):
                turn_into(y_turned[b][:, t, :], y[t][:, block_cols(b)], True, True)

        def looked_up(t, lists_sb, span):
            return y[t][:].indirect(lists_sb[:, list_cols(span)])

        def gather_east(t, half):
            tag = "both%d" % t if half and t < 2 else "east%d_%d" % (t, half)
            east_vals[t, half] = keep.tile([P, HALF], F32, name=tag, tag=tag)
            span = cols(HALF * half, HALF)
            if (t, half) == (2, 1):
                nc.vector.tensor_copy(east_of(t, span), looked_up(t, east_sb, span))
            else:
                nc.scalar.activation(east_of(t, span), looked_up(t, east_sb, span), COPY)

        def east_of(t, span):
            return east_vals[t, span.start // HALF][:, cols(span.start % HALF, span.stop - span.start)]

        def west_added(t, span, dst):
            nc.vector.tensor_tensor(dst, looked_up(t, west_sb, span), east_of(t, span), ADD)

        def turn_sum(b, t, terms):
            for k, term in enumerate(terms):
                turn_into(sum_turned[b][:, t, :], term, k == 0, k == len(terms) - 1)

        def west_on_scalar(t, b):
            tile = keep.tile([P, P], F32, name="west%d_%d" % (t, b))
            nc.scalar.activation(tile[:], looked_up(t, west_sb, block_cols(b)), COPY)
            turn_sum(b, t, [east_of(t, block_cols(b)), tile[:]])

        def take_own_term(b):
            own_term[b] = keep.tile([P, PACK, P], F32, name="own_term%d" % b, tag="own_term%d" % b)
            nc.scalar.activation(own_term[b][:], y_turned[b][:], COPY, scale=d_col[:, b : b + 1])

        def combine(b, index):
            turned = keep.tile([P, PACK, P], F32, name="combined%d" % b, tag="combined%d" % b)
            nc.vector.scalar_tensor_tensor(turned[:], sum_turned[b][:], c_col[:, b : b + 1], own_term[b][:], MULT, ADD)
            z_bank[b] = bank(index, [P, PACK, P], "z_bank%d" % b)
            for t in range(PACK):
                turn_into(z_bank[b][:, t, :], turned[:, t, :], True, True)

        def finish_z(b):
            z_grouped[b] = keep.tile([P, P * PACK], BF16, name="z_grouped%d" % b, align_bytes=64)
            nc.vector.tensor_tensor(
                z_grouped[b][:].rearrange("p (g i t) -> p g t i", i=2, t=PACK),
                z_bank[b][:].rearrange("p t (g i) -> p g t i", i=2),
                prev_half[b // 2][:, :, block_cols(b % 2)].rearrange("p t (g i) -> p g t i", i=2),
                SUB,
            )

        def second_product(b, *indices):
            z_codes = keep.tile([P, P], U32, name="z_codes%d" % b, align_bytes=64)
            z_scales = keep.tile([P, P], U8, name="z_scales%d" % b, align_bytes=64)
            nc.vector.quantize_mx(out=z_codes[:].bitcast(FP8X4), scales=z_scales[:], in_=z_grouped[b][:])
            step = PACK // len(indices)
            out_bank[b] = [bank(index, [P, step, P], "out_bank%d_%d" % (b, index)) for index in indices]
            for t in range(PACK):
                product(out_bank[b][t // step][:, t % step, :], w2_codes[:, t, :], w2_plane[:, t, :], z_codes[:], z_scales[:])

        def take_out(b):
            out_sb[b] = keep.tile([P, PACK, P], F32, name="out_sb%d" % b)
            step = PACK // len(out_bank[b])
            for n, part in enumerate(out_bank[b]):
                nc.scalar.copy(out_sb[b][:, cols(step * n, step), :], part[:])
            queue = nc.scalar if b == 2 else nc.sync
            queue.dma_start(out_rows[:, :, block_cols(b)], out_sb[b][:])

        def round_out(b):
            out_grouped[b] = keep.tile([P, P * PACK], BF16, name="out_grouped%d" % b, align_bytes=64)
            nc.vector.tensor_copy(
                out_grouped[b][:].rearrange("p (g i t) -> p g t i", i=2, t=PACK),
                out_sb[b][:].rearrange("p t (g i) -> p g t i", i=2),
            )

        def round_out_of_bank(b):
            out_grouped[b] = keep.tile([P, P * PACK], BF16, name="out_grouped%d" % b, align_bytes=64)
            nc.scalar.copy(
                out_grouped[b][:].rearrange("p (j t) -> p j t", t=PACK), out_bank[b][0][:].rearrange("p t j -> p j t")
            )

        def hand_on(b):
            span = block_cols(b)
            nc.vector.quantize_mx(out=out_words[:, span].bitcast(FP8X4), scales=out_scales[:, span], in_=out_grouped[b][:])

        halves = [cols(0, HALF), cols(HALF, HALF)]
        parts = [(0, halves[0], 0), (0, halves[1], 1)] + [(t, cols(0, S), t + 1) for t in range(1, PACK)]
        banks = [first_product(*part) for part in parts]
        for b in (0, 1):
            first_product_turned(b, 5 + b)
        c_bank = bank(7, [P, P], "c_bank")
        nc.tensor.transpose(c_bank[:], c_rows[:], ident[:])
        c_col = keep.tile([P, LAST], F32, name="c_col")
        d_col = keep.tile([P, LAST], F32, name="d_col")
        for n, ((t, span, index), y_bank) in enumerate(zip(parts, banks)):
            if n in (0, 3):
                nc.scalar.copy(y[t][:, span], y_bank[:])
            else:
                nc.vector.tensor_copy(y[t][:, span], y_bank[:])
        nc.vector.tensor_copy(c_col[:], c_bank[:, 0:LAST])
        nc.vector.tensor_scalar(d_col[:], c_bank[:, 0:LAST], -2.0, 2.0, MULT, ADD)
        for b in (0, 1):
            sum_turned[b] = bank(b, [P, PACK, P], "sum_turned%d" % b)
        for t in range(PACK):
            gather_east(t, 0)
            both = keep.tile([P, HALF], F32, name="both%d" % t, tag="both%d" % t)
            nc.vector.tensor_copy(both[:], looked_up(t, west_sb, halves[0]))
            for b in (0, 1):
                turn_sum(b, t, [both[:, block_cols(b)], east_of(t, block_cols(b))])
        turn_y(2, 7)
        for b in (0, 1):
            take_own_term(b)
        own_last = keep.tile([P, PACK, P], F32, name="own_last")
        for t in range(PACK):
            nc.gpsimd.tensor_tensor(own_last[:, t, :], y[t][:, block_cols(LAST)], d_last[:], MULT)
        gather_east(2, 1)
        for b in (0, 1):
            combine(b, 5 + b)
        rest_last = keep.tile([P, PACK, P], F32, name="rest_last")
        nc.gpsimd.tensor_tensor(rest_last[:], own_last[:], prev_half[1][:, :, block_cols(1)], SUB)
        for t in (0, 1, LAST):
            gather_east(t, 1)
        sum_early = keep.tile([P, LAST, P], F32, name="sum_early", tag="own_term0")
        for t in (2, 0, 1):
            west_added(t, block_cols(LAST), sum_early[:, t, :])
        scaled = keep.tile([P, PACK, P], F32, name="scaled")
        nc.gpsimd.tensor_tensor(scaled[:, 0:LAST], sum_early[:], c_last[:].unsqueeze(1).to_broadcast([P, LAST, P]), MULT)
        finish_z(0)
        sum_turned[2] = bank(5, [P, PACK, P], "sum_turned2")
        finish_z(1)
        for t in range(PACK):
            west_on_scalar(t, 2)
        take_own_term(2)
        second_product(0, 3)
        sum_late = shared.tile([P, P], F32, name="sum_late", offset=1024, align_bytes=64)
        west_added(LAST, block_cols(LAST), sum_late[:])
        second_product(1, 4)
        nc.vector.tensor_tensor(scaled[:, LAST], sum_late[:], c_last[:], MULT)
        combine(2, 7)
        z_grouped[LAST] = keep.tile([P, P * PACK], BF16, name="z_grouped%d" % LAST, align_bytes=64)
        nc.vector.tensor_tensor(
            z_grouped[LAST][:].rearrange("p (g i t) -> p g t i", i=2, t=PACK),
            scaled[:].rearrange("p t (g i) -> p g t i", i=2),
            rest_last[:].rearrange("p t (g i) -> p g t i", i=2),
            ADD,
        )
        for b in (0, 1):
            take_out(b)
            round_out_of_bank(b)
        hand_on(0)
        second_product(LAST, 0)
        finish_z(2)
        hand_on(1)
        second_product(2, 1, 2)
        nc.sync.dma_start(out_word_rows[:, halves[0]], out_words[:, halves[0]].bitcast(I32))
        for b in (LAST, 2):
            take_out(b)
            round_out(b)
            hand_on(b)
            nc.sync.dma_start(out_word_rows[:, block_cols(b)], out_words[:, block_cols(b)].bitcast(I32))

        for q in range(P // QUAD):
            queue = nc.scalar if q % 2 else nc.sync
            queue.dma_start(
                out_2[0, cols(PACK * q, PACK), :].bitcast(I32), out_scales[cols(QUAD * q, PACK), :].bitcast(I32)
            )
